import numpy as np
import ml_dtypes


def mxq(x, axis, fmt="e4m3"):
    dtype, down = {"e4m3": (ml_dtypes.float8_e4m3fn, 7), "e5m2": (ml_dtypes.float8_e5m2, 14)}[fmt]
    v = np.moveaxis(np.asarray(x, np.float32).astype(ml_dtypes.bfloat16).astype(np.float64), axis, -1)
    blocks = v.reshape(v.shape[:-1] + (-1, 32))
    amax = np.abs(blocks).max(-1, keepdims=True)
    byte = np.maximum(np.where(amax > 0, np.frexp(amax)[1] - 1 + 127, 0) - down, 1)
    scale = np.exp2(byte - 127.0)
    codes = (blocks / scale).astype(np.float32).astype(dtype).astype(np.float64)
    return np.moveaxis((codes * scale).reshape(v.shape), -1, axis)


WIDE = False


def mx_kscale(k):
    if not WIDE:
        return np.ones(k)
    levels = np.array([10, -10, 5, -5, 0])
    if k % 512:
        return np.exp2(np.random.permutation(np.resize(levels, k // 32))).repeat(32)
    a = np.empty((k // 512, 16))
    for p in range(k // 512):
        a[p, :8] = np.random.permutation(np.resize(levels, 8))
        for g in range(8):
            far = levels[np.abs(levels - a[p, g]) >= 10]
            a[p, g + 8] = far[np.random.randint(len(far))]
    return np.exp2(a.ravel()).repeat(32)


def f64(x):
    return np.asarray(x).astype(np.float64)


def striped(idx):
    return np.tile(idx.reshape(-1, 16).T, (8, 1)).astype(np.uint16)


def unstriped(offs):
    return offs[:16].T.reshape(-1).astype(np.int64)


E2M1 = np.array([0.0, 0.5, 1.0, 1.5, 2.0, 3.0, 4.0, 6.0, -0.0, -0.5, -1.0, -1.5, -2.0, -3.0, -4.0, -6.0])


def pack_weight(w, fmt):
    k, n = w.shape
    w = f64(np.asarray(w, np.float32).astype(ml_dtypes.bfloat16)).reshape(k // 32, 32, n)
    amax = np.abs(w).max(1)
    if fmt == "e4m3":
        byte = np.frexp(amax)[1] - 1 + 127 - 7
    else:
        mant, ex = np.frexp(amax / 6.0)
        byte = np.where(mant > 0.5, ex, ex - 1) + 127
    byte = np.clip(np.where(amax > 0, byte, 1), 1, 254)
    scaled = (w * np.exp2(127.0 - byte)[:, None, :]).reshape(k, n).astype(np.float32)
    by_word = np.ascontiguousarray(scaled.reshape(k // 512, 128, 4, n).transpose(0, 1, 3, 2))
    if fmt == "e4m3":
        words = by_word.astype(ml_dtypes.float8_e4m3fn).view(np.uint8)
    else:
        c = by_word.astype(ml_dtypes.float4_e2m1fn).view(np.uint8) & 0xF
        words = (c[..., 0::2] | (c[..., 1::2] << 4)).reshape(k // 512, 128, 2 * n)
    return np.ascontiguousarray(words), np.ascontiguousarray(byte.astype(np.uint8).reshape(k // 512, 16, n))


def unpack_weight(words, scales, fmt):
    g, _, n = scales.shape
    words = np.ascontiguousarray(words).reshape(g, 128, n, -1)
    if fmt == "e4m3":
        vals = words.view(ml_dtypes.float8_e4m3fn).astype(np.float64)
    else:
        nib = np.empty((g, 128, n, 4), np.uint8)
        nib[..., 0::2] = words & 0xF
        nib[..., 1::2] = words >> 4
        vals = E2M1[nib]
    vals = vals * np.repeat(np.exp2(scales.astype(np.float64) - 127.0), 8, axis=1)[..., None]
    return vals.transpose(0, 1, 3, 2).reshape(g * 512, n)


def gelu(v):
    return 0.5 * v * (1.0 + np.tanh(np.sqrt(2.0 / np.pi) * (v + 0.044715 * v**3)))


def bf(x):
    return np.asarray(x, np.float32).astype(ml_dtypes.bfloat16)


def planes(Y):
    n, m = Y.shape
    b = f64(bf(Y)).reshape(n // 32, 32, m)
    amax = np.abs(b).max(1)
    byte = np.clip(np.where(amax > 0, np.frexp(amax)[1] - 1 + 127 - 7, 1), 1, 254)
    codes = (b * np.exp2(127.0 - byte)[:, None, :]).reshape(n, m).astype(np.float32).astype(ml_dtypes.float8_e4m3fn).view(np.uint8)
    words = codes.reshape(n // 512, 128, 4, m).transpose(0, 1, 3, 2)
    return np.ascontiguousarray(words), np.ascontiguousarray(byte.astype(np.uint8).reshape(n // 512, 16, m))


T, S, K, H, M, N = 2048, 1024, 1024, 1024, 512, 512

def setup_inputs():
    n = np.random.standard_normal
    s = mx_kscale(K)[:, None]
    u = mx_kscale(H)[:, None]
    s2 = mx_kscale(M)[:, None]
    tab_words, tab_scales = pack_weight(n((K, T)) * s, "e4m3")
    w4_words, w4_scales = pack_weight(1.4 * n((H, N)) / np.sqrt(H) / u, "e2m1")
    return {
        "tab_words": tab_words,
        "tab_scales": tab_scales,
        "offs": striped(np.random.permutation(T)[:S]),
        "gT": (n((N, T)) * np.exp(0.8 * n(N))[:, None]).astype(np.float32),
        "w1": (1.5 * n((K, H)) / np.sqrt(K) / s).astype(np.float32),
        "b1": (0.5 * n(H)).astype(np.float32),
        "gain": (np.random.uniform(0.5, 1.5, H) * u[:, 0]).astype(np.float32),
        "w4_words": w4_words,
        "w4_scales": w4_scales,
        "tick": (n((M, S)) * s2).astype(np.float32),
        "w3": (0.7 * n((M, N)) / np.sqrt(M) / s2).astype(np.float32),
    }

def reference(tab_words, tab_scales, offs, gT, w1, b1, gain, w4_words, w4_scales, tick, w3):
    v = unpack_weight(tab_words, tab_scales, "e4m3")[:, unstriped(offs)]
    w4 = unpack_weight(w4_words, w4_scales, "e2m1")
    x = (mxq(f64(w1), 0, "e4m3").T @ v) + f64(b1)[:, None]
    h = f64(gain)[:, None] / (1.0 + np.exp(-x))
    e = (w4.T @ mxq(h, 0, "e4m3")
              + mxq(f64(w3), 0, "e4m3").T @ mxq(f64(tick), 0, "e4m3"))
    g = f64(gT)[:, unstriped(offs)]
    new = g / (1.0 + e * e)
    y = f64(gT).copy()
    y[:, unstriped(offs)] = new
    words, scales = planes(y)
    return y, words, scales

@@ -1,0 +1,309 @@
+from contextlib import ExitStack
+
+import concourse.mybir as mybir
+
+T, S, K, H, M, N = 2048, 1024, 1024, 1024, 512, 512
+FLOPS = 2 * K * H * S + 2 * H * N * S + 2 * M * N * S
+
+F32 = mybir.dt.float32
+BF16 = mybir.dt.bfloat16
+I32 = mybir.dt.int32
+U32 = mybir.dt.uint32
+U16 = mybir.dt.uint16
+U8 = mybir.dt.uint8
+FP8X4 = mybir.dt.float8_e4m3fn_x4
+FP4X4 = mybir.dt.float4_e2m1fn_x4
+ACT = mybir.ActivationFunctionType
+MULT = mybir.AluOpType.mult
+
+P = 128
+PACK = 4
+G = P * PACK
+HALF = 512
+HALVES = S // HALF
+LIST_COLS = HALF // 16
+
+
+def tile_list_gallery_state_damping_kernel(
+    tc, tab_words, tab_scales, offs, gT, w1, b1, gain, w4_words, w4_scales, tick, w3, out_0, out_1, out_2
+):
+    nc = tc.nc
+    with ExitStack() as ctx:
+        keep = ctx.enter_context(tc.tile_pool(name="keep", bufs=1))
+        ring = ctx.enter_context(tc.tile_pool(name="ring", bufs=2))
+        psum = ctx.enter_context(tc.psum_pool(name="psum", bufs=4))
+
+        def kept(name, shape, dtype):
+            return keep.tile(shape, dtype, name=name, align_bytes=64)
+
+        def staged(name, shape, dtype):
+            return keep.tile(shape, dtype, name=name, tag="staged", bufs=4, align_bytes=64)
+
+        def scale_rows(name, shape):
+            rows = keep.tile(shape, U8, name=name, tag="scale_rows", align_bytes=64)
+            nc.gpsimd.memset(rows[:].bitcast(I32), 0)
+            return rows
+
+        def load_rows(name, rows):
+            raw = staged(name, [P, PACK, G], F32)
+            nc.sync.dma_start(out=raw[:], in_=rows.rearrange("(p j) c -> p j c", j=PACK))
+            return raw
+
+        def load_table(a):
+            words = staged("tab_w%d" % a, [P, T], I32)
+            nc.sync.dma_start(out=words[:], in_=tab_words[a].rearrange("p n t -> p (n t)").bitcast(I32))
+            return words
+
+        offsets = keep.tile([P, S // 16], U16, name="offsets")
+        nc.sync.dma_start(offsets[:], offs)
+        w4_raw = []
+        for b in range(2):
+            w4_raw.append(staged("w4_raw%d" % b, [P, 2 * N], U8))
+            nc.sync.dma_start(out=w4_raw[b][:].bitcast(I32), in_=w4_words[b].bitcast(I32))
+        tab_w = [load_table(0)]
+        w1_raw = {}
+        w1_raw[0, 0] = load_rows("w1_raw00", w1[0:G, 0:G])
+        tab_s = scale_rows("tab_s", [P, T])
+        for q in range(4):
+            nc.sync.dma_start(
+                out=tab_s[32 * q : 32 * q + 8, :].bitcast(I32), in_=tab_scales[:, 4 * q : 4 * q + 4, :].bitcast(I32)
+            )
+        bias = kept("bias", [P, 2, PACK], F32)
+        gains = kept("gains", [P, 2, PACK], F32)
+        nc.sync.dma_start(out=bias[:], in_=b1.rearrange("(b p t) -> p b t", b=2, t=PACK))
+        nc.sync.dma_start(out=gains[:], in_=gain.rearrange("(b p t) -> p b t", b=2, t=PACK))
+
+        def grouped_tile():
+            return ring.tile([P, G * PACK], BF16, name="grouped", tag="grouped", bufs=4, align_bytes=64)
+
+        def quantize(name, grouped):
+            codes = kept(name + "_codes", [P, G], U32)
+            scales = kept(name + "_scales", [P, G], U8)
+            nc.vector.quantize_mx(out=codes[:].bitcast(FP8X4), scales=scales[:], in_=grouped[:])
+            return codes, scales
+
+        def dealt_views(grouped, raw):
+            return (
+                grouped[:].rearrange("p (t m j) -> p m j t", t=PACK, j=PACK),
+                raw[:].rearrange("p j (m t) -> p m j t", t=PACK),
+            )
+
+        def woven_views(grouped, raw):
+            return (
+                grouped[:].rearrange("p (c i t) -> p c t i", i=4, t=PACK),
+                raw.rearrange("p t (c i) -> p c t i", i=4),
+            )
+
+        def list_half(h):
+            return offsets[:, h * LIST_COLS : (h + 1) * LIST_COLS]
+
+        v_words, v_scales = {}, {}
+
+        def gather_words(a, h):
+            v_words[a, h] = kept("v_words%d%d" % (a, h), [P, HALF], U32)
+            nc.vector.tensor_copy(v_words[a, h][:], tab_w[a][:].bitcast(U32).indirect(list_half(h)))
+
+        def gather_scales(h):
+            v_scales[h] = kept("v_scales%d" % h, [P, HALF], U8)
+            nc.vector.tensor_copy(v_scales[h][:], tab_s[:].indirect(list_half(h)))
+
+        w1_q = {}
+
+        def quantize_w1(a, b, copy):
+            grouped = grouped_tile()
+            dst, src = dealt_views(grouped, w1_raw[a, b])
+            copy(out=dst, in_=src)
+            w1_q[a, b] = quantize("w1_%d%d" % (a, b), grouped)
+
+        sig = {}
+
+        def stage_one(b, h):
+            sig[b, h] = ring.tile([P, PACK, HALF], F32, name="sig", tag="sig", bufs=4, align_bytes=64)
+            for t in range(PACK):
+                cols = slice(t * P, (t + 1) * P)
+                acc = psum.tile([P, HALF], F32, name="x_acc", tag="x_acc")
+                for a in range(2):
+                    codes, scales = w1_q[a, b]
+                    nc.tensor.matmul_mx(
+                        out=acc[:],
+                        lhsT=codes[:, cols].bitcast(FP8X4),
+                        lhsT_scale=scales[:, cols],
+                        rhs=v_words[a, h][:].bitcast(FP8X4),
+                        rhs_scale=v_scales[h][4 * a : P, :],
+                        start=(a == 0),
+                        stop=(a == 1),
+                    )
+                nc.scalar.activation(out=sig[b, h][:, t, :], in_=acc[:], func=ACT.Sigmoid, bias=bias[:, b, t : t + 1])
+
+        h_q = {}
+
+        def quantize_h(b, h, grouped):
+            dst, src = woven_views(grouped, sig[b, h][:])
+            factor = gains[:, b, :].unsqueeze(1).unsqueeze(3).broadcast_to([P, HALF // 4, PACK, 4])
+            nc.vector.tensor_tensor(out=dst, in0=src, in1=factor, op=MULT)
+            h_q[b, h] = quantize("h_%d%d" % (b, h), grouped)
+
+        def quantize_h_on_scalar(b, h, grouped):
+            scaled = ring.tile([P, PACK, HALF], BF16, name="scaled", tag="scaled", align_bytes=64)
+            for t in range(PACK):
+                nc.scalar.activation(
+                    out=scaled[:, t, :], in_=sig[b, h][:, t, :], func=ACT.Copy, scale=gains[:, b, t : t + 1]
+                )
+            dst, src = woven_views(grouped, scaled[:])
+            nc.scalar.copy(out=dst, in_=src)
+            h_q[b, h] = quantize("h_%d%d" % (b, h), grouped)
+
+        tick_q = {}
+
+        def quantize_tick(h, copy):
+            grouped = grouped_tile()
+            dst, src = woven_views(grouped, tick_raw[h][:])
+            copy(out=dst, in_=src)
+            tick_q[h] = quantize("tick_%d" % h, grouped)
+
+        picked = {}
+
+        def gather_states(h):
+            into = keep.tile([P, PACK, HALF], F32, name="picked", tag="late%d" % h, align_bytes=64)
+            for t in range(PACK):
+                picked[t, h] = into[:, t, :]
+                nc.vector.tensor_copy(picked[t, h], pages[t][:].indirect(list_half(h)))
+
+        damp = {}
+
+        def stage_two(t, h):
+            cols = slice(t * P, (t + 1) * P)
+            acc = psum.tile([P, HALF], F32, name="e_acc", tag="e_acc")
+            nc.tensor.matmul_mx(
+                out=acc[:],
+                lhsT=w3_q[0][:, cols].bitcast(FP8X4),
+                lhsT_scale=w3_q[1][:, cols],
+                rhs=tick_q[h][0][:].bitcast(FP8X4),
+                rhs_scale=tick_q[h][1][:],
+                start=True,
+                stop=False,
+            )
+            for b in range(2):
+                nc.tensor.matmul_mx(
+                    out=acc[:],
+                    lhsT=w4_codes[b][:, 2 * t * P : 2 * (t + 1) * P].bitcast(FP4X4),
+                    lhsT_scale=w4_planes[b][:, cols],
+                    rhs=h_q[b, h][0][:].bitcast(FP8X4),
+                    rhs_scale=h_q[b, h][1][:],
+                    start=False,
+                    stop=(b == 1),
+                )
+            square = ring.tile([P, HALF], F32, name="square", tag="square", bufs=4)
+            nc.scalar.activation(out=square[:], in_=acc[:], func=ACT.Square)
+            root = ring.tile([P, HALF], F32, name="root", tag="root", bufs=4)
+            nc.scalar.activation(out=root[:], in_=square[:], func=ACT.Abs_reciprocal_sqrt, bias=1.0)
+            damp[t, h] = ring.tile([P, HALF], F32, name="damp", tag="damp", bufs=4)
+            nc.scalar.activation(out=damp[t, h][:], in_=root[:], func=ACT.Square)
+
+        def scatter_state(t, h):
+            nc.vector.tensor_tensor(pages[t][:].indirect(list_half(h)), picked[t, h], damp[t, h][:], MULT)
+
+        w4_codes = []
+        for b in range(2):
+            w4_codes.append(kept("w4_codes%d" % b, [P, 2 * N], U8))
+            nc.vector.tensor_copy(
+                out=w4_codes[b][:].rearrange("p (t m y) -> p m t y", t=PACK, y=2),
+                in_=w4_raw[b][:].rearrange("p (m t y) -> p m t y", t=PACK, y=2),
+            )
+        w1_raw[1, 0] = load_rows("w1_raw10", w1[G : 2 * G, 0:G])
+        tab_w.append(load_table(1))
+        gather_words(0, 0)
+        gather_words(0, 1)
+        gather_scales(0)
+        gather_scales(1)
+        w1_raw[0, 1] = load_rows("w1_raw01", w1[0:G, G : 2 * G])
+        quantize_w1(0, 0, nc.scalar.copy)
+        w1_raw[1, 1] = load_rows("w1_raw11", w1[G : 2 * G, G : 2 * G])
+        gather_words(1, 0)
+        quantize_w1(1, 0, nc.scalar.copy)
+        w3_raw = load_rows("w3_raw", w3)
+        w4_raw_s = scale_rows("w4_raw_s", [P, 2 * N])
+        for q in range(4):
+            nc.sync.dma_start(
+                out=w4_raw_s[32 * q : 32 * q + 4, :].bitcast(I32).rearrange("i (a n) -> i a n", a=2),
+                in_=w4_scales[:, 4 * q : 4 * q + 4, :].rearrange("a i n -> i a n").bitcast(I32),
+            )
+        gather_words(1, 1)
+        tick_raw = [load_rows("tick_raw0", tick[:, 0:HALF])]
+        quantize_w1(0, 1, nc.scalar.copy)
+        stage_one(0, 0)
+        g_rows = gT.rearrange("(p t) m -> t p m", t=PACK)
+        pages = []
+
+        def load_page(t):
+            pages.append(staged("page%d" % t, [P, T], F32))
+            nc.sync.dma_start(out=pages[t][:], in_=g_rows[t])
+
+        load_page(0)
+        quantize_w1(1, 1, nc.vector.tensor_copy)
+        quantize_h(0, 0, grouped_tile())
+        load_page(1)
+        w4_plane = kept("w4_plane", [P, 2 * N], U8)
+        nc.vector.tensor_copy(
+            out=w4_plane[:].rearrange("p (a t m) -> p a m t", a=2, t=PACK),
+            in_=w4_raw_s[:].rearrange("p (a m t) -> p a m t", a=2, t=PACK),
+        )
+        w4_planes = [w4_plane[:, 0:N], w4_plane[:, N : 2 * N]]
+        stage_one(1, 0)
+        stage_one(0, 1)
+        grouped = keep.tile([P, G * PACK], BF16, name="w3_grouped", tag="late_tick", align_bytes=64)
+        dst, src = dealt_views(grouped, w3_raw)
+        nc.vector.tensor_copy(out=dst, in_=src)
+        w3_q = quantize("w3", grouped)
+        load_page(2)
+        quantize_tick(0, nc.vector.tensor_copy)
+        load_page(3)
+        quantize_h(1, 0, keep.tile([P, G * PACK], BF16, name="last_h", tag="late0", align_bytes=64))
+        stage_one(1, 1)
+        late_tick = keep.tile([P, PACK, HALF], F32, name="tick_raw1", tag="late_tick", align_bytes=64)
+        nc.sync.dma_start(out=late_tick[:], in_=tick[:, HALF : 2 * HALF].rearrange("(p j) c -> p j c", j=PACK))
+        tick_raw.append(late_tick)
+        for t in range(PACK):
+            stage_two(t, 0)
+        gather_states(0)
+        scatter_state(0, 0)
+        scatter_state(1, 0)
+        quantize_h_on_scalar(0, 1, grouped_tile())
+        scatter_state(2, 0)
+        scatter_state(3, 0)
+        quantize_tick(1, nc.scalar.copy)
+        quantize_h_on_scalar(1, 1, keep.tile([P, G * PACK], BF16, name="last_h", tag="late1", align_bytes=64))
+        gather_states(1)
+
+        y_rows = out_0.rearrange("(p t) m -> t p m", t=PACK)
+        chunks = T // G
+        rounded = [
+            kept("rounded%d" % c, [P, PACK, G], BF16) for c in range(chunks)
+        ]
+        for t in range(PACK):
+            stage_two(t, 1)
+        for t in range(PACK):
+            scatter_state(t, 1)
+            nc.sync.dma_start(out=y_rows[t], in_=pages[t][:])
+            for c in range(chunks):
+                nc.scalar.copy(out=rounded[c][:, t, :], in_=pages[t][:, c * G : (c + 1) * G])
+
+        y_scales = kept("y_scales", [P, T], U8)
+        y_words = out_1[0].rearrange("p m t -> p (m t)").bitcast(I32)
+        woven = []
+        for c in range(chunks + 1):
+            if c < chunks:
+                grouped = grouped_tile()
+                dst, src = woven_views(grouped, rounded[c][:])
+                copy = nc.scalar.copy if c == chunks - 1 else nc.vector.tensor_copy
+                copy(out=dst, in_=src)
+                woven.append(grouped)
+            if c > 0:
+                cols = slice((c - 1) * G, c * G)
+                codes = keep.tile([P, G], I32, name="y_codes", tag="y_codes", bufs=4, align_bytes=64)
+                nc.vector.quantize_mx(out=codes[:].bitcast(FP8X4), scales=y_scales[:, cols], in_=woven[c - 1][:])
+                nc.sync.dma_start(out=y_words[:, cols], in_=codes[:])
+        for q in range(4):
+            nc.sync.dma_start(
+                out=out_2[0, 4 * q : 4 * q + 4, :].bitcast(I32), in_=y_scales[32 * q : 32 * q + 4, :].bitcast(I32)
+            )

@@ -88,10 +88,10 @@ def tile_list_gallery_state_damping_kernel(
                 raw[:].rearrange("p j (m t) -> p m j t", t=PACK),
             )
 
-        def woven_views(grouped, raw):
+        def woven_views(grouped, raw, run=4):
             return (
-                grouped[:].rearrange("p (c i t) -> p c t i", i=4, t=PACK),
-                raw.rearrange("p t (c i) -> p c t i", i=4),
+                grouped.rearrange("p (c i t) -> p c t i", i=run, t=PACK),
+                raw.rearrange("p t (c i) -> p c t i", i=run),
             )
 
         def list_half(h):
@@ -138,8 +138,8 @@ def tile_list_gallery_state_damping_kernel(
         h_q = {}
 
         def quantize_h(b, h, grouped):
-            dst, src = woven_views(grouped, sig[b, h][:])
-            factor = gains[:, b, :].unsqueeze(1).unsqueeze(3).broadcast_to([P, HALF // 4, PACK, 4])
+            dst, src = woven_views(grouped[:], sig[b, h][:], run=2)
+            factor = gains[:, b, :].unsqueeze(1).unsqueeze(3).broadcast_to([P, HALF // 2, PACK, 2])
             nc.vector.tensor_tensor(out=dst, in0=src, in1=factor, op=MULT)
             h_q[b, h] = quantize("h_%d%d" % (b, h), grouped)
 
@@ -149,7 +149,7 @@ def tile_list_gallery_state_damping_kernel(
                 nc.scalar.activation(
                     out=scaled[:, t, :], in_=sig[b, h][:, t, :], func=ACT.Copy, scale=gains[:, b, t : t + 1]
                 )
-            dst, src = woven_views(grouped, scaled[:])
+            dst, src = woven_views(grouped[:], scaled[:])
             nc.scalar.copy(out=dst, in_=src)
             h_q[b, h] = quantize("h_%d%d" % (b, h), grouped)
 
@@ -157,7 +157,7 @@ def tile_list_gallery_state_damping_kernel(
 
         def quantize_tick(h, copy):
             grouped = grouped_tile()
-            dst, src = woven_views(grouped, tick_raw[h][:])
+            dst, src = woven_views(grouped[:], tick_raw[h][:])
             copy(out=dst, in_=src)
             tick_q[h] = quantize("tick_%d" % h, grouped)
 
@@ -230,7 +230,7 @@ def tile_list_gallery_state_damping_kernel(
             )
         gather_words(1, 1)
         tick_raw = [load_rows("tick_raw0", tick[:, 0:HALF])]
-        quantize_w1(0, 1, nc.scalar.copy)
+        quantize_w1(0, 1, nc.vector.tensor_copy)
         stage_one(0, 0)
         g_rows = gT.rearrange("(p t) m -> t p m", t=PACK)
         pages = []
@@ -241,7 +241,6 @@ def tile_list_gallery_state_damping_kernel(
 
         load_page(0)
         quantize_w1(1, 1, nc.vector.tensor_copy)
-        quantize_h(0, 0, grouped_tile())
         load_page(1)
         w4_plane = kept("w4_plane", [P, 2 * N], U8)
         nc.vector.tensor_copy(
@@ -249,6 +248,7 @@ def tile_list_gallery_state_damping_kernel(
             in_=w4_raw_s[:].rearrange("p (a m t) -> p a m t", a=2, t=PACK),
         )
         w4_planes = [w4_plane[:, 0:N], w4_plane[:, N : 2 * N]]
+        quantize_h_on_scalar(0, 0, grouped_tile())
         stage_one(1, 0)
         stage_one(0, 1)
         grouped = keep.tile([P, G * PACK], BF16, name="w3_grouped", tag="late_tick", align_bytes=64)
@@ -271,38 +271,45 @@ def tile_list_gallery_state_damping_kernel(
         quantize_h_on_scalar(0, 1, grouped_tile())
         scatter_state(2, 0)
         scatter_state(3, 0)
-        quantize_tick(1, nc.scalar.copy)
+        quantize_tick(1, nc.vector.tensor_copy)
         quantize_h_on_scalar(1, 1, keep.tile([P, G * PACK], BF16, name="last_h", tag="late1", align_bytes=64))
         gather_states(1)
 
         y_rows = out_0.rearrange("(p t) m -> t p m", t=PACK)
-        chunks = T // G
-        rounded = [
-            kept("rounded%d" % c, [P, PACK, G], BF16) for c in range(chunks)
-        ]
+        spans = [(0, 512), (512, 1024), (1024, 1536), (1536, 1792), (1792, 2048)]
+        rounded = [kept("rounded%d" % lo, [P, PACK, hi - lo], BF16) for lo, hi in spans]
         for t in range(PACK):
             stage_two(t, 1)
         for t in range(PACK):
             scatter_state(t, 1)
             nc.sync.dma_start(out=y_rows[t], in_=pages[t][:])
-            for c in range(chunks):
-                nc.scalar.copy(out=rounded[c][:, t, :], in_=pages[t][:, c * G : (c + 1) * G])
+            for c, (lo, hi) in enumerate(spans):
+                copy = nc.vector.tensor_copy if (t, c) == (PACK - 1, 0) else nc.scalar.copy
+                copy(out=rounded[c][:, t, :], in_=pages[t][:, lo:hi])
 
         y_scales = kept("y_scales", [P, T], U8)
         y_words = out_1[0].rearrange("p m t -> p (m t)").bitcast(I32)
-        woven = []
-        for c in range(chunks + 1):
-            if c < chunks:
-                grouped = grouped_tile()
-                dst, src = woven_views(grouped, rounded[c][:])
-                copy = nc.scalar.copy if c == chunks - 1 else nc.vector.tensor_copy
-                copy(out=dst, in_=src)
-                woven.append(grouped)
-            if c > 0:
-                cols = slice((c - 1) * G, c * G)
-                codes = keep.tile([P, G], I32, name="y_codes", tag="y_codes", bufs=4, align_bytes=64)
-                nc.vector.quantize_mx(out=codes[:].bitcast(FP8X4), scales=y_scales[:, cols], in_=woven[c - 1][:])
-                nc.sync.dma_start(out=y_words[:, cols], in_=codes[:])
+        woven = [kept("woven%d" % lo, [P, (hi - lo) * PACK], BF16) for lo, hi in spans]
+
+        def weave(c, lo, hi, copy):
+            dst, src = woven_views(woven[c][:, lo * PACK : hi * PACK], rounded[c][:, :, lo:hi])
+            copy(out=dst, in_=src)
+
+        def quantize_y(c):
+            lo, hi = spans[c]
+            codes = kept("y_codes%d" % lo, [P, hi - lo], I32)
+            nc.vector.quantize_mx(out=codes[:].bitcast(FP8X4), scales=y_scales[:, lo:hi], in_=woven[c][:])
+            nc.sync.dma_start(out=y_words[:, lo:hi], in_=codes[:])
+
+        weave(0, 0, 512, nc.vector.tensor_copy)
+        weave(1, 0, 512, nc.vector.tensor_copy)
+        weave(2, 256, 512, nc.scalar.copy)
+        weave(3, 0, 256, nc.scalar.copy)
+        weave(4, 0, 256, nc.scalar.copy)
+        quantize_y(0)
+        weave(2, 0, 256, nc.vector.tensor_copy)
+        for c in range(1, len(spans)):
+            quantize_y(c)
         for q in range(4):
             nc.sync.dma_start(
                 out=out_2[0, 4 * q : 4 * q + 4, :].bitcast(I32), in_=y_scales[32 * q : 32 * q + 4, :].bitcast(I32)

@@ -36,6 +36,9 @@ def tile_list_gallery_state_damping_kernel(
         def kept(name, shape, dtype):
             return keep.tile(shape, dtype, name=name, align_bytes=64)
 
+        def held(name, shape, dtype, tag):
+            return keep.tile(shape, dtype, name=name, tag=tag, align_bytes=64)
+
         def staged(name, shape, dtype):
             return keep.tile(shape, dtype, name=name, tag="staged", bufs=4, align_bytes=64)
 
@@ -144,7 +147,7 @@ def tile_list_gallery_state_damping_kernel(
             h_q[b, h] = quantize("h_%d%d" % (b, h), grouped)
 
         def quantize_h_on_scalar(b, h, grouped):
-            scaled = ring.tile([P, PACK, HALF], BF16, name="scaled", tag="scaled", align_bytes=64)
+            scaled = held("scaled", [P, PACK, HALF], BF16, "last_square")
             for t in range(PACK):
                 nc.scalar.activation(
                     out=scaled[:, t, :], in_=sig[b, h][:, t, :], func=ACT.Copy, scale=gains[:, b, t : t + 1]
@@ -155,8 +158,7 @@ def tile_list_gallery_state_damping_kernel(
 
         tick_q = {}
 
-        def quantize_tick(h, copy):
-            grouped = grouped_tile()
+        def quantize_tick(h, copy, grouped):
             dst, src = woven_views(grouped[:], tick_raw[h][:])
             copy(out=dst, in_=src)
             tick_q[h] = quantize("tick_%d" % h, grouped)
@@ -193,9 +195,13 @@ def tile_list_gallery_state_damping_kernel(
                     start=False,
                     stop=(b == 1),
                 )
-            square = ring.tile([P, HALF], F32, name="square", tag="square", bufs=4)
+            if (t, h) == (PACK - 1, 0):
+                square = held("square", [P, HALF], F32, "last_square")
+                root = held("root", [P, HALF], F32, "last_root")
+            else:
+                square = ring.tile([P, HALF], F32, name="square", tag="square", bufs=4)
+                root = ring.tile([P, HALF], F32, name="root", tag="root", bufs=4)
             nc.scalar.activation(out=square[:], in_=acc[:], func=ACT.Square)
-            root = ring.tile([P, HALF], F32, name="root", tag="root", bufs=4)
             nc.scalar.activation(out=root[:], in_=square[:], func=ACT.Abs_reciprocal_sqrt, bias=1.0)
             damp[t, h] = ring.tile([P, HALF], F32, name="damp", tag="damp", bufs=4)
             nc.scalar.activation(out=damp[t, h][:], in_=root[:], func=ACT.Square)
@@ -251,12 +257,12 @@ def tile_list_gallery_state_damping_kernel(
         quantize_h_on_scalar(0, 0, grouped_tile())
         stage_one(1, 0)
         stage_one(0, 1)
-        grouped = keep.tile([P, G * PACK], BF16, name="w3_grouped", tag="late_tick", align_bytes=64)
+        grouped = grouped_tile()
         dst, src = dealt_views(grouped, w3_raw)
         nc.vector.tensor_copy(out=dst, in_=src)
         w3_q = quantize("w3", grouped)
         load_page(2)
-        quantize_tick(0, nc.vector.tensor_copy)
+        quantize_tick(0, nc.vector.tensor_copy, held("tick_grouped0", [P, G * PACK], BF16, "late_tick"))
         load_page(3)
         quantize_h(1, 0, keep.tile([P, G * PACK], BF16, name="last_h", tag="late0", align_bytes=64))
         stage_one(1, 1)
@@ -271,7 +277,7 @@ def tile_list_gallery_state_damping_kernel(
         quantize_h_on_scalar(0, 1, grouped_tile())
         scatter_state(2, 0)
         scatter_state(3, 0)
-        quantize_tick(1, nc.vector.tensor_copy)
+        quantize_tick(1, nc.scalar.copy, held("tick_grouped1", [P, G * PACK], BF16, "last_root"))
         quantize_h_on_scalar(1, 1, keep.tile([P, G * PACK], BF16, name="last_h", tag="late1", align_bytes=64))
         gather_states(1)
 

@@ -15,13 +15,14 @@ FP8X4 = mybir.dt.float8_e4m3fn_x4
 FP4X4 = mybir.dt.float4_e2m1fn_x4
 ACT = mybir.ActivationFunctionType
 MULT = mybir.AluOpType.mult
+ADD = mybir.AluOpType.add
 
 P = 128
 PACK = 4
 G = P * PACK
 HALF = 512
-HALVES = S // HALF
 LIST_COLS = HALF // 16
+SPAN = 512
 
 
 def tile_list_gallery_state_damping_kernel(
@@ -30,65 +31,44 @@ def tile_list_gallery_state_damping_kernel(
     nc = tc.nc
     with ExitStack() as ctx:
         keep = ctx.enter_context(tc.tile_pool(name="keep", bufs=1))
-        ring = ctx.enter_context(tc.tile_pool(name="ring", bufs=2))
         psum = ctx.enter_context(tc.psum_pool(name="psum", bufs=4))
 
         def kept(name, shape, dtype):
             return keep.tile(shape, dtype, name=name, align_bytes=64)
 
-        def held(name, shape, dtype, tag):
-            return keep.tile(shape, dtype, name=name, tag=tag, align_bytes=64)
+        def slot(tag, name, shape, dtype, bufs=1):
+            return keep.tile(shape, dtype, name=name, tag=tag, bufs=bufs, align_bytes=64)
 
-        def staged(name, shape, dtype):
-            return keep.tile(shape, dtype, name=name, tag="staged", bufs=4, align_bytes=64)
-
-        def scale_rows(name, shape):
-            rows = keep.tile(shape, U8, name=name, tag="scale_rows", align_bytes=64)
-            nc.gpsimd.memset(rows[:].bitcast(I32), 0)
-            return rows
-
-        def load_rows(name, rows):
-            raw = staged(name, [P, PACK, G], F32)
+        def load_rows(tag, name, rows):
+            raw = slot(tag, name, [P, PACK, G], F32)
             nc.sync.dma_start(out=raw[:], in_=rows.rearrange("(p j) c -> p j c", j=PACK))
             return raw
 
-        def load_table(a):
-            words = staged("tab_w%d" % a, [P, T], I32)
+        def load_table(tag, a):
+            words = slot(tag, "tab_w%d" % a, [P, T], I32)
             nc.sync.dma_start(out=words[:], in_=tab_words[a].rearrange("p n t -> p (n t)").bitcast(I32))
             return words
 
-        offsets = keep.tile([P, S // 16], U16, name="offsets")
-        nc.sync.dma_start(offsets[:], offs)
-        w4_raw = []
-        for b in range(2):
-            w4_raw.append(staged("w4_raw%d" % b, [P, 2 * N], U8))
-            nc.sync.dma_start(out=w4_raw[b][:].bitcast(I32), in_=w4_words[b].bitcast(I32))
-        tab_w = [load_table(0)]
-        w1_raw = {}
-        w1_raw[0, 0] = load_rows("w1_raw00", w1[0:G, 0:G])
-        tab_s = scale_rows("tab_s", [P, T])
-        for q in range(4):
-            nc.sync.dma_start(
-                out=tab_s[32 * q : 32 * q + 8, :].bitcast(I32), in_=tab_scales[:, 4 * q : 4 * q + 4, :].bitcast(I32)
-            )
-        bias = kept("bias", [P, 2, PACK], F32)
-        gains = kept("gains", [P, 2, PACK], F32)
-        nc.sync.dma_start(out=bias[:], in_=b1.rearrange("(b p t) -> p b t", b=2, t=PACK))
-        nc.sync.dma_start(out=gains[:], in_=gain.rearrange("(b p t) -> p b t", b=2, t=PACK))
+        g_rows = gT.rearrange("(p t) m -> t p m", t=PACK)
+        pages = {}
+
+        def load_page(tag, t):
+            pages[t] = slot(tag, "page%d" % t, [P, T], F32)
+            nc.sync.dma_start(out=pages[t][:], in_=g_rows[t])
 
         def grouped_tile():
-            return ring.tile([P, G * PACK], BF16, name="grouped", tag="grouped", bufs=4, align_bytes=64)
+            return slot("grouped", "grouped", [P, G * PACK], BF16, bufs=3)
 
-        def quantize(name, grouped):
-            codes = kept(name + "_codes", [P, G], U32)
-            scales = kept(name + "_scales", [P, G], U8)
-            nc.vector.quantize_mx(out=codes[:].bitcast(FP8X4), scales=scales[:], in_=grouped[:])
+        def quantize(name, grouped, width=G):
+            codes = kept(name + "_codes", [P, width], U32)
+            scales = kept(name + "_scales", [P, width], U8)
+            nc.vector.quantize_mx(out=codes[:].bitcast(FP8X4), scales=scales[:], in_=grouped)
             return codes, scales
 
-        def dealt_views(grouped, raw):
-            return (
-                grouped[:].rearrange("p (t m j) -> p m j t", t=PACK, j=PACK),
-                raw[:].rearrange("p j (m t) -> p m j t", t=PACK),
+        def deal(copy, grouped, raw):
+            copy(
+                out=grouped.rearrange("p (t m j) -> p m j t", t=PACK, j=PACK),
+                in_=raw.rearrange("p j (m t) -> p m j t", t=PACK),
             )
 
         def woven_views(grouped, raw, run=4):
@@ -97,31 +77,82 @@ def tile_list_gallery_state_damping_kernel(
                 raw.rearrange("p t (c i) -> p c t i", i=run),
             )
 
+        def weave(copy, grouped, raw):
+            dst, src = woven_views(grouped, raw)
+            copy(out=dst, in_=src)
+
+        def gpsimd_copy(out, in_):
+            nc.gpsimd.tensor_scalar(out=out, in0=in_, scalar1=1.0, scalar2=0.0, op0=MULT, op1=ADD)
+
         def list_half(h):
             return offsets[:, h * LIST_COLS : (h + 1) * LIST_COLS]
 
-        v_words, v_scales = {}, {}
+        def half(h):
+            return slice(h * HALF, (h + 1) * HALF)
 
-        def gather_words(a, h):
-            v_words[a, h] = kept("v_words%d%d" % (a, h), [P, HALF], U32)
-            nc.vector.tensor_copy(v_words[a, h][:], tab_w[a][:].bitcast(U32).indirect(list_half(h)))
+        offsets = keep.tile([P, S // 16], U16, name="offsets")
+        nc.sync.dma_start(offsets[:], offs)
+        w4_raw = slot("A", "w4_raw", [P, 2, 2 * N], U8)
+        nc.sync.dma_start(out=w4_raw[:].bitcast(I32), in_=w4_words.rearrange("b p y -> p b y").bitcast(I32))
+        w1_raw = {}
+        w1_raw[0, 0] = load_rows("B", "w1_raw00", w1[0:G, 0:G])
+        tab_w = [load_table("C", 0)]
+        tab_s = slot("D", "tab_s", [P, T], U8)
+        nc.gpsimd.memset(tab_s[:].bitcast(I32), 0)
+        for q in range(4):
+            nc.scalar.dma_start(
+                out=tab_s[32 * q : 32 * q + 8, :].bitcast(I32), in_=tab_scales[:, 4 * q : 4 * q + 4, :].bitcast(I32)
+            )
+        w4_raw_s = slot("small", "w4_raw_s", [P, 2 * N], U8)
+        nc.gpsimd.memset(w4_raw_s[:].bitcast(I32), 0)
+        for q in range(4):
+            nc.gpsimd.dma_start(
+                out=w4_raw_s[32 * q : 32 * q + 4, :].bitcast(I32).rearrange("i (a n) -> i a n", a=2),
+                in_=w4_scales[:, 4 * q : 4 * q + 4, :].rearrange("a i n -> i a n").bitcast(I32),
+            )
+        bias = kept("bias", [P, 2, PACK], F32)
+        gains = kept("gains", [P, 2, PACK], F32)
+        nc.gpsimd.dma_start(out=bias[:], in_=b1.rearrange("(b p t) -> p b t", b=2, t=PACK))
+        nc.gpsimd.dma_start(out=gains[:], in_=gain.rearrange("(b p t) -> p b t", b=2, t=PACK))
 
-        def gather_scales(h):
-            v_scales[h] = kept("v_scales%d" % h, [P, HALF], U8)
-            nc.vector.tensor_copy(v_scales[h][:], tab_s[:].indirect(list_half(h)))
+        w4_codes = kept("w4_codes", [P, 2, 2 * N], U8)
+        for b in range(2):
+            nc.vector.tensor_copy(
+                out=w4_codes[:, b, :].rearrange("p (t m y) -> p m t y", t=PACK, y=2),
+                in_=w4_raw[:, b, :].rearrange("p (m t y) -> p m t y", t=PACK, y=2),
+            )
+        w1_raw[1, 0] = load_rows("A", "w1_raw10", w1[G : 2 * G, 0:G])
 
+        v_words = [kept("v_words%d" % a, [P, S], U32) for a in range(2)]
+        v_scales = kept("v_scales", [P, S], U8)
         w1_q = {}
 
         def quantize_w1(a, b, copy):
             grouped = grouped_tile()
-            dst, src = dealt_views(grouped, w1_raw[a, b])
-            copy(out=dst, in_=src)
-            w1_q[a, b] = quantize("w1_%d%d" % (a, b), grouped)
+            deal(copy, grouped[:], w1_raw[a, b][:])
+            w1_q[a, b] = quantize("w1_%d%d" % (a, b), grouped[:])
+
+        nc.vector.tensor_copy(v_scales[:], tab_s[:].indirect(offsets[:]))
+        tab_w.append(load_table("D", 1))
+        w4_plane = kept("w4_plane", [P, 2 * N], U8)
+        nc.vector.tensor_copy(
+            out=w4_plane[:].rearrange("p (a t m) -> p a m t", a=2, t=PACK),
+            in_=w4_raw_s[:].rearrange("p (a m t) -> p a m t", a=2, t=PACK),
+        )
+        nc.vector.tensor_copy(v_words[0][:], tab_w[0][:].bitcast(U32).indirect(offsets[:]))
+        quantize_w1(0, 0, nc.scalar.copy)
+        w1_raw[0, 1] = load_rows("B", "w1_raw01", w1[0:G, G : 2 * G])
+        w1_raw[1, 1] = load_rows("C", "w1_raw11", w1[G : 2 * G, G : 2 * G])
+        nc.vector.tensor_copy(v_words[1][:, half(0)], tab_w[1][:].bitcast(U32).indirect(list_half(0)))
+        quantize_w1(1, 0, nc.scalar.copy)
+        nc.vector.tensor_copy(v_words[1][:, half(1)], tab_w[1][:].bitcast(U32).indirect(list_half(1)))
+        tick_raw = [load_rows("A", "tick_raw0", tick[:, half(0)])]
+        load_page("D", 0)
 
         sig = {}
 
-        def stage_one(b, h):
-            sig[b, h] = ring.tile([P, PACK, HALF], F32, name="sig", tag="sig", bufs=4, align_bytes=64)
+        def stage_one(b, h, tag):
+            sig[b, h] = slot(tag, "sig%d%d" % (b, h), [P, PACK, HALF], F32)
             for t in range(PACK):
                 cols = slice(t * P, (t + 1) * P)
                 acc = psum.tile([P, HALF], F32, name="x_acc", tag="x_acc")
@@ -131,192 +162,206 @@ def tile_list_gallery_state_damping_kernel(
                         out=acc[:],
                         lhsT=codes[:, cols].bitcast(FP8X4),
                         lhsT_scale=scales[:, cols],
-                        rhs=v_words[a, h][:].bitcast(FP8X4),
-                        rhs_scale=v_scales[h][4 * a : P, :],
+                        rhs=v_words[a][:, half(h)].bitcast(FP8X4),
+                        rhs_scale=v_scales[4 * a : P, half(h)],
                         start=(a == 0),
                         stop=(a == 1),
                     )
                 nc.scalar.activation(out=sig[b, h][:, t, :], in_=acc[:], func=ACT.Sigmoid, bias=bias[:, b, t : t + 1])
 
-        h_q = {}
-
-        def quantize_h(b, h, grouped):
-            dst, src = woven_views(grouped[:], sig[b, h][:], run=2)
-            factor = gains[:, b, :].unsqueeze(1).unsqueeze(3).broadcast_to([P, HALF // 2, PACK, 2])
-            nc.vector.tensor_tensor(out=dst, in0=src, in1=factor, op=MULT)
-            h_q[b, h] = quantize("h_%d%d" % (b, h), grouped)
-
-        def quantize_h_on_scalar(b, h, grouped):
-            scaled = held("scaled", [P, PACK, HALF], BF16, "last_square")
+        def scale_on_scalar(b, h, scaled):
             for t in range(PACK):
                 nc.scalar.activation(
                     out=scaled[:, t, :], in_=sig[b, h][:, t, :], func=ACT.Copy, scale=gains[:, b, t : t + 1]
                 )
-            dst, src = woven_views(grouped[:], scaled[:])
-            nc.scalar.copy(out=dst, in_=src)
-            h_q[b, h] = quantize("h_%d%d" % (b, h), grouped)
 
-        tick_q = {}
+        def scale_on_gpsimd(b, h, scaled):
+            for t in range(PACK):
+                nc.gpsimd.tensor_scalar(
+                    out=scaled[:, t, :],
+                    in0=sig[b, h][:, t, :],
+                    scalar1=gains[:, b, t : t + 1],
+                    scalar2=0.0,
+                    op0=MULT,
+                    op1=ADD,
+                )
 
-        def quantize_tick(h, copy, grouped):
-            dst, src = woven_views(grouped[:], tick_raw[h][:])
-            copy(out=dst, in_=src)
-            tick_q[h] = quantize("tick_%d" % h, grouped)
+        def weave_on_gpsimd(grouped, scaled):
+            for c in range(2):
+                lo, hi = c * HALF // 2, (c + 1) * HALF // 2
+                weave(gpsimd_copy, grouped[:, lo * PACK : hi * PACK], scaled[:, :, lo:hi])
 
         picked = {}
 
-        def gather_states(h):
-            into = keep.tile([P, PACK, HALF], F32, name="picked", tag="late%d" % h, align_bytes=64)
-            for t in range(PACK):
-                picked[t, h] = into[:, t, :]
-                nc.vector.tensor_copy(picked[t, h], pages[t][:].indirect(list_half(h)))
+        def gather_page(t, tag):
+            into = slot(tag, "picked%d" % t, [P, S], F32)
+            nc.vector.tensor_copy(into[:], pages[t][:].indirect(offsets[:]))
+            for h in range(2):
+                picked[t, h] = into[:, half(h)]
 
-        damp = {}
+        def gather_half(t, h, into):
+            nc.vector.tensor_copy(into[:], pages[t][:].indirect(list_half(h)))
+            picked[t, h] = into[:]
+
+        h_q, tick_q = {}, {}
+        e_acc, root, damp = {}, {}, {}
 
         def stage_two(t, h):
             cols = slice(t * P, (t + 1) * P)
-            acc = psum.tile([P, HALF], F32, name="e_acc", tag="e_acc")
-            nc.tensor.matmul_mx(
-                out=acc[:],
-                lhsT=w3_q[0][:, cols].bitcast(FP8X4),
-                lhsT_scale=w3_q[1][:, cols],
-                rhs=tick_q[h][0][:].bitcast(FP8X4),
-                rhs_scale=tick_q[h][1][:],
-                start=True,
-                stop=False,
-            )
+            e_acc[t, h] = psum.tile([P, HALF], F32, name="e_acc", tag="e_acc")
             for b in range(2):
                 nc.tensor.matmul_mx(
-                    out=acc[:],
-                    lhsT=w4_codes[b][:, 2 * t * P : 2 * (t + 1) * P].bitcast(FP4X4),
-                    lhsT_scale=w4_planes[b][:, cols],
-                    rhs=h_q[b, h][0][:].bitcast(FP8X4),
-                    rhs_scale=h_q[b, h][1][:],
-                    start=False,
-                    stop=(b == 1),
+                    out=e_acc[t, h][:],
+                    lhsT=w4_codes[:, b, 2 * t * P : 2 * (t + 1) * P].bitcast(FP4X4),
+                    lhsT_scale=w4_plane[:, b * N + t * P : b * N + (t + 1) * P],
+                    rhs=h_q[b, h][0].bitcast(FP8X4),
+                    rhs_scale=h_q[b, h][1],
+                    start=(b == 0),
+                    stop=False,
                 )
-            if (t, h) == (PACK - 1, 0):
-                square = held("square", [P, HALF], F32, "last_square")
-                root = held("root", [P, HALF], F32, "last_root")
-            else:
-                square = ring.tile([P, HALF], F32, name="square", tag="square", bufs=4)
-                root = ring.tile([P, HALF], F32, name="root", tag="root", bufs=4)
-            nc.scalar.activation(out=square[:], in_=acc[:], func=ACT.Square)
-            nc.scalar.activation(out=root[:], in_=square[:], func=ACT.Abs_reciprocal_sqrt, bias=1.0)
-            damp[t, h] = ring.tile([P, HALF], F32, name="damp", tag="damp", bufs=4)
-            nc.scalar.activation(out=damp[t, h][:], in_=root[:], func=ACT.Square)
+            nc.tensor.matmul_mx(
+                out=e_acc[t, h][:],
+                lhsT=w3_q[0][:, cols].bitcast(FP8X4),
+                lhsT_scale=w3_q[1][:, cols],
+                rhs=tick_q[h][0].bitcast(FP8X4),
+                rhs_scale=tick_q[h][1],
+                start=False,
+                stop=True,
+            )
+
+        def inverse_root(t, h):
+            last = (t, h) == (PACK - 1, 1)
+            tag = {(1, 1): "sig11", (3, 1): "sig01"}.get((t, h), "square")
+            square = slot(tag, "square", [P, HALF], F32, bufs=2 if tag == "square" else 1)
+            nc.scalar.activation(out=square[:], in_=e_acc[t, h][:], func=ACT.Square)
+            root[t, h] = slot("sig10" if last else "root", "root", [P, HALF], F32, bufs=1 if last else 3)
+            nc.scalar.activation(out=root[t, h][:], in_=square[:], func=ACT.Abs_reciprocal_sqrt, bias=1.0)
+
+        def damping(t, h):
+            last = (t, h) == (PACK - 1, 1)
+            damp[t, h] = slot("E" if last else "damp", "damp", [P, HALF], F32, bufs=1 if last else 5)
+            nc.scalar.activation(out=damp[t, h][:], in_=root[t, h][:], func=ACT.Square)
 
         def scatter_state(t, h):
             nc.vector.tensor_tensor(pages[t][:].indirect(list_half(h)), picked[t, h], damp[t, h][:], MULT)
 
-        w4_codes = []
-        for b in range(2):
-            w4_codes.append(kept("w4_codes%d" % b, [P, 2 * N], U8))
-            nc.vector.tensor_copy(
-                out=w4_codes[b][:].rearrange("p (t m y) -> p m t y", t=PACK, y=2),
-                in_=w4_raw[b][:].rearrange("p (m t y) -> p m t y", t=PACK, y=2),
-            )
-        w1_raw[1, 0] = load_rows("w1_raw10", w1[G : 2 * G, 0:G])
-        tab_w.append(load_table(1))
-        gather_words(0, 0)
-        gather_words(0, 1)
-        gather_scales(0)
-        gather_scales(1)
-        w1_raw[0, 1] = load_rows("w1_raw01", w1[0:G, G : 2 * G])
-        quantize_w1(0, 0, nc.scalar.copy)
-        w1_raw[1, 1] = load_rows("w1_raw11", w1[G : 2 * G, G : 2 * G])
-        gather_words(1, 0)
-        quantize_w1(1, 0, nc.scalar.copy)
-        w3_raw = load_rows("w3_raw", w3)
-        w4_raw_s = scale_rows("w4_raw_s", [P, 2 * N])
-        for q in range(4):
-            nc.sync.dma_start(
-                out=w4_raw_s[32 * q : 32 * q + 4, :].bitcast(I32).rearrange("i (a n) -> i a n", a=2),
-                in_=w4_scales[:, 4 * q : 4 * q + 4, :].rearrange("a i n -> i a n").bitcast(I32),
-            )
-        gather_words(1, 1)
-        tick_raw = [load_rows("tick_raw0", tick[:, 0:HALF])]
+        def whole(pair):
+            return pair[0][:], pair[1][:]
+
+        stage_one(0, 0, "E")
         quantize_w1(0, 1, nc.vector.tensor_copy)
-        stage_one(0, 0)
-        g_rows = gT.rearrange("(p t) m -> t p m", t=PACK)
-        pages = []
-
-        def load_page(t):
-            pages.append(staged("page%d" % t, [P, T], F32))
-            nc.sync.dma_start(out=pages[t][:], in_=g_rows[t])
-
-        load_page(0)
+        w3_raw = load_rows("B", "w3_raw", w3)
         quantize_w1(1, 1, nc.vector.tensor_copy)
-        load_page(1)
-        w4_plane = kept("w4_plane", [P, 2 * N], U8)
-        nc.vector.tensor_copy(
-            out=w4_plane[:].rearrange("p (a t m) -> p a m t", a=2, t=PACK),
-            in_=w4_raw_s[:].rearrange("p (a m t) -> p a m t", a=2, t=PACK),
-        )
-        w4_planes = [w4_plane[:, 0:N], w4_plane[:, N : 2 * N]]
-        quantize_h_on_scalar(0, 0, grouped_tile())
-        stage_one(1, 0)
-        stage_one(0, 1)
+        load_page("C", 1)
+        scaled = slot("scaled", "scaled00", [P, PACK, HALF], BF16)
+        scale_on_scalar(0, 0, scaled)
+        load_page("E", 2)
+        grouped = slot("h00_grouped", "tick_grouped", [P, G * PACK], BF16)
+        weave(nc.vector.tensor_copy, grouped[:], tick_raw[0][:])
+        tick_q[0] = whole(quantize("tick0", grouped[:]))
+        load_page("A", 3)
+        gather_page(0, "picked0")
+        grouped = slot("h00_grouped", "h00_grouped", [P, G * PACK], BF16)
+        weave_on_gpsimd(grouped, scaled)
+        h_q[0, 0] = whole(quantize("h00", grouped[:]))
+        stage_one(1, 0, "sig10")
         grouped = grouped_tile()
-        dst, src = dealt_views(grouped, w3_raw)
-        nc.vector.tensor_copy(out=dst, in_=src)
-        w3_q = quantize("w3", grouped)
-        load_page(2)
-        quantize_tick(0, nc.vector.tensor_copy, held("tick_grouped0", [P, G * PACK], BF16, "late_tick"))
-        load_page(3)
-        quantize_h(1, 0, keep.tile([P, G * PACK], BF16, name="last_h", tag="late0", align_bytes=64))
-        stage_one(1, 1)
-        late_tick = keep.tile([P, PACK, HALF], F32, name="tick_raw1", tag="late_tick", align_bytes=64)
-        nc.sync.dma_start(out=late_tick[:], in_=tick[:, HALF : 2 * HALF].rearrange("(p j) c -> p j c", j=PACK))
-        tick_raw.append(late_tick)
+        dst, src = woven_views(grouped[:], sig[1, 0][:], run=2)
+        factor = gains[:, 1, :].unsqueeze(1).unsqueeze(3).broadcast_to([P, HALF // 2, PACK, 2])
+        nc.vector.tensor_tensor(out=dst, in0=src, in1=factor, op=MULT)
+        h_q[1, 0] = whole(quantize("h10", grouped[:]))
+        grouped = slot("w3_grouped", "w3_grouped", [P, G * PACK], BF16)
+        deal(nc.scalar.copy, grouped[:], w3_raw[:])
+        w3_q = quantize("w3", grouped[:])
+        tick_raw.append(load_rows("B", "tick_raw1", tick[:, half(1)]))
+        stage_one(0, 1, "sig01")
+        stage_one(1, 1, "sig11")
+        gather_page(1, "h00_grouped")
+        gather_half(2, 1, kept("picked21", [P, HALF], F32))
+        gather_page(3, "picked3")
         for t in range(PACK):
             stage_two(t, 0)
-        gather_states(0)
+
+        inverse_root(0, 0)
+        damping(0, 0)
         scatter_state(0, 0)
+        late = slot("late", "late_grouped", [P, 2 * G * PACK], BF16)
+        scaled = slot("w3_grouped", "scaled01", [P, PACK, HALF], BF16)
+        scale_on_gpsimd(0, 1, scaled)
+        weave_on_gpsimd(late[:, 0 : G * PACK], scaled)
+        inverse_root(1, 0)
+        damping(1, 0)
         scatter_state(1, 0)
-        quantize_h_on_scalar(0, 1, grouped_tile())
-        scatter_state(2, 0)
-        scatter_state(3, 0)
-        quantize_tick(1, nc.scalar.copy, held("tick_grouped1", [P, G * PACK], BF16, "last_root"))
-        quantize_h_on_scalar(1, 1, keep.tile([P, G * PACK], BF16, name="last_h", tag="late1", align_bytes=64))
-        gather_states(1)
+        grouped = grouped_tile()
+        weave(nc.scalar.copy, grouped[:], tick_raw[1][:])
+        tick_q[1] = whole(quantize("tick1", grouped[:]))
+        scaled = slot("scaled", "scaled11", [P, PACK, HALF], BF16)
+        scale_on_scalar(1, 1, scaled)
+        weave(nc.scalar.copy, late[:, G * PACK : 2 * G * PACK], scaled[:])
+        codes, scales = quantize("late", late[:], width=2 * G)
+        for b in range(2):
+            h_q[b, 1] = codes[:, b * G : (b + 1) * G], scales[:, b * G : (b + 1) * G]
+        gather_half(2, 0, slot("late", "picked20", [P, HALF], F32))
+        for t in (2, 3):
+            inverse_root(t, 0)
+            damping(t, 0)
+            scatter_state(t, 0)
 
         y_rows = out_0.rearrange("(p t) m -> t p m", t=PACK)
-        spans = [(0, 512), (512, 1024), (1024, 1536), (1536, 1792), (1792, 2048)]
-        rounded = [kept("rounded%d" % lo, [P, PACK, hi - lo], BF16) for lo, hi in spans]
-        for t in range(PACK):
+        order = (2, 0, 1, 3)
+        for t in order:
             stage_two(t, 1)
-        for t in range(PACK):
+
+        def finish_page(t):
+            damping(t, 1)
             scatter_state(t, 1)
             nc.sync.dma_start(out=y_rows[t], in_=pages[t][:])
-            for c, (lo, hi) in enumerate(spans):
-                copy = nc.vector.tensor_copy if (t, c) == (PACK - 1, 0) else nc.scalar.copy
-                copy(out=rounded[c][:, t, :], in_=pages[t][:, lo:hi])
+
+        for t in order[:3]:
+            inverse_root(t, 1)
+            finish_page(t)
+        inverse_root(3, 1)
+
+        pairs = [slot(tag, "pairs", [P, 2, T // 2, 2], BF16) for tag in ("sig01", "sig11")]
+
+        def round_page(copy, t, side, lo, hi):
+            base = side * T // 2
+            copy(out=pairs[side][:, t // 2, lo:hi, t % 2], in_=pages[t][:, base + lo : base + hi])
+
+        for side in range(2):
+            round_page(nc.scalar.copy, 2, side, 0, T // 2)
+        finish_page(3)
+        for t in (0, 1):
+            for side in range(2):
+                round_page(nc.scalar.copy, t, side, 0, T // 2)
 
         y_scales = kept("y_scales", [P, T], U8)
         y_words = out_1[0].rearrange("p m t -> p (m t)").bitcast(I32)
-        woven = [kept("woven%d" % lo, [P, (hi - lo) * PACK], BF16) for lo, hi in spans]
+        woven = [slot("woven", "woven", [P, SPAN * PACK], BF16, bufs=4) for c in range(T // SPAN)]
 
-        def weave(c, lo, hi, copy):
-            dst, src = woven_views(woven[c][:, lo * PACK : hi * PACK], rounded[c][:, :, lo:hi])
-            copy(out=dst, in_=src)
+        def weave_words(copy, c):
+            side, lo = divmod(c * SPAN, T // 2)
+            words = pairs[side][:].rearrange("p u c e -> p (u c e)").bitcast(F32).rearrange("p (u c) -> p u c", u=2)
+            copy(
+                out=woven[c][:].bitcast(F32).rearrange("p (c i u) -> p c u i", i=4, u=2),
+                in_=words[:, :, lo : lo + SPAN].rearrange("p u (c i) -> p c u i", i=4),
+            )
 
         def quantize_y(c):
-            lo, hi = spans[c]
-            codes = kept("y_codes%d" % lo, [P, hi - lo], I32)
-            nc.vector.quantize_mx(out=codes[:].bitcast(FP8X4), scales=y_scales[:, lo:hi], in_=woven[c][:])
-            nc.sync.dma_start(out=y_words[:, lo:hi], in_=codes[:])
+            cols = slice(c * SPAN, (c + 1) * SPAN)
+            codes = kept("y_codes%d" % c, [P, SPAN], I32)
+            nc.vector.quantize_mx(out=codes[:].bitcast(FP8X4), scales=y_scales[:, cols], in_=woven[c][:])
+            nc.sync.dma_start(out=y_words[:, cols], in_=codes[:])
 
-        weave(0, 0, 512, nc.vector.tensor_copy)
-        weave(1, 0, 512, nc.vector.tensor_copy)
-        weave(2, 256, 512, nc.scalar.copy)
-        weave(3, 0, 256, nc.scalar.copy)
-        weave(4, 0, 256, nc.scalar.copy)
-        quantize_y(0)
-        weave(2, 0, 256, nc.vector.tensor_copy)
-        for c in range(1, len(spans)):
+        round_page(nc.vector.tensor_copy, 3, 0, 0, T // 2)
+        weave_words(nc.vector.tensor_copy, 0)
+        weave_words(nc.vector.tensor_copy, 1)
+        for c in (2, 3):
+            round_page(nc.scalar.copy, 3, 1, (c - 2) * SPAN, (c - 1) * SPAN)
+            weave_words(nc.scalar.copy, c)
+        for c in range(T // SPAN):
             quantize_y(c)
         for q in range(4):
-            nc.sync.dma_start(
+            nc.scalar.dma_start(
                 out=out_2[0, 4 * q : 4 * q + 4, :].bitcast(I32), in_=y_scales[32 * q : 32 * q + 4, :].bitcast(I32)
             )

@@ -31,7 +31,7 @@ def tile_list_gallery_state_damping_kernel(
     nc = tc.nc
     with ExitStack() as ctx:
         keep = ctx.enter_context(tc.tile_pool(name="keep", bufs=1))
-        psum = ctx.enter_context(tc.psum_pool(name="psum", bufs=4))
+        psum = ctx.enter_context(tc.psum_pool(name="psum", bufs=8))
 
         def kept(name, shape, dtype):
             return keep.tile(shape, dtype, name=name, align_bytes=64)
@@ -92,23 +92,17 @@ def tile_list_gallery_state_damping_kernel(
 
         offsets = keep.tile([P, S // 16], U16, name="offsets")
         nc.sync.dma_start(offsets[:], offs)
-        w4_raw = slot("A", "w4_raw", [P, 2, 2 * N], U8)
-        nc.sync.dma_start(out=w4_raw[:].bitcast(I32), in_=w4_words.rearrange("b p y -> p b y").bitcast(I32))
+        w4_raw = [slot(tag, "w4_raw", [P, 2 * N], U8) for tag in "AD"]
+        for b in range(2):
+            nc.sync.dma_start(out=w4_raw[b][:].bitcast(I32), in_=w4_words[b].bitcast(I32))
         w1_raw = {}
-        w1_raw[0, 0] = load_rows("B", "w1_raw00", w1[0:G, 0:G])
         tab_w = [load_table("C", 0)]
-        tab_s = slot("D", "tab_s", [P, T], U8)
+        w1_raw[0, 0] = load_rows("B", "w1_raw00", w1[0:G, 0:G])
+        tab_s = slot("small", "tab_s", [P, T], U8)
         nc.gpsimd.memset(tab_s[:].bitcast(I32), 0)
         for q in range(4):
-            nc.scalar.dma_start(
+            nc.sync.dma_start(
                 out=tab_s[32 * q : 32 * q + 8, :].bitcast(I32), in_=tab_scales[:, 4 * q : 4 * q + 4, :].bitcast(I32)
-            )
-        w4_raw_s = slot("small", "w4_raw_s", [P, 2 * N], U8)
-        nc.gpsimd.memset(w4_raw_s[:].bitcast(I32), 0)
-        for q in range(4):
-            nc.gpsimd.dma_start(
-                out=w4_raw_s[32 * q : 32 * q + 4, :].bitcast(I32).rearrange("i (a n) -> i a n", a=2),
-                in_=w4_scales[:, 4 * q : 4 * q + 4, :].rearrange("a i n -> i a n").bitcast(I32),
             )
         bias = kept("bias", [P, 2, PACK], F32)
         gains = kept("gains", [P, 2, PACK], F32)
@@ -119,9 +113,10 @@ def tile_list_gallery_state_damping_kernel(
         for b in range(2):
             nc.vector.tensor_copy(
                 out=w4_codes[:, b, :].rearrange("p (t m y) -> p m t y", t=PACK, y=2),
-                in_=w4_raw[:, b, :].rearrange("p (m t y) -> p m t y", t=PACK, y=2),
+                in_=w4_raw[b][:].rearrange("p (m t y) -> p m t y", t=PACK, y=2),
             )
         w1_raw[1, 0] = load_rows("A", "w1_raw10", w1[G : 2 * G, 0:G])
+        tab_w.append(load_table("D", 1))
 
         v_words = [kept("v_words%d" % a, [P, S], U32) for a in range(2)]
         v_scales = kept("v_scales", [P, S], U8)
@@ -132,17 +127,18 @@ def tile_list_gallery_state_damping_kernel(
             deal(copy, grouped[:], w1_raw[a, b][:])
             w1_q[a, b] = quantize("w1_%d%d" % (a, b), grouped[:])
 
-        nc.vector.tensor_copy(v_scales[:], tab_s[:].indirect(offsets[:]))
-        tab_w.append(load_table("D", 1))
-        w4_plane = kept("w4_plane", [P, 2 * N], U8)
-        nc.vector.tensor_copy(
-            out=w4_plane[:].rearrange("p (a t m) -> p a m t", a=2, t=PACK),
-            in_=w4_raw_s[:].rearrange("p (a m t) -> p a m t", a=2, t=PACK),
-        )
         nc.vector.tensor_copy(v_words[0][:], tab_w[0][:].bitcast(U32).indirect(offsets[:]))
+        nc.vector.tensor_copy(v_scales[:], tab_s[:].indirect(offsets[:]))
+        w4_raw_s = slot("small", "w4_raw_s", [P, 2 * N], U8)
+        nc.gpsimd.memset(w4_raw_s[:].bitcast(I32), 0)
+        for q in range(4):
+            nc.sync.dma_start(
+                out=w4_raw_s[32 * q : 32 * q + 4, :].bitcast(I32).rearrange("i (a n) -> i a n", a=2),
+                in_=w4_scales[:, 4 * q : 4 * q + 4, :].rearrange("a i n -> i a n").bitcast(I32),
+            )
         quantize_w1(0, 0, nc.scalar.copy)
-        w1_raw[0, 1] = load_rows("B", "w1_raw01", w1[0:G, G : 2 * G])
-        w1_raw[1, 1] = load_rows("C", "w1_raw11", w1[G : 2 * G, G : 2 * G])
+        w1_raw[0, 1] = load_rows("C", "w1_raw01", w1[0:G, G : 2 * G])
+        w1_raw[1, 1] = load_rows("B", "w1_raw11", w1[G : 2 * G, G : 2 * G])
         nc.vector.tensor_copy(v_words[1][:, half(0)], tab_w[1][:].bitcast(U32).indirect(list_half(0)))
         quantize_w1(1, 0, nc.scalar.copy)
         nc.vector.tensor_copy(v_words[1][:, half(1)], tab_w[1][:].bitcast(U32).indirect(list_half(1)))
@@ -155,7 +151,7 @@ def tile_list_gallery_state_damping_kernel(
             sig[b, h] = slot(tag, "sig%d%d" % (b, h), [P, PACK, HALF], F32)
             for t in range(PACK):
                 cols = slice(t * P, (t + 1) * P)
-                acc = psum.tile([P, HALF], F32, name="x_acc", tag="x_acc")
+                acc = psum.tile([P, HALF], F32, name="x_acc", tag="bank")
                 for a in range(2):
                     codes, scales = w1_q[a, b]
                     nc.tensor.matmul_mx(
@@ -189,7 +185,10 @@ def tile_list_gallery_state_damping_kernel(
         def weave_on_gpsimd(grouped, scaled):
             for c in range(2):
                 lo, hi = c * HALF // 2, (c + 1) * HALF // 2
-                weave(gpsimd_copy, grouped[:, lo * PACK : hi * PACK], scaled[:, :, lo:hi])
+                gpsimd_copy(
+                    out=grouped[:, lo * PACK : hi * PACK].rearrange("p (c t) -> p c t", t=PACK),
+                    in_=scaled[:, :, lo:hi].rearrange("p t c -> p c t"),
+                )
 
         picked = {}
 
@@ -200,15 +199,15 @@ def tile_list_gallery_state_damping_kernel(
                 picked[t, h] = into[:, half(h)]
 
         def gather_half(t, h, into):
-            nc.vector.tensor_copy(into[:], pages[t][:].indirect(list_half(h)))
-            picked[t, h] = into[:]
+            nc.vector.tensor_copy(into, pages[t][:].indirect(list_half(h)))
+            picked[t, h] = into
 
         h_q, tick_q = {}, {}
         e_acc, root, damp = {}, {}, {}
 
         def stage_two(t, h):
             cols = slice(t * P, (t + 1) * P)
-            e_acc[t, h] = psum.tile([P, HALF], F32, name="e_acc", tag="e_acc")
+            e_acc[t, h] = psum.tile([P, HALF], F32, name="e_acc", tag="bank")
             for b in range(2):
                 nc.tensor.matmul_mx(
                     out=e_acc[t, h][:],
@@ -237,22 +236,26 @@ def tile_list_gallery_state_damping_kernel(
             root[t, h] = slot("sig10" if last else "root", "root", [P, HALF], F32, bufs=1 if last else 3)
             nc.scalar.activation(out=root[t, h][:], in_=square[:], func=ACT.Abs_reciprocal_sqrt, bias=1.0)
 
-        def damping(t, h):
-            last = (t, h) == (PACK - 1, 1)
-            damp[t, h] = slot("E" if last else "damp", "damp", [P, HALF], F32, bufs=1 if last else 5)
-            nc.scalar.activation(out=damp[t, h][:], in_=root[t, h][:], func=ACT.Square)
+        def damping(t, h, into=None):
+            damp[t, h] = slot("damp", "damp", [P, HALF], F32, bufs=5)[:] if into is None else into
+            nc.scalar.activation(out=damp[t, h], in_=root[t, h][:], func=ACT.Square)
 
         def scatter_state(t, h):
-            nc.vector.tensor_tensor(pages[t][:].indirect(list_half(h)), picked[t, h], damp[t, h][:], MULT)
+            nc.vector.tensor_tensor(pages[t][:].indirect(list_half(h)), picked[t, h], damp[t, h], MULT)
 
         def whole(pair):
             return pair[0][:], pair[1][:]
 
         stage_one(0, 0, "E")
         quantize_w1(0, 1, nc.vector.tensor_copy)
-        w3_raw = load_rows("B", "w3_raw", w3)
+        w3_raw = load_rows("C", "w3_raw", w3)
+        w4_plane = kept("w4_plane", [P, 2 * N], U8)
+        nc.vector.tensor_copy(
+            out=w4_plane[:].rearrange("p (a t m) -> p a m t", a=2, t=PACK),
+            in_=w4_raw_s[:].rearrange("p (a m t) -> p a m t", a=2, t=PACK),
+        )
         quantize_w1(1, 1, nc.vector.tensor_copy)
-        load_page("C", 1)
+        load_page("B", 1)
         scaled = slot("scaled", "scaled00", [P, PACK, HALF], BF16)
         scale_on_scalar(0, 0, scaled)
         load_page("E", 2)
@@ -265,7 +268,7 @@ def tile_list_gallery_state_damping_kernel(
         weave_on_gpsimd(grouped, scaled)
         h_q[0, 0] = whole(quantize("h00", grouped[:]))
         stage_one(1, 0, "sig10")
-        grouped = grouped_tile()
+        grouped = slot("h10_grouped", "h10_grouped", [P, G * PACK], BF16)
         dst, src = woven_views(grouped[:], sig[1, 0][:], run=2)
         factor = gains[:, 1, :].unsqueeze(1).unsqueeze(3).broadcast_to([P, HALF // 2, PACK, 2])
         nc.vector.tensor_tensor(out=dst, in0=src, in1=factor, op=MULT)
@@ -273,11 +276,11 @@ def tile_list_gallery_state_damping_kernel(
         grouped = slot("w3_grouped", "w3_grouped", [P, G * PACK], BF16)
         deal(nc.scalar.copy, grouped[:], w3_raw[:])
         w3_q = quantize("w3", grouped[:])
-        tick_raw.append(load_rows("B", "tick_raw1", tick[:, half(1)]))
+        tick_raw.append(load_rows("C", "tick_raw1", tick[:, half(1)]))
         stage_one(0, 1, "sig01")
         stage_one(1, 1, "sig11")
-        gather_page(1, "h00_grouped")
-        gather_half(2, 1, kept("picked21", [P, HALF], F32))
+        gather_page(1, "w3_grouped")
+        gather_half(2, 1, kept("picked21", [P, HALF], F32)[:])
         gather_page(3, "picked3")
         for t in range(PACK):
             stage_two(t, 0)
@@ -286,25 +289,26 @@ def tile_list_gallery_state_damping_kernel(
         damping(0, 0)
         scatter_state(0, 0)
         late = slot("late", "late_grouped", [P, 2 * G * PACK], BF16)
-        scaled = slot("w3_grouped", "scaled01", [P, PACK, HALF], BF16)
+        scaled = slot("h10_grouped", "scaled01", [P, PACK, HALF], BF16)
         scale_on_gpsimd(0, 1, scaled)
         weave_on_gpsimd(late[:, 0 : G * PACK], scaled)
         inverse_root(1, 0)
         damping(1, 0)
         scatter_state(1, 0)
+        scaled = slot("scaled", "scaled11", [P, PACK, HALF], BF16)
+        scale_on_scalar(1, 1, scaled)
         grouped = grouped_tile()
         weave(nc.scalar.copy, grouped[:], tick_raw[1][:])
         tick_q[1] = whole(quantize("tick1", grouped[:]))
-        scaled = slot("scaled", "scaled11", [P, PACK, HALF], BF16)
-        scale_on_scalar(1, 1, scaled)
         weave(nc.scalar.copy, late[:, G * PACK : 2 * G * PACK], scaled[:])
         codes, scales = quantize("late", late[:], width=2 * G)
         for b in range(2):
             h_q[b, 1] = codes[:, b * G : (b + 1) * G], scales[:, b * G : (b + 1) * G]
-        gather_half(2, 0, slot("late", "picked20", [P, HALF], F32))
+        held = slot("late", "held", [P, 2, HALF], F32)
+        gather_half(2, 0, held[:, 0, :])
         for t in (2, 3):
             inverse_root(t, 0)
-            damping(t, 0)
+            damping(t, 0, held[:, 1, :] if t == 3 else None)
             scatter_state(t, 0)
 
         y_rows = out_0.rearrange("(p t) m -> t p m", t=PACK)
@@ -313,7 +317,7 @@ def tile_list_gallery_state_damping_kernel(
             stage_two(t, 1)
 
         def finish_page(t):
-            damping(t, 1)
+            damping(t, 1, slot("E", "last_damp", [P, HALF], F32)[:] if t == 3 else None)
             scatter_state(t, 1)
             nc.sync.dma_start(out=y_rows[t], in_=pages[t][:])
 
@@ -336,30 +340,32 @@ def tile_list_gallery_state_damping_kernel(
                 round_page(nc.scalar.copy, t, side, 0, T // 2)
 
         y_scales = kept("y_scales", [P, T], U8)
+        y_codes = kept("y_codes", [P, T], I32)
         y_words = out_1[0].rearrange("p m t -> p (m t)").bitcast(I32)
-        woven = [slot("woven", "woven", [P, SPAN * PACK], BF16, bufs=4) for c in range(T // SPAN)]
+        spans = [(0, 512), (512, 1024), (1024, 1536), (1536, 1792), (1792, 2048)]
+        woven = [kept("woven%d" % lo, [P, (hi - lo) * PACK], BF16) for lo, hi in spans]
 
         def weave_words(copy, c):
-            side, lo = divmod(c * SPAN, T // 2)
+            side, lo = divmod(spans[c][0], T // 2)
+            hi = lo + spans[c][1] - spans[c][0]
             words = pairs[side][:].rearrange("p u c e -> p (u c e)").bitcast(F32).rearrange("p (u c) -> p u c", u=2)
             copy(
                 out=woven[c][:].bitcast(F32).rearrange("p (c i u) -> p c u i", i=4, u=2),
-                in_=words[:, :, lo : lo + SPAN].rearrange("p u (c i) -> p c u i", i=4),
+                in_=words[:, :, lo:hi].rearrange("p u (c i) -> p c u i", i=4),
             )
 
         def quantize_y(c):
-            cols = slice(c * SPAN, (c + 1) * SPAN)
-            codes = kept("y_codes%d" % c, [P, SPAN], I32)
-            nc.vector.quantize_mx(out=codes[:].bitcast(FP8X4), scales=y_scales[:, cols], in_=woven[c][:])
-            nc.sync.dma_start(out=y_words[:, cols], in_=codes[:])
+            lo, hi = spans[c]
+            nc.vector.quantize_mx(out=y_codes[:, lo:hi].bitcast(FP8X4), scales=y_scales[:, lo:hi], in_=woven[c][:])
+            if c > 0:
+                lo = lo if c > 1 else 0
+                nc.sync.dma_start(out=y_words[:, lo:hi], in_=y_codes[:, lo:hi])
 
         round_page(nc.vector.tensor_copy, 3, 0, 0, T // 2)
-        weave_words(nc.vector.tensor_copy, 0)
-        weave_words(nc.vector.tensor_copy, 1)
-        for c in (2, 3):
-            round_page(nc.scalar.copy, 3, 1, (c - 2) * SPAN, (c - 1) * SPAN)
-            weave_words(nc.scalar.copy, c)
-        for c in range(T // SPAN):
+        round_page(nc.scalar.copy, 3, 1, 0, T // 2)
+        for c in range(len(spans)):
+            weave_words(nc.vector.tensor_copy if c < 2 else nc.scalar.copy, c)
+        for c in range(len(spans)):
             quantize_y(c)
         for q in range(4):
             nc.scalar.dma_start(

@@ -56,9 +56,6 @@ def tile_list_gallery_state_damping_kernel(
             pages[t] = slot(tag, "page%d" % t, [P, T], F32)
             nc.sync.dma_start(out=pages[t][:], in_=g_rows[t])
 
-        def grouped_tile():
-            return slot("grouped", "grouped", [P, G * PACK], BF16, bufs=3)
-
         def quantize(name, grouped, width=G):
             codes = kept(name + "_codes", [P, width], U32)
             scales = kept(name + "_scales", [P, width], U8)
@@ -80,9 +77,6 @@ def tile_list_gallery_state_damping_kernel(
         def weave(copy, grouped, raw):
             dst, src = woven_views(grouped, raw)
             copy(out=dst, in_=src)
-
-        def gpsimd_copy(out, in_):
-            nc.gpsimd.tensor_scalar(out=out, in0=in_, scalar1=1.0, scalar2=0.0, op0=MULT, op1=ADD)
 
         def list_half(h):
             return offsets[:, h * LIST_COLS : (h + 1) * LIST_COLS]
@@ -122,8 +116,8 @@ def tile_list_gallery_state_damping_kernel(
         v_scales = kept("v_scales", [P, S], U8)
         w1_q = {}
 
-        def quantize_w1(a, b, copy):
-            grouped = grouped_tile()
+        def quantize_w1(a, b, copy, tag):
+            grouped = slot(tag, "w1_grouped", [P, G * PACK], BF16)
             deal(copy, grouped[:], w1_raw[a, b][:])
             w1_q[a, b] = quantize("w1_%d%d" % (a, b), grouped[:])
 
@@ -136,14 +130,14 @@ def tile_list_gallery_state_damping_kernel(
                 out=w4_raw_s[32 * q : 32 * q + 4, :].bitcast(I32).rearrange("i (a n) -> i a n", a=2),
                 in_=w4_scales[:, 4 * q : 4 * q + 4, :].rearrange("a i n -> i a n").bitcast(I32),
             )
-        quantize_w1(0, 0, nc.scalar.copy)
+        quantize_w1(0, 0, nc.scalar.copy, "h10_grouped")
         w1_raw[0, 1] = load_rows("C", "w1_raw01", w1[0:G, G : 2 * G])
         w1_raw[1, 1] = load_rows("B", "w1_raw11", w1[G : 2 * G, G : 2 * G])
         nc.vector.tensor_copy(v_words[1][:, half(0)], tab_w[1][:].bitcast(U32).indirect(list_half(0)))
-        quantize_w1(1, 0, nc.scalar.copy)
+        quantize_w1(1, 0, nc.scalar.copy, "w3_grouped")
         nc.vector.tensor_copy(v_words[1][:, half(1)], tab_w[1][:].bitcast(U32).indirect(list_half(1)))
-        tick_raw = [load_rows("A", "tick_raw0", tick[:, half(0)])]
-        load_page("D", 0)
+        load_page("A", 3)
+        tick_raw = [load_rows("D", "tick_raw0", tick[:, half(0)])]
 
         sig = {}
 
@@ -165,36 +159,25 @@ def tile_list_gallery_state_damping_kernel(
                     )
                 nc.scalar.activation(out=sig[b, h][:, t, :], in_=acc[:], func=ACT.Sigmoid, bias=bias[:, b, t : t + 1])
 
-        def scale_on_scalar(b, h, scaled):
-            for t in range(PACK):
-                nc.scalar.activation(
-                    out=scaled[:, t, :], in_=sig[b, h][:, t, :], func=ACT.Copy, scale=gains[:, b, t : t + 1]
-                )
+        def scale_on_scalar(b, h, t, scaled):
+            nc.scalar.activation(
+                out=scaled[:, t, :], in_=sig[b, h][:, t, :], func=ACT.Copy, scale=gains[:, b, t : t + 1]
+            )
 
-        def scale_on_gpsimd(b, h, scaled):
-            for t in range(PACK):
-                nc.gpsimd.tensor_scalar(
-                    out=scaled[:, t, :],
-                    in0=sig[b, h][:, t, :],
-                    scalar1=gains[:, b, t : t + 1],
-                    scalar2=0.0,
-                    op0=MULT,
-                    op1=ADD,
-                )
-
-        def weave_on_gpsimd(grouped, scaled):
-            for c in range(2):
-                lo, hi = c * HALF // 2, (c + 1) * HALF // 2
-                gpsimd_copy(
-                    out=grouped[:, lo * PACK : hi * PACK].rearrange("p (c t) -> p c t", t=PACK),
-                    in_=scaled[:, :, lo:hi].rearrange("p t c -> p c t"),
-                )
+        def scale_on_gpsimd(b, h, t, scaled):
+            nc.gpsimd.tensor_scalar(
+                out=scaled[:, t, :],
+                in0=sig[b, h][:, t, :],
+                scalar1=gains[:, b, t : t + 1],
+                scalar2=0.0,
+                op0=MULT,
+                op1=ADD,
+            )
 
         picked = {}
 
-        def gather_page(t, tag):
-            into = slot(tag, "picked%d" % t, [P, S], F32)
-            nc.vector.tensor_copy(into[:], pages[t][:].indirect(offsets[:]))
+        def gather_page(t, into):
+            nc.vector.tensor_copy(into, pages[t][:].indirect(offsets[:]))
             for h in range(2):
                 picked[t, h] = into[:, half(h)]
 
@@ -206,39 +189,51 @@ def tile_list_gallery_state_damping_kernel(
         e_acc, root, damp = {}, {}, {}
 
         def stage_two(t, h):
-            cols = slice(t * P, (t + 1) * P)
             e_acc[t, h] = psum.tile([P, HALF], F32, name="e_acc", tag="bank")
-            for b in range(2):
+            cols = slice(t % 2 * P, (t % 2 + 1) * P)
+            ticket = [(w3_q[t // 2][0][:, cols].bitcast(FP8X4), w3_q[t // 2][1][:, cols], tick_q[h])]
+            gallery = [
+                (
+                    w4_codes[:, b, 2 * t * P : 2 * (t + 1) * P].bitcast(FP4X4),
+                    w4_plane[:, b * N + t * P : b * N + (t + 1) * P],
+                    h_q[b, h],
+                )
+                for b in range(2)
+            ]
+            passes = gallery + ticket if h == 0 else ticket + gallery
+            for i, (weights, weight_scales, moving) in enumerate(passes):
                 nc.tensor.matmul_mx(
                     out=e_acc[t, h][:],
-                    lhsT=w4_codes[:, b, 2 * t * P : 2 * (t + 1) * P].bitcast(FP4X4),
-                    lhsT_scale=w4_plane[:, b * N + t * P : b * N + (t + 1) * P],
-                    rhs=h_q[b, h][0].bitcast(FP8X4),
-                    rhs_scale=h_q[b, h][1],
-                    start=(b == 0),
-                    stop=False,
+                    lhsT=weights,
+                    lhsT_scale=weight_scales,
+                    rhs=moving[0].bitcast(FP8X4),
+                    rhs_scale=moving[1],
+                    start=(i == 0),
+                    stop=(i == len(passes) - 1),
                 )
-            nc.tensor.matmul_mx(
-                out=e_acc[t, h][:],
-                lhsT=w3_q[0][:, cols].bitcast(FP8X4),
-                lhsT_scale=w3_q[1][:, cols],
-                rhs=tick_q[h][0].bitcast(FP8X4),
-                rhs_scale=tick_q[h][1],
-                start=False,
-                stop=True,
-            )
+
+        def pieces(t, h):
+            width = HALF // 2 if (t, h) in ((0, 0), (2, 0), (2, 1), (3, 1)) else HALF
+            return [slice(lo, lo + width) for lo in range(0, HALF, width)]
 
         def inverse_root(t, h):
-            last = (t, h) == (PACK - 1, 1)
-            tag = {(1, 1): "sig11", (3, 1): "sig01"}.get((t, h), "square")
-            square = slot(tag, "square", [P, HALF], F32, bufs=2 if tag == "square" else 1)
-            nc.scalar.activation(out=square[:], in_=e_acc[t, h][:], func=ACT.Square)
+            last = (t, h) == (3, 1)
+            if last:
+                squares = [slot(tag, "square", [P, HALF // 2], F32)[:] for tag in ("sig01", "sig11")]
+            else:
+                held = (t, h) == (2, 0)
+                square = slot("scaled" if held else "square", "square", [P, HALF], F32, bufs=1 if held else 2)
+                squares = [square[:, cols] for cols in pieces(t, h)]
+            for cols, square in zip(pieces(t, h), squares):
+                nc.scalar.activation(out=square, in_=e_acc[t, h][:, cols], func=ACT.Square)
             root[t, h] = slot("sig10" if last else "root", "root", [P, HALF], F32, bufs=1 if last else 3)
-            nc.scalar.activation(out=root[t, h][:], in_=square[:], func=ACT.Abs_reciprocal_sqrt, bias=1.0)
+            for cols, square in zip(pieces(t, h), squares):
+                nc.scalar.activation(out=root[t, h][:, cols], in_=square, func=ACT.Abs_reciprocal_sqrt, bias=1.0)
 
-        def damping(t, h, into=None):
-            damp[t, h] = slot("damp", "damp", [P, HALF], F32, bufs=5)[:] if into is None else into
-            nc.scalar.activation(out=damp[t, h], in_=root[t, h][:], func=ACT.Square)
+        def damping(t, h):
+            damp[t, h] = slot("damp", "damp", [P, HALF], F32, bufs=5)[:]
+            for cols in pieces(t, h):
+                nc.scalar.activation(out=damp[t, h][:, cols], in_=root[t, h][:, cols], func=ACT.Square)
 
         def scatter_state(t, h):
             nc.vector.tensor_tensor(pages[t][:].indirect(list_half(h)), picked[t, h], damp[t, h], MULT)
@@ -247,69 +242,73 @@ def tile_list_gallery_state_damping_kernel(
             return pair[0][:], pair[1][:]
 
         stage_one(0, 0, "E")
-        quantize_w1(0, 1, nc.vector.tensor_copy)
+        quantize_w1(0, 1, nc.vector.tensor_copy, "F")
         w3_raw = load_rows("C", "w3_raw", w3)
+        load_page("F", 1)
         w4_plane = kept("w4_plane", [P, 2 * N], U8)
         nc.vector.tensor_copy(
             out=w4_plane[:].rearrange("p (a t m) -> p a m t", a=2, t=PACK),
             in_=w4_raw_s[:].rearrange("p (a m t) -> p a m t", a=2, t=PACK),
         )
-        quantize_w1(1, 1, nc.vector.tensor_copy)
-        load_page("B", 1)
-        scaled = slot("scaled", "scaled00", [P, PACK, HALF], BF16)
-        scale_on_scalar(0, 0, scaled)
-        load_page("E", 2)
-        grouped = slot("h00_grouped", "tick_grouped", [P, G * PACK], BF16)
+        quantize_w1(1, 1, nc.vector.tensor_copy, "h00_grouped")
+        load_page("B", 2)
+        gather_page(3, kept("picked3", [P, S], F32)[:])
+        scaled = slot("h00_grouped", "scaled00", [P, PACK, HALF], BF16)
+        for t in range(PACK - 1):
+            scale_on_gpsimd(0, 0, t, scaled)
+        scale_on_scalar(0, 0, PACK - 1, scaled)
+        load_page("E", 0)
+        grouped = slot("tick_grouped", "tick_grouped", [P, G * PACK], BF16)
         weave(nc.vector.tensor_copy, grouped[:], tick_raw[0][:])
         tick_q[0] = whole(quantize("tick0", grouped[:]))
-        load_page("A", 3)
-        gather_page(0, "picked0")
-        grouped = slot("h00_grouped", "h00_grouped", [P, G * PACK], BF16)
-        weave_on_gpsimd(grouped, scaled)
-        h_q[0, 0] = whole(quantize("h00", grouped[:]))
+        stage_one(0, 1, "sig01")
         stage_one(1, 0, "sig10")
         grouped = slot("h10_grouped", "h10_grouped", [P, G * PACK], BF16)
         dst, src = woven_views(grouped[:], sig[1, 0][:], run=2)
         factor = gains[:, 1, :].unsqueeze(1).unsqueeze(3).broadcast_to([P, HALF // 2, PACK, 2])
         nc.vector.tensor_tensor(out=dst, in0=src, in1=factor, op=MULT)
         h_q[1, 0] = whole(quantize("h10", grouped[:]))
-        grouped = slot("w3_grouped", "w3_grouped", [P, G * PACK], BF16)
-        deal(nc.scalar.copy, grouped[:], w3_raw[:])
-        w3_q = quantize("w3", grouped[:])
+        grouped = slot("woven00", "h00_grouped", [P, G * PACK], BF16)
+        weave(nc.scalar.copy, grouped[:], scaled[:])
+        h_q[0, 0] = whole(quantize("h00", grouped[:]))
+        w3_q = []
+        for u, tag in enumerate(("scaled", "w3_grouped")):
+            grouped = slot(tag, "w3_grouped", [P, G * PACK // 2], BF16)
+            nc.scalar.copy(
+                out=grouped[:].rearrange("p (t m j) -> p m j t", t=2, j=PACK),
+                in_=w3_raw[:].rearrange("p j (m t) -> p m j t", t=PACK)[:, :, :, 2 * u : 2 * u + 2],
+            )
+            w3_q.append(quantize("w3_%d" % u, grouped[:], width=G // 2))
         tick_raw.append(load_rows("C", "tick_raw1", tick[:, half(1)]))
-        stage_one(0, 1, "sig01")
         stage_one(1, 1, "sig11")
-        gather_page(1, "w3_grouped")
-        gather_half(2, 1, kept("picked21", [P, HALF], F32)[:])
-        gather_page(3, "picked3")
+        filler = slot("w3_grouped", "picked", [P, 2 * S + HALF], F32)
+        gather_page(1, filler[:, 0:S])
+        gather_half(2, 1, filler[:, 2 * S :])
+        gather_page(0, filler[:, S : 2 * S])
         for t in range(PACK):
             stage_two(t, 0)
 
-        inverse_root(0, 0)
-        damping(0, 0)
-        scatter_state(0, 0)
+        scaled = slot("scaled", "scaled_late", [P, 2, PACK, HALF], BF16)
+        for b in range(2):
+            for t in range(PACK):
+                scale_on_gpsimd(b, 1, t, scaled[:, b])
         late = slot("late", "late_grouped", [P, 2 * G * PACK], BF16)
-        scaled = slot("h10_grouped", "scaled01", [P, PACK, HALF], BF16)
-        scale_on_gpsimd(0, 1, scaled)
-        weave_on_gpsimd(late[:, 0 : G * PACK], scaled)
-        inverse_root(1, 0)
-        damping(1, 0)
-        scatter_state(1, 0)
-        scaled = slot("scaled", "scaled11", [P, PACK, HALF], BF16)
-        scale_on_scalar(1, 1, scaled)
-        grouped = grouped_tile()
+        for t in (0, 1, 3):
+            inverse_root(t, 0)
+            damping(t, 0)
+            scatter_state(t, 0)
+        grouped = slot("h10_grouped", "tick_grouped", [P, G * PACK], BF16)
         weave(nc.scalar.copy, grouped[:], tick_raw[1][:])
         tick_q[1] = whole(quantize("tick1", grouped[:]))
-        weave(nc.scalar.copy, late[:, G * PACK : 2 * G * PACK], scaled[:])
+        for b in range(2):
+            weave(nc.scalar.copy, late[:, b * G * PACK : (b + 1) * G * PACK], scaled[:, b])
         codes, scales = quantize("late", late[:], width=2 * G)
         for b in range(2):
             h_q[b, 1] = codes[:, b * G : (b + 1) * G], scales[:, b * G : (b + 1) * G]
-        held = slot("late", "held", [P, 2, HALF], F32)
-        gather_half(2, 0, held[:, 0, :])
-        for t in (2, 3):
-            inverse_root(t, 0)
-            damping(t, 0, held[:, 1, :] if t == 3 else None)
-            scatter_state(t, 0)
+        gather_half(2, 0, slot("late", "picked20", [P, HALF], F32)[:])
+        inverse_root(2, 0)
+        damping(2, 0)
+        scatter_state(2, 0)
 
         y_rows = out_0.rearrange("(p t) m -> t p m", t=PACK)
         order = (2, 0, 1, 3)
@@ -317,7 +316,7 @@ def tile_list_gallery_state_damping_kernel(
             stage_two(t, 1)
 
         def finish_page(t):
-            damping(t, 1, slot("E", "last_damp", [P, HALF], F32)[:] if t == 3 else None)
+            damping(t, 1)
             scatter_state(t, 1)
             nc.sync.dma_start(out=y_rows[t], in_=pages[t][:])
 
@@ -332,9 +331,9 @@ def tile_list_gallery_state_damping_kernel(
             base = side * T // 2
             copy(out=pairs[side][:, t // 2, lo:hi, t % 2], in_=pages[t][:, base + lo : base + hi])
 
-        for side in range(2):
-            round_page(nc.scalar.copy, 2, side, 0, T // 2)
+        round_page(nc.scalar.copy, 2, 0, 0, T // 2)
         finish_page(3)
+        round_page(nc.scalar.copy, 2, 1, 0, T // 2)
         for t in (0, 1):
             for side in range(2):
                 round_page(nc.scalar.copy, t, side, 0, T // 2)

@@ -92,16 +92,16 @@ def tile_list_gallery_state_damping_kernel(
         w1_raw = {}
         tab_w = [load_table("C", 0)]
         w1_raw[0, 0] = load_rows("B", "w1_raw00", w1[0:G, 0:G])
+        bias = kept("bias", [P, 2, PACK], F32)
+        gains = kept("gains", [P, 2, PACK], F32)
+        nc.sync.dma_start(out=bias[:], in_=b1.rearrange("(b p t) -> p b t", b=2, t=PACK))
+        nc.sync.dma_start(out=gains[:], in_=gain.rearrange("(b p t) -> p b t", b=2, t=PACK))
         tab_s = slot("small", "tab_s", [P, T], U8)
         nc.gpsimd.memset(tab_s[:].bitcast(I32), 0)
         for q in range(4):
             nc.sync.dma_start(
                 out=tab_s[32 * q : 32 * q + 8, :].bitcast(I32), in_=tab_scales[:, 4 * q : 4 * q + 4, :].bitcast(I32)
             )
-        bias = kept("bias", [P, 2, PACK], F32)
-        gains = kept("gains", [P, 2, PACK], F32)
-        nc.gpsimd.dma_start(out=bias[:], in_=b1.rearrange("(b p t) -> p b t", b=2, t=PACK))
-        nc.gpsimd.dma_start(out=gains[:], in_=gain.rearrange("(b p t) -> p b t", b=2, t=PACK))
 
         w4_codes = kept("w4_codes", [P, 2, 2 * N], U8)
         for b in range(2):
@@ -254,9 +254,9 @@ def tile_list_gallery_state_damping_kernel(
         load_page("B", 2)
         gather_page(3, kept("picked3", [P, S], F32)[:])
         scaled = slot("h00_grouped", "scaled00", [P, PACK, HALF], BF16)
-        for t in range(PACK - 1):
+        for t in range(PACK // 2):
             scale_on_gpsimd(0, 0, t, scaled)
-        scale_on_scalar(0, 0, PACK - 1, scaled)
+            scale_on_scalar(0, 0, PACK // 2 + t, scaled)
         load_page("E", 0)
         grouped = slot("tick_grouped", "tick_grouped", [P, G * PACK], BF16)
         weave(nc.vector.tensor_copy, grouped[:], tick_raw[0][:])
@@ -289,14 +289,15 @@ def tile_list_gallery_state_damping_kernel(
             stage_two(t, 0)
 
         scaled = slot("scaled", "scaled_late", [P, 2, PACK, HALF], BF16)
-        for b in range(2):
-            for t in range(PACK):
-                scale_on_gpsimd(b, 1, t, scaled[:, b])
+        for b, t in [(0, t) for t in range(PACK)] + [(1, t) for t in range(PACK // 2)]:
+            scale_on_gpsimd(b, 1, t, scaled[:, b])
         late = slot("late", "late_grouped", [P, 2 * G * PACK], BF16)
         for t in (0, 1, 3):
             inverse_root(t, 0)
             damping(t, 0)
             scatter_state(t, 0)
+        for t in range(PACK // 2, PACK):
+            scale_on_scalar(1, 1, t, scaled[:, 1])
         grouped = slot("h10_grouped", "tick_grouped", [P, G * PACK], BF16)
         weave(nc.scalar.copy, grouped[:], tick_raw[1][:])
         tick_q[1] = whole(quantize("tick1", grouped[:]))

@@ -121,8 +121,10 @@ def tile_list_gallery_state_damping_kernel(
             deal(copy, grouped[:], w1_raw[a, b][:])
             w1_q[a, b] = quantize("w1_%d%d" % (a, b), grouped[:])
 
-        nc.vector.tensor_copy(v_words[0][:], tab_w[0][:].bitcast(U32).indirect(offsets[:]))
-        nc.vector.tensor_copy(v_scales[:], tab_s[:].indirect(offsets[:]))
+        for h in range(2):
+            nc.vector.tensor_copy(v_words[0][:, half(h)], tab_w[0][:].bitcast(U32).indirect(list_half(h)))
+        for h in range(2):
+            nc.vector.tensor_copy(v_scales[:, half(h)], tab_s[:].indirect(list_half(h)))
         w4_raw_s = slot("small", "w4_raw_s", [P, 2 * N], U8)
         nc.gpsimd.memset(w4_raw_s[:].bitcast(I32), 0)
         for q in range(4):
@@ -177,9 +179,8 @@ def tile_list_gallery_state_damping_kernel(
         picked = {}
 
         def gather_page(t, into):
-            nc.vector.tensor_copy(into, pages[t][:].indirect(offsets[:]))
             for h in range(2):
-                picked[t, h] = into[:, half(h)]
+                gather_half(t, h, into[:, half(h)])
 
         def gather_half(t, h, into):
             nc.vector.tensor_copy(into, pages[t][:].indirect(list_half(h)))
@@ -368,6 +369,6 @@ def tile_list_gallery_state_damping_kernel(
         for c in range(len(spans)):
             quantize_y(c)
         for q in range(4):
-            nc.scalar.dma_start(
+            nc.sync.dma_start(
                 out=out_2[0, 4 * q : 4 * q + 4, :].bitcast(I32), in_=y_scales[32 * q : 32 * q + 4, :].bitcast(I32)
             )

@@ -92,16 +92,29 @@ def tile_list_gallery_state_damping_kernel(
         w1_raw = {}
         tab_w = [load_table("C", 0)]
         w1_raw[0, 0] = load_rows("B", "w1_raw00", w1[0:G, 0:G])
-        bias = kept("bias", [P, 2, PACK], F32)
-        gains = kept("gains", [P, 2, PACK], F32)
-        nc.sync.dma_start(out=bias[:], in_=b1.rearrange("(b p t) -> p b t", b=2, t=PACK))
-        nc.sync.dma_start(out=gains[:], in_=gain.rearrange("(b p t) -> p b t", b=2, t=PACK))
-        tab_s = slot("small", "tab_s", [P, T], U8)
+        tab_s = kept("tab_s", [P, T], U8)
         nc.gpsimd.memset(tab_s[:].bitcast(I32), 0)
         for q in range(4):
             nc.sync.dma_start(
                 out=tab_s[32 * q : 32 * q + 8, :].bitcast(I32), in_=tab_scales[:, 4 * q : 4 * q + 4, :].bitcast(I32)
             )
+
+        bias = kept("bias", [P, 2, PACK], F32)
+        gains = kept("gains", [P, 2, PACK], F32)
+        nc.gpsimd.dma_start(out=bias[:], in_=b1.rearrange("(b p t) -> p b t", b=2, t=PACK))
+        nc.gpsimd.dma_start(out=gains[:], in_=gain.rearrange("(b p t) -> p b t", b=2, t=PACK))
+        w4_raw_s = kept("w4_raw_s", [P, 2 * N], U8)
+        nc.gpsimd.memset(w4_raw_s[:].bitcast(I32), 0)
+        for q in range(4):
+            nc.gpsimd.dma_start(
+                out=w4_raw_s[32 * q : 32 * q + 4, :].bitcast(I32).rearrange("i (a n) -> i a n", a=2),
+                in_=w4_scales[:, 4 * q : 4 * q + 4, :].rearrange("a i n -> i a n").bitcast(I32),
+            )
+        w4_plane = kept("w4_plane", [P, 2 * N], U8)
+        nc.gpsimd.tensor_copy(
+            out=w4_plane[:].rearrange("p (a t m) -> p a t m", a=2, t=PACK),
+            in_=w4_raw_s[:].rearrange("p (a m t) -> p a t m", a=2, t=PACK),
+        )
 
         w4_codes = kept("w4_codes", [P, 2, 2 * N], U8)
         for b in range(2):
@@ -125,13 +138,6 @@ def tile_list_gallery_state_damping_kernel(
             nc.vector.tensor_copy(v_words[0][:, half(h)], tab_w[0][:].bitcast(U32).indirect(list_half(h)))
         for h in range(2):
             nc.vector.tensor_copy(v_scales[:, half(h)], tab_s[:].indirect(list_half(h)))
-        w4_raw_s = slot("small", "w4_raw_s", [P, 2 * N], U8)
-        nc.gpsimd.memset(w4_raw_s[:].bitcast(I32), 0)
-        for q in range(4):
-            nc.sync.dma_start(
-                out=w4_raw_s[32 * q : 32 * q + 4, :].bitcast(I32).rearrange("i (a n) -> i a n", a=2),
-                in_=w4_scales[:, 4 * q : 4 * q + 4, :].rearrange("a i n -> i a n").bitcast(I32),
-            )
         quantize_w1(0, 0, nc.scalar.copy, "h10_grouped")
         w1_raw[0, 1] = load_rows("C", "w1_raw01", w1[0:G, G : 2 * G])
         w1_raw[1, 1] = load_rows("B", "w1_raw11", w1[G : 2 * G, G : 2 * G])
@@ -214,16 +220,16 @@ def tile_list_gallery_state_damping_kernel(
                 )
 
         def pieces(t, h):
-            width = HALF // 2 if (t, h) in ((0, 0), (2, 0), (2, 1), (3, 1)) else HALF
+            width = HALF // 2 if (t, h) in ((0, 0), (2, 0), (3, 1)) else HALF
             return [slice(lo, lo + width) for lo in range(0, HALF, width)]
 
-        def inverse_root(t, h):
+        def inverse_root(t, h, square=None):
             last = (t, h) == (3, 1)
             if last:
                 squares = [slot(tag, "square", [P, HALF // 2], F32)[:] for tag in ("sig01", "sig11")]
             else:
-                held = (t, h) == (2, 0)
-                square = slot("scaled" if held else "square", "square", [P, HALF], F32, bufs=1 if held else 2)
+                if square is None:
+                    square = slot("square", "square", [P, HALF], F32, bufs=2)
                 squares = [square[:, cols] for cols in pieces(t, h)]
             for cols, square in zip(pieces(t, h), squares):
                 nc.scalar.activation(out=square, in_=e_acc[t, h][:, cols], func=ACT.Square)
@@ -231,8 +237,8 @@ def tile_list_gallery_state_damping_kernel(
             for cols, square in zip(pieces(t, h), squares):
                 nc.scalar.activation(out=root[t, h][:, cols], in_=square, func=ACT.Abs_reciprocal_sqrt, bias=1.0)
 
-        def damping(t, h):
-            damp[t, h] = slot("damp", "damp", [P, HALF], F32, bufs=5)[:]
+        def damping(t, h, into=None):
+            damp[t, h] = slot("damp", "damp", [P, HALF], F32, bufs=5)[:] if into is None else into
             for cols in pieces(t, h):
                 nc.scalar.activation(out=damp[t, h][:, cols], in_=root[t, h][:, cols], func=ACT.Square)
 
@@ -246,19 +252,14 @@ def tile_list_gallery_state_damping_kernel(
         quantize_w1(0, 1, nc.vector.tensor_copy, "F")
         w3_raw = load_rows("C", "w3_raw", w3)
         load_page("F", 1)
-        w4_plane = kept("w4_plane", [P, 2 * N], U8)
-        nc.vector.tensor_copy(
-            out=w4_plane[:].rearrange("p (a t m) -> p a m t", a=2, t=PACK),
-            in_=w4_raw_s[:].rearrange("p (a m t) -> p a m t", a=2, t=PACK),
-        )
         quantize_w1(1, 1, nc.vector.tensor_copy, "h00_grouped")
-        load_page("B", 2)
+        load_page("B", 0)
         gather_page(3, kept("picked3", [P, S], F32)[:])
         scaled = slot("h00_grouped", "scaled00", [P, PACK, HALF], BF16)
         for t in range(PACK // 2):
             scale_on_gpsimd(0, 0, t, scaled)
             scale_on_scalar(0, 0, PACK // 2 + t, scaled)
-        load_page("E", 0)
+        load_page("E", 2)
         grouped = slot("tick_grouped", "tick_grouped", [P, G * PACK], BF16)
         weave(nc.vector.tensor_copy, grouped[:], tick_raw[0][:])
         tick_q[0] = whole(quantize("tick0", grouped[:]))
@@ -282,38 +283,39 @@ def tile_list_gallery_state_damping_kernel(
             w3_q.append(quantize("w3_%d" % u, grouped[:], width=G // 2))
         tick_raw.append(load_rows("C", "tick_raw1", tick[:, half(1)]))
         stage_one(1, 1, "sig11")
-        filler = slot("w3_grouped", "picked", [P, 2 * S + HALF], F32)
-        gather_page(1, filler[:, 0:S])
-        gather_half(2, 1, filler[:, 2 * S :])
-        gather_page(0, filler[:, S : 2 * S])
+        filler = slot("w3_grouped", "picked", [P, PACK - 1, S], F32)
+        for t in (1, 0, 2):
+            gather_page(t, filler[:, t, :])
         for t in range(PACK):
             stage_two(t, 0)
 
         scaled = slot("scaled", "scaled_late", [P, 2, PACK, HALF], BF16)
-        for b, t in [(0, t) for t in range(PACK)] + [(1, t) for t in range(PACK // 2)]:
-            scale_on_gpsimd(b, 1, t, scaled[:, b])
-        late = slot("late", "late_grouped", [P, 2 * G * PACK], BF16)
-        for t in (0, 1, 3):
-            inverse_root(t, 0)
-            damping(t, 0)
-            scatter_state(t, 0)
-        for t in range(PACK // 2, PACK):
-            scale_on_scalar(1, 1, t, scaled[:, 1])
+        for b in range(2):
+            for t in range(PACK):
+                scale_on_gpsimd(b, 1, t, scaled[:, b])
+        inverse_root(0, 0)
+        damping(0, 0)
+        scatter_state(0, 0)
+        inverse_root(1, 0)
+        inverse_root(3, 0)
+        damping(1, 0)
+        scatter_state(1, 0)
         grouped = slot("h10_grouped", "tick_grouped", [P, G * PACK], BF16)
         weave(nc.scalar.copy, grouped[:], tick_raw[1][:])
         tick_q[1] = whole(quantize("tick1", grouped[:]))
-        for b in range(2):
-            weave(nc.scalar.copy, late[:, b * G * PACK : (b + 1) * G * PACK], scaled[:, b])
-        codes, scales = quantize("late", late[:], width=2 * G)
-        for b in range(2):
-            h_q[b, 1] = codes[:, b * G : (b + 1) * G], scales[:, b * G : (b + 1) * G]
-        gather_half(2, 0, slot("late", "picked20", [P, HALF], F32)[:])
-        inverse_root(2, 0)
+        for b, tag in enumerate(("woven00", "tick_grouped")):
+            grouped = slot(tag, "late_grouped", [P, G * PACK], BF16)
+            weave(nc.scalar.copy, grouped[:], scaled[:, b])
+            h_q[b, 1] = whole(quantize("h%d1" % b, grouped[:]))
+        held = slot("scaled", "held", [P, 2, HALF], F32)
+        damping(3, 0, held[:, 0, :])
+        scatter_state(3, 0)
+        inverse_root(2, 0, held[:, 1, :])
         damping(2, 0)
         scatter_state(2, 0)
 
         y_rows = out_0.rearrange("(p t) m -> t p m", t=PACK)
-        order = (2, 0, 1, 3)
+        order = (0, 2, 1, 3)
         for t in order:
             stage_two(t, 1)
 
@@ -333,12 +335,13 @@ def tile_list_gallery_state_damping_kernel(
             base = side * T // 2
             copy(out=pairs[side][:, t // 2, lo:hi, t % 2], in_=pages[t][:, base + lo : base + hi])
 
+        for side in range(2):
+            round_page(nc.scalar.copy, 0, side, 0, T // 2)
         round_page(nc.scalar.copy, 2, 0, 0, T // 2)
         finish_page(3)
         round_page(nc.scalar.copy, 2, 1, 0, T // 2)
-        for t in (0, 1):
-            for side in range(2):
-                round_page(nc.scalar.copy, t, side, 0, T // 2)
+        for side in range(2):
+            round_page(nc.scalar.copy, 1, side, 0, T // 2)
 
         y_scales = kept("y_scales", [P, T], U8)
         y_codes = kept("y_codes", [P, T], I32)

@@ -1,6 +1,7 @@
 from contextlib import ExitStack
 
 import concourse.mybir as mybir
+from concourse.masks import make_identity
 
 T, S, K, H, M, N = 2048, 1024, 1024, 1024, 512, 512
 FLOPS = 2 * K * H * S + 2 * H * N * S + 2 * M * N * S
@@ -22,7 +23,8 @@ PACK = 4
 G = P * PACK
 HALF = 512
 LIST_COLS = HALF // 16
-SPAN = 512
+LAST = 64
+SHARE = 384
 
 
 def tile_list_gallery_state_damping_kernel(
@@ -31,7 +33,7 @@ def tile_list_gallery_state_damping_kernel(
     nc = tc.nc
     with ExitStack() as ctx:
         keep = ctx.enter_context(tc.tile_pool(name="keep", bufs=1))
-        psum = ctx.enter_context(tc.psum_pool(name="psum", bufs=8))
+        psum = ctx.enter_context(tc.psum_pool(name="psum", bufs=7))
 
         def kept(name, shape, dtype):
             return keep.tile(shape, dtype, name=name, align_bytes=64)
@@ -100,9 +102,13 @@ def tile_list_gallery_state_damping_kernel(
             )
 
         bias = kept("bias", [P, 2, PACK], F32)
-        gains = kept("gains", [P, 2, PACK], F32)
+        padded = kept("padded", [P, P], F32)
+        nc.gpsimd.memset(padded[:], 0.0)
+        gains = padded[:, 0 : 2 * PACK].rearrange("p (b t) -> p b t", b=2)
         nc.gpsimd.dma_start(out=bias[:], in_=b1.rearrange("(b p t) -> p b t", b=2, t=PACK))
-        nc.gpsimd.dma_start(out=gains[:], in_=gain.rearrange("(b p t) -> p b t", b=2, t=PACK))
+        nc.sync.dma_start(out=gains, in_=gain.rearrange("(b p t) -> p b t", b=2, t=PACK))
+        identity = kept("identity", [P, P], F32)
+        make_identity(nc, identity[:])
         w4_raw_s = kept("w4_raw_s", [P, 2 * N], U8)
         nc.gpsimd.memset(w4_raw_s[:].bitcast(I32), 0)
         for q in range(4):
@@ -144,6 +150,12 @@ def tile_list_gallery_state_damping_kernel(
         nc.vector.tensor_copy(v_words[1][:, half(0)], tab_w[1][:].bitcast(U32).indirect(list_half(0)))
         quantize_w1(1, 0, nc.scalar.copy, "w3_grouped")
         nc.vector.tensor_copy(v_words[1][:, half(1)], tab_w[1][:].bitcast(U32).indirect(list_half(1)))
+        turned = psum.tile([P, P], F32, name="turned", tag="bank")
+        nc.tensor.transpose(turned[:], padded[:], identity[:])
+        flipped = kept("flipped", [P, P], F32)
+        nc.scalar.copy(out=flipped[:], in_=turned[:])
+        gains_psum = psum.tile([P, P], F32, name="gains_psum", tag="gain_bank", bufs=1)
+        nc.tensor.transpose(gains_psum[:], flipped[:], identity[:])
         load_page("A", 3)
         tick_raw = [load_rows("D", "tick_raw0", tick[:, half(0)])]
 
@@ -226,7 +238,7 @@ def tile_list_gallery_state_damping_kernel(
         def inverse_root(t, h, square=None):
             last = (t, h) == (3, 1)
             if last:
-                squares = [slot(tag, "square", [P, HALF // 2], F32)[:] for tag in ("sig01", "sig11")]
+                squares = [slot(tag, "square", [P, HALF // 2], F32)[:] for tag in ("sig01", "C")]
             else:
                 if square is None:
                     square = slot("square", "square", [P, HALF], F32, bufs=2)
@@ -237,10 +249,13 @@ def tile_list_gallery_state_damping_kernel(
             for cols, square in zip(pieces(t, h), squares):
                 nc.scalar.activation(out=root[t, h][:, cols], in_=square, func=ACT.Abs_reciprocal_sqrt, bias=1.0)
 
-        def damping(t, h, into=None):
+        def square_root_factor(t, h, cols):
+            nc.scalar.activation(out=damp[t, h][:, cols], in_=root[t, h][:, cols], func=ACT.Square)
+
+        def damping(t, h, into=None, width=HALF):
             damp[t, h] = slot("damp", "damp", [P, HALF], F32, bufs=5)[:] if into is None else into
-            for cols in pieces(t, h):
-                nc.scalar.activation(out=damp[t, h][:, cols], in_=root[t, h][:, cols], func=ACT.Square)
+            for cols in pieces(t, h) if width == HALF else [slice(0, width)]:
+                square_root_factor(t, h, cols)
 
         def scatter_state(t, h):
             nc.vector.tensor_tensor(pages[t][:].indirect(list_half(h)), picked[t, h], damp[t, h], MULT)
@@ -256,33 +271,44 @@ def tile_list_gallery_state_damping_kernel(
         load_page("B", 0)
         gather_page(3, kept("picked3", [P, S], F32)[:])
         scaled = slot("h00_grouped", "scaled00", [P, PACK, HALF], BF16)
-        for t in range(PACK // 2):
+        for t in range(PACK - 1):
             scale_on_gpsimd(0, 0, t, scaled)
-            scale_on_scalar(0, 0, PACK // 2 + t, scaled)
+        scale_on_scalar(0, 0, PACK - 1, scaled)
         load_page("E", 2)
-        grouped = slot("tick_grouped", "tick_grouped", [P, G * PACK], BF16)
-        weave(nc.vector.tensor_copy, grouped[:], tick_raw[0][:])
-        tick_q[0] = whole(quantize("tick0", grouped[:]))
+        tick_grouped = slot("tick_grouped", "tick_grouped", [P, G * PACK], BF16)
+        weave(nc.vector.tensor_copy, tick_grouped[:, 0 : G * PACK // 2], tick_raw[0][:, :, 0 : HALF // 2])
         stage_one(0, 1, "sig01")
         stage_one(1, 0, "sig10")
+        weave(nc.scalar.copy, tick_grouped[:, G * PACK // 2 :], tick_raw[0][:, :, HALF // 2 :])
         grouped = slot("h10_grouped", "h10_grouped", [P, G * PACK], BF16)
         dst, src = woven_views(grouped[:], sig[1, 0][:], run=2)
-        factor = gains[:, 1, :].unsqueeze(1).unsqueeze(3).broadcast_to([P, HALF // 2, PACK, 2])
+        factor = gains_psum[:, PACK : 2 * PACK].unsqueeze(1).unsqueeze(3).broadcast_to([P, HALF // 2, PACK, 2])
         nc.vector.tensor_tensor(out=dst, in0=src, in1=factor, op=MULT)
+        tick_q[0] = whole(quantize("tick0", tick_grouped[:]))
         h_q[1, 0] = whole(quantize("h10", grouped[:]))
         grouped = slot("woven00", "h00_grouped", [P, G * PACK], BF16)
-        weave(nc.scalar.copy, grouped[:], scaled[:])
+        for lo in (0, SHARE // 2):
+            hi = lo + SHARE // 2
+            nc.gpsimd.tensor_scalar(
+                out=grouped[:, lo * PACK : hi * PACK].rearrange("p (c t) -> p c t", t=PACK),
+                in0=scaled[:, :, lo:hi].rearrange("p t c -> p c t"),
+                scalar1=1.0,
+                scalar2=0.0,
+                op0=MULT,
+                op1=ADD,
+            )
+        weave(nc.scalar.copy, grouped[:, SHARE * PACK :], scaled[:, :, SHARE:])
         h_q[0, 0] = whole(quantize("h00", grouped[:]))
         w3_q = []
-        for u, tag in enumerate(("scaled", "w3_grouped")):
+        for u, tag in enumerate(("w3_grouped", "scaled")):
             grouped = slot(tag, "w3_grouped", [P, G * PACK // 2], BF16)
             nc.scalar.copy(
                 out=grouped[:].rearrange("p (t m j) -> p m j t", t=2, j=PACK),
                 in_=w3_raw[:].rearrange("p j (m t) -> p m j t", t=PACK)[:, :, :, 2 * u : 2 * u + 2],
             )
             w3_q.append(quantize("w3_%d" % u, grouped[:], width=G // 2))
-        tick_raw.append(load_rows("C", "tick_raw1", tick[:, half(1)]))
-        stage_one(1, 1, "sig11")
+        tick_raw.append(load_rows("D", "tick_raw1", tick[:, half(1)]))
+        stage_one(1, 1, "C")
         filler = slot("w3_grouped", "picked", [P, PACK - 1, S], F32)
         for t in (1, 0, 2):
             gather_page(t, filler[:, t, :])
@@ -320,24 +346,27 @@ def tile_list_gallery_state_damping_kernel(
             stage_two(t, 1)
 
         def finish_page(t):
-            damping(t, 1)
             scatter_state(t, 1)
             nc.sync.dma_start(out=y_rows[t], in_=pages[t][:])
 
         for t in order[:3]:
             inverse_root(t, 1)
+            damping(t, 1)
             finish_page(t)
         inverse_root(3, 1)
+        damping(3, 1, width=HALF // 2)
+        square_root_factor(3, 1, slice(HALF // 2, HALF - LAST))
 
-        pairs = [slot(tag, "pairs", [P, 2, T // 2, 2], BF16) for tag in ("sig01", "sig11")]
+        pairs = [slot(tag, "pairs", [P, 2 * T], BF16) for tag in ("sig01", "C")]
 
         def round_page(copy, t, side, lo, hi):
             base = side * T // 2
-            copy(out=pairs[side][:, t // 2, lo:hi, t % 2], in_=pages[t][:, base + lo : base + hi])
+            copy(out=pairs[side][:].rearrange("p (u c e) -> p u c e", u=2, e=2)[:, t // 2, lo:hi, t % 2], in_=pages[t][:, base + lo : base + hi])
 
         for side in range(2):
             round_page(nc.scalar.copy, 0, side, 0, T // 2)
         round_page(nc.scalar.copy, 2, 0, 0, T // 2)
+        square_root_factor(3, 1, slice(HALF - LAST, HALF))
         finish_page(3)
         round_page(nc.scalar.copy, 2, 1, 0, T // 2)
         for side in range(2):
@@ -352,7 +381,7 @@ def tile_list_gallery_state_damping_kernel(
         def weave_words(copy, c):
             side, lo = divmod(spans[c][0], T // 2)
             hi = lo + spans[c][1] - spans[c][0]
-            words = pairs[side][:].rearrange("p u c e -> p (u c e)").bitcast(F32).rearrange("p (u c) -> p u c", u=2)
+            words = pairs[side][:].bitcast(F32).rearrange("p (u c) -> p u c", u=2)
             copy(
                 out=woven[c][:].bitcast(F32).rearrange("p (c i u) -> p c u i", i=4, u=2),
                 in_=words[:, :, lo:hi].rearrange("p u (c i) -> p c u i", i=4),
@@ -361,12 +390,14 @@ def tile_list_gallery_state_damping_kernel(
         def quantize_y(c):
             lo, hi = spans[c]
             nc.vector.quantize_mx(out=y_codes[:, lo:hi].bitcast(FP8X4), scales=y_scales[:, lo:hi], in_=woven[c][:])
-            if c > 0:
-                lo = lo if c > 1 else 0
+            if c != 3:
+                lo = spans[min(c, 3)][0]
                 nc.sync.dma_start(out=y_words[:, lo:hi], in_=y_codes[:, lo:hi])
 
-        round_page(nc.vector.tensor_copy, 3, 0, 0, T // 2)
-        round_page(nc.scalar.copy, 3, 1, 0, T // 2)
+        round_page(nc.vector.tensor_copy, 3, 0, 0, T // 4)
+        round_page(nc.vector.tensor_copy, 3, 0, T // 4, T // 2)
+        round_page(nc.scalar.copy, 3, 1, 0, T // 4)
+        round_page(nc.scalar.copy, 3, 1, T // 4, T // 2)
         for c in range(len(spans)):
             weave_words(nc.vector.tensor_copy if c < 2 else nc.scalar.copy, c)
         for c in range(len(spans)):

@@ -25,6 +25,7 @@ HALF = 512
 LIST_COLS = HALF // 16
 LAST = 64
 SHARE = 384
+LATE_SHARE = 192
 
 
 def tile_list_gallery_state_damping_kernel(
@@ -86,27 +87,27 @@ def tile_list_gallery_state_damping_kernel(
         def half(h):
             return slice(h * HALF, (h + 1) * HALF)
 
-        offsets = keep.tile([P, S // 16], U16, name="offsets")
-        nc.sync.dma_start(offsets[:], offs)
-        w4_raw = [slot(tag, "w4_raw", [P, 2 * N], U8) for tag in "AD"]
-        for b in range(2):
-            nc.sync.dma_start(out=w4_raw[b][:].bitcast(I32), in_=w4_words[b].bitcast(I32))
         w1_raw = {}
-        tab_w = [load_table("C", 0)]
-        w1_raw[0, 0] = load_rows("B", "w1_raw00", w1[0:G, 0:G])
         tab_s = kept("tab_s", [P, T], U8)
         nc.gpsimd.memset(tab_s[:].bitcast(I32), 0)
+        tab_w = [load_table("C", 0)]
+        offsets = keep.tile([P, S // 16], U16, name="offsets")
+        nc.sync.dma_start(offsets[:], offs)
+        w1_raw[0, 0] = load_rows("B", "w1_raw00", w1[0:G, 0:G])
+        bias = kept("bias", [P, 2, PACK], F32)
+        nc.sync.dma_start(out=bias[:], in_=b1.rearrange("(b p t) -> p b t", b=2, t=PACK))
         for q in range(4):
             nc.sync.dma_start(
                 out=tab_s[32 * q : 32 * q + 8, :].bitcast(I32), in_=tab_scales[:, 4 * q : 4 * q + 4, :].bitcast(I32)
             )
+        tab_w.append(load_table("D", 1))
+        w4_raw = slot("A", "w4_raw", [P, 2, 2 * N], U8)
+        nc.sync.dma_start(out=w4_raw[:].bitcast(I32), in_=w4_words.rearrange("b p n -> p b n").bitcast(I32))
 
-        bias = kept("bias", [P, 2, PACK], F32)
         padded = kept("padded", [P, P], F32)
         nc.gpsimd.memset(padded[:], 0.0)
         gains = padded[:, 0 : 2 * PACK].rearrange("p (b t) -> p b t", b=2)
-        nc.gpsimd.dma_start(out=bias[:], in_=b1.rearrange("(b p t) -> p b t", b=2, t=PACK))
-        nc.sync.dma_start(out=gains, in_=gain.rearrange("(b p t) -> p b t", b=2, t=PACK))
+        nc.gpsimd.dma_start(out=gains, in_=gain.rearrange("(b p t) -> p b t", b=2, t=PACK))
         identity = kept("identity", [P, P], F32)
         make_identity(nc, identity[:])
         w4_raw_s = kept("w4_raw_s", [P, 2 * N], U8)
@@ -116,73 +117,81 @@ def tile_list_gallery_state_damping_kernel(
                 out=w4_raw_s[32 * q : 32 * q + 4, :].bitcast(I32).rearrange("i (a n) -> i a n", a=2),
                 in_=w4_scales[:, 4 * q : 4 * q + 4, :].rearrange("a i n -> i a n").bitcast(I32),
             )
-        w4_plane = kept("w4_plane", [P, 2 * N], U8)
-        nc.gpsimd.tensor_copy(
-            out=w4_plane[:].rearrange("p (a t m) -> p a t m", a=2, t=PACK),
-            in_=w4_raw_s[:].rearrange("p (a m t) -> p a t m", a=2, t=PACK),
-        )
-
         w4_codes = kept("w4_codes", [P, 2, 2 * N], U8)
-        for b in range(2):
-            nc.vector.tensor_copy(
-                out=w4_codes[:, b, :].rearrange("p (t m y) -> p m t y", t=PACK, y=2),
-                in_=w4_raw[b][:].rearrange("p (m t y) -> p m t y", t=PACK, y=2),
-            )
-        w1_raw[1, 0] = load_rows("A", "w1_raw10", w1[G : 2 * G, 0:G])
-        tab_w.append(load_table("D", 1))
+        nc.scalar.copy(
+            out=w4_codes[:].bitcast(U16).rearrange("p b (t m) -> p b m t", t=PACK),
+            in_=w4_raw[:].bitcast(U16).rearrange("p b (m t) -> p b m t", t=PACK),
+        )
 
         v_words = [kept("v_words%d" % a, [P, S], U32) for a in range(2)]
         v_scales = kept("v_scales", [P, S], U8)
         w1_q = {}
 
-        def quantize_w1(a, b, copy, tag):
-            grouped = slot(tag, "w1_grouped", [P, G * PACK], BF16)
-            deal(copy, grouped[:], w1_raw[a, b][:])
-            w1_q[a, b] = quantize("w1_%d%d" % (a, b), grouped[:])
+        def quantize_w1(a, b, copies, tags):
+            parts = len(copies)
+            rows = PACK // parts
+            grouped = [slot(tag, "w1_grouped", [P, G * rows], BF16) for tag in tags]
+            for u, copy in enumerate(copies):
+                copy(
+                    out=grouped[u][:].rearrange("p (t m j) -> p m j t", t=rows, j=PACK),
+                    in_=w1_raw[a, b][:].rearrange("p j (m t) -> p m j t", t=PACK)[:, :, :, rows * u : rows * (u + 1)],
+                )
+            for u in range(parts):
+                codes, scales = quantize("w1_%d%d%d" % (a, b, u), grouped[u][:], width=P * rows)
+                for e in range(rows):
+                    w1_q[a, b, rows * u + e] = codes[:, e * P : (e + 1) * P], scales[:, e * P : (e + 1) * P]
 
-        for h in range(2):
-            nc.vector.tensor_copy(v_words[0][:, half(h)], tab_w[0][:].bitcast(U32).indirect(list_half(h)))
-        for h in range(2):
-            nc.vector.tensor_copy(v_scales[:, half(h)], tab_s[:].indirect(list_half(h)))
-        quantize_w1(0, 0, nc.scalar.copy, "h10_grouped")
-        w1_raw[0, 1] = load_rows("C", "w1_raw01", w1[0:G, G : 2 * G])
-        w1_raw[1, 1] = load_rows("B", "w1_raw11", w1[G : 2 * G, G : 2 * G])
-        nc.vector.tensor_copy(v_words[1][:, half(0)], tab_w[1][:].bitcast(U32).indirect(list_half(0)))
-        quantize_w1(1, 0, nc.scalar.copy, "w3_grouped")
-        nc.vector.tensor_copy(v_words[1][:, half(1)], tab_w[1][:].bitcast(U32).indirect(list_half(1)))
-        turned = psum.tile([P, P], F32, name="turned", tag="bank")
+        def gather_words(a):
+            nc.vector.tensor_copy(v_words[a][:], tab_w[a][:].bitcast(U32).indirect(offsets[:]))
+
+        gather_words(0)
+        nc.vector.tensor_copy(v_scales[:], tab_s[:].indirect(offsets[:]))
+        w1_raw[1, 0] = load_rows("C", "w1_raw10", w1[G : 2 * G, 0:G])
+        quantize_w1(0, 0, [nc.scalar.copy], ["g00"])
+        w4_plane = slot("g00", "w4_plane", [P, 2 * N], U8)
+        nc.gpsimd.tensor_copy(
+            out=w4_plane[:].rearrange("p (a t m) -> p a t m", a=2, t=PACK),
+            in_=w4_raw_s[:].rearrange("p (a m t) -> p a t m", a=2, t=PACK),
+        )
+        w1_raw[0, 1] = load_rows("B", "w1_raw01", w1[0:G, G : 2 * G])
+        gather_words(1)
+        w1_raw[1, 1] = load_rows("A", "w1_raw11", w1[G : 2 * G, G : 2 * G])
+        quantize_w1(1, 0, [nc.vector.tensor_copy] * 2, ["w3_grouped", "g10b"])
+        turned = psum.tile([P, P], F32, name="turned", tag="bank6", bufs=1)
         nc.tensor.transpose(turned[:], padded[:], identity[:])
         flipped = kept("flipped", [P, P], F32)
         nc.scalar.copy(out=flipped[:], in_=turned[:])
         gains_psum = psum.tile([P, P], F32, name="gains_psum", tag="gain_bank", bufs=1)
         nc.tensor.transpose(gains_psum[:], flipped[:], identity[:])
-        load_page("A", 3)
-        tick_raw = [load_rows("D", "tick_raw0", tick[:, half(0)])]
+        load_page("C", 3)
 
         sig = {}
 
-        def stage_one(b, h, tag):
-            sig[b, h] = slot(tag, "sig%d%d" % (b, h), [P, PACK, HALF], F32)
-            for t in range(PACK):
-                cols = slice(t * P, (t + 1) * P)
-                acc = psum.tile([P, HALF], F32, name="x_acc", tag="bank")
+        x_acc = {}
+
+        def stage_one(b, h, banks):
+            for t in banks:
+                acc = psum.tile([P, HALF], F32, name="x_acc", tag="bank%d" % banks[t], bufs=1)
+                x_acc[b, h, t] = acc
                 for a in range(2):
-                    codes, scales = w1_q[a, b]
+                    codes, scales = w1_q[a, b, t]
                     nc.tensor.matmul_mx(
                         out=acc[:],
-                        lhsT=codes[:, cols].bitcast(FP8X4),
-                        lhsT_scale=scales[:, cols],
+                        lhsT=codes.bitcast(FP8X4),
+                        lhsT_scale=scales,
                         rhs=v_words[a][:, half(h)].bitcast(FP8X4),
                         rhs_scale=v_scales[4 * a : P, half(h)],
                         start=(a == 0),
                         stop=(a == 1),
                     )
-                nc.scalar.activation(out=sig[b, h][:, t, :], in_=acc[:], func=ACT.Sigmoid, bias=bias[:, b, t : t + 1])
 
-        def scale_on_scalar(b, h, t, scaled):
-            nc.scalar.activation(
-                out=scaled[:, t, :], in_=sig[b, h][:, t, :], func=ACT.Copy, scale=gains[:, b, t : t + 1]
-            )
+        def sigmoids(b, h, tag, rows=range(PACK)):
+            if tag:
+                sig[b, h] = slot(tag, "sig%d%d" % (b, h), [P, PACK, HALF], F32)
+            for t in rows:
+                nc.scalar.activation(
+                    out=sig[b, h][:, t, :], in_=x_acc[b, h, t][:], func=ACT.Sigmoid, bias=bias[:, b, t : t + 1]
+                )
 
         def scale_on_gpsimd(b, h, t, scaled):
             nc.gpsimd.tensor_scalar(
@@ -194,23 +203,30 @@ def tile_list_gallery_state_damping_kernel(
                 op1=ADD,
             )
 
+        def weave_on_gpsimd(grouped, scaled, lo, hi):
+            nc.gpsimd.tensor_scalar(
+                out=grouped[:, lo * PACK : hi * PACK].rearrange("p (c t) -> p c t", t=PACK),
+                in0=scaled[:, :, lo:hi].rearrange("p t c -> p c t"),
+                scalar1=1.0,
+                scalar2=0.0,
+                op0=MULT,
+                op1=ADD,
+            )
+
         picked = {}
 
         def gather_page(t, into):
+            nc.vector.tensor_copy(into, pages[t][:].indirect(offsets[:]))
             for h in range(2):
-                gather_half(t, h, into[:, half(h)])
-
-        def gather_half(t, h, into):
-            nc.vector.tensor_copy(into, pages[t][:].indirect(list_half(h)))
-            picked[t, h] = into
+                picked[t, h] = into[:, half(h)]
 
         h_q, tick_q = {}, {}
         e_acc, root, damp = {}, {}, {}
 
         def stage_two(t, h):
-            e_acc[t, h] = psum.tile([P, HALF], F32, name="e_acc", tag="bank")
-            cols = slice(t % 2 * P, (t % 2 + 1) * P)
-            ticket = [(w3_q[t // 2][0][:, cols].bitcast(FP8X4), w3_q[t // 2][1][:, cols], tick_q[h])]
+            e_acc[t, h] = psum.tile([P, HALF], F32, name="e_acc", tag="bank%d" % ((0, 1, 3, 6), (4, 2, 5, 0))[h][t], bufs=1)
+            cols = slice(t * P, (t + 1) * P)
+            ticket = [(w3_q[0][:, cols].bitcast(FP8X4), w3_q[1][:, cols], tick_q[h])]
             gallery = [
                 (
                     w4_codes[:, b, 2 * t * P : 2 * (t + 1) * P].bitcast(FP4X4),
@@ -219,7 +235,7 @@ def tile_list_gallery_state_damping_kernel(
                 )
                 for b in range(2)
             ]
-            passes = gallery + ticket if h == 0 else ticket + gallery
+            passes = gallery + ticket
             for i, (weights, weight_scales, moving) in enumerate(passes):
                 nc.tensor.matmul_mx(
                     out=e_acc[t, h][:],
@@ -238,7 +254,7 @@ def tile_list_gallery_state_damping_kernel(
         def inverse_root(t, h, square=None):
             last = (t, h) == (3, 1)
             if last:
-                squares = [slot(tag, "square", [P, HALF // 2], F32)[:] for tag in ("sig01", "C")]
+                squares = [slot(tag, "square", [P, HALF // 2], F32)[:] for tag in ("D", "A")]
             else:
                 if square is None:
                     square = slot("square", "square", [P, HALF], F32, bufs=2)
@@ -257,29 +273,32 @@ def tile_list_gallery_state_damping_kernel(
             for cols in pieces(t, h) if width == HALF else [slice(0, width)]:
                 square_root_factor(t, h, cols)
 
-        def scatter_state(t, h):
-            nc.vector.tensor_tensor(pages[t][:].indirect(list_half(h)), picked[t, h], damp[t, h], MULT)
+        def scatter_state(t, h, lo=0, hi=HALF):
+            entries = list_half(h)[:, lo // 16 : hi // 16]
+            nc.vector.tensor_tensor(pages[t][:].indirect(entries), picked[t, h][:, lo:hi], damp[t, h][:, lo:hi], MULT)
 
         def whole(pair):
             return pair[0][:], pair[1][:]
 
-        stage_one(0, 0, "E")
-        quantize_w1(0, 1, nc.vector.tensor_copy, "F")
-        w3_raw = load_rows("C", "w3_raw", w3)
+        stage_one(0, 0, {0: 0, 1: 1, 2: 2, 3: 3})
+        sigmoids(0, 0, "E")
+        quantize_w1(0, 1, [nc.vector.tensor_copy] * 2, ["g01a", "g01b"])
+        tick_raw = [load_rows("B", "tick_raw0", tick[:, half(0)])]
+        quantize_w1(1, 1, [nc.vector.tensor_copy] * 2, ["F", "h00_grouped"])
+        w3_raw = load_rows("A", "w3_raw", w3)
         load_page("F", 1)
-        quantize_w1(1, 1, nc.vector.tensor_copy, "h00_grouped")
-        load_page("B", 0)
         gather_page(3, kept("picked3", [P, S], F32)[:])
         scaled = slot("h00_grouped", "scaled00", [P, PACK, HALF], BF16)
-        for t in range(PACK - 1):
+        for t in range(PACK):
             scale_on_gpsimd(0, 0, t, scaled)
-        scale_on_scalar(0, 0, PACK - 1, scaled)
-        load_page("E", 2)
         tick_grouped = slot("tick_grouped", "tick_grouped", [P, G * PACK], BF16)
-        weave(nc.vector.tensor_copy, tick_grouped[:, 0 : G * PACK // 2], tick_raw[0][:, :, 0 : HALF // 2])
-        stage_one(0, 1, "sig01")
-        stage_one(1, 0, "sig10")
-        weave(nc.scalar.copy, tick_grouped[:, G * PACK // 2 :], tick_raw[0][:, :, HALF // 2 :])
+        stage_one(1, 0, {0: 1, 1: 2, 2: 3, 3: 0})
+        sigmoids(1, 0, "sig10")
+        stage_one(0, 1, {0: 4, 1: 5, 2: 6})
+
+        load_page("E", 0)
+        weave(nc.scalar.copy, tick_grouped[:], tick_raw[0][:])
+        load_page("B", 2)
         grouped = slot("h10_grouped", "h10_grouped", [P, G * PACK], BF16)
         dst, src = woven_views(grouped[:], sig[1, 0][:], run=2)
         factor = gains_psum[:, PACK : 2 * PACK].unsqueeze(1).unsqueeze(3).broadcast_to([P, HALF // 2, PACK, 2])
@@ -288,37 +307,30 @@ def tile_list_gallery_state_damping_kernel(
         h_q[1, 0] = whole(quantize("h10", grouped[:]))
         grouped = slot("woven00", "h00_grouped", [P, G * PACK], BF16)
         for lo in (0, SHARE // 2):
-            hi = lo + SHARE // 2
-            nc.gpsimd.tensor_scalar(
-                out=grouped[:, lo * PACK : hi * PACK].rearrange("p (c t) -> p c t", t=PACK),
-                in0=scaled[:, :, lo:hi].rearrange("p t c -> p c t"),
-                scalar1=1.0,
-                scalar2=0.0,
-                op0=MULT,
-                op1=ADD,
-            )
+            weave_on_gpsimd(grouped[:], scaled, lo, lo + SHARE // 2)
         weave(nc.scalar.copy, grouped[:, SHARE * PACK :], scaled[:, :, SHARE:])
         h_q[0, 0] = whole(quantize("h00", grouped[:]))
-        w3_q = []
-        for u, tag in enumerate(("w3_grouped", "scaled")):
-            grouped = slot(tag, "w3_grouped", [P, G * PACK // 2], BF16)
-            nc.scalar.copy(
-                out=grouped[:].rearrange("p (t m j) -> p m j t", t=2, j=PACK),
-                in_=w3_raw[:].rearrange("p j (m t) -> p m j t", t=PACK)[:, :, :, 2 * u : 2 * u + 2],
-            )
-            w3_q.append(quantize("w3_%d" % u, grouped[:], width=G // 2))
-        tick_raw.append(load_rows("D", "tick_raw1", tick[:, half(1)]))
-        stage_one(1, 1, "C")
-        filler = slot("w3_grouped", "picked", [P, PACK - 1, S], F32)
+        grouped = slot("scaled", "w3_grouped", [P, G * PACK], BF16)
+        deal(nc.scalar.copy, grouped[:], w3_raw[:])
+        w3_q = quantize("w3", grouped[:])
+        sigmoids(0, 1, "D", range(PACK - 1))
+        tick_raw.append(load_rows("h00_grouped", "tick_raw1", tick[:, half(1)]))
+        stage_one(1, 1, {0: 2, 1: 3, 2: 4, 3: 5})
+        sigmoids(1, 1, "A")
+        stage_one(0, 1, {3: 2})
+        sigmoids(0, 1, None, [PACK - 1])
+        filler = kept("picked", [P, PACK - 1, S], F32)
         for t in (1, 0, 2):
             gather_page(t, filler[:, t, :])
         for t in range(PACK):
             stage_two(t, 0)
 
-        scaled = slot("scaled", "scaled_late", [P, 2, PACK, HALF], BF16)
+        scaled = [slot(tag, "scaled_late", [P, PACK, HALF], BF16) for tag in ("h10_grouped", "scaled")]
+        late = slot("woven00", "late_grouped", [P, 2 * G * PACK], BF16)
         for b in range(2):
             for t in range(PACK):
-                scale_on_gpsimd(b, 1, t, scaled[:, b])
+                scale_on_gpsimd(b, 1, t, scaled[b])
+        weave_on_gpsimd(late[:], scaled[0], 0, LATE_SHARE)
         inverse_root(0, 0)
         damping(0, 0)
         scatter_state(0, 0)
@@ -326,17 +338,19 @@ def tile_list_gallery_state_damping_kernel(
         inverse_root(3, 0)
         damping(1, 0)
         scatter_state(1, 0)
-        grouped = slot("h10_grouped", "tick_grouped", [P, G * PACK], BF16)
+        weave(nc.scalar.copy, late[:, LATE_SHARE * PACK : G * PACK], scaled[0][:, :, LATE_SHARE:])
+        weave(nc.scalar.copy, late[:, G * PACK :], scaled[1][:])
+        codes, scales = quantize("h_late", late[:], width=2 * G)
+        for b in range(2):
+            h_q[b, 1] = codes[:, b * G : (b + 1) * G], scales[:, b * G : (b + 1) * G]
+        damping(3, 0, width=HALF // 2)
+        scatter_state(3, 0, 0, HALF // 2)
+        grouped = slot("w3_grouped", "tick_grouped", [P, G * PACK], BF16)
         weave(nc.scalar.copy, grouped[:], tick_raw[1][:])
+        square_root_factor(3, 0, slice(HALF // 2, HALF))
         tick_q[1] = whole(quantize("tick1", grouped[:]))
-        for b, tag in enumerate(("woven00", "tick_grouped")):
-            grouped = slot(tag, "late_grouped", [P, G * PACK], BF16)
-            weave(nc.scalar.copy, grouped[:], scaled[:, b])
-            h_q[b, 1] = whole(quantize("h%d1" % b, grouped[:]))
-        held = slot("scaled", "held", [P, 2, HALF], F32)
-        damping(3, 0, held[:, 0, :])
-        scatter_state(3, 0)
-        inverse_root(2, 0, held[:, 1, :])
+        scatter_state(3, 0, HALF // 2, HALF)
+        inverse_root(2, 0)
         damping(2, 0)
         scatter_state(2, 0)
 
@@ -357,7 +371,7 @@ def tile_list_gallery_state_damping_kernel(
         damping(3, 1, width=HALF // 2)
         square_root_factor(3, 1, slice(HALF // 2, HALF - LAST))
 
-        pairs = [slot(tag, "pairs", [P, 2 * T], BF16) for tag in ("sig01", "C")]
+        pairs = [slot(tag, "pairs", [P, 2 * T], BF16) for tag in ("D", "A")]
 
         def round_page(copy, t, side, lo, hi):
             base = side * T // 2
@@ -372,7 +386,7 @@ def tile_list_gallery_state_damping_kernel(
         for side in range(2):
             round_page(nc.scalar.copy, 1, side, 0, T // 2)
 
-        y_scales = kept("y_scales", [P, T], U8)
+        y_scales = kept("y_scales", [P, T // 2], U8)
         y_codes = kept("y_codes", [P, T], I32)
         y_words = out_1[0].rearrange("p m t -> p (m t)").bitcast(I32)
         spans = [(0, 512), (512, 1024), (1024, 1536), (1536, 1792), (1792, 2048)]
@@ -389,7 +403,9 @@ def tile_list_gallery_state_damping_kernel(
 
         def quantize_y(c):
             lo, hi = spans[c]
-            nc.vector.quantize_mx(out=y_codes[:, lo:hi].bitcast(FP8X4), scales=y_scales[:, lo:hi], in_=woven[c][:])
+            side = lo // (T // 2)
+            plane = y_scales[4 * side : P, lo - side * T // 2 : hi - side * T // 2]
+            nc.vector.quantize_mx(out=y_codes[:, lo:hi].bitcast(FP8X4), scales=plane, in_=woven[c][:])
             if c != 3:
                 lo = spans[min(c, 3)][0]
                 nc.sync.dma_start(out=y_words[:, lo:hi], in_=y_codes[:, lo:hi])
@@ -404,5 +420,6 @@ def tile_list_gallery_state_damping_kernel(
             quantize_y(c)
         for q in range(4):
             nc.sync.dma_start(
-                out=out_2[0, 4 * q : 4 * q + 4, :].bitcast(I32), in_=y_scales[32 * q : 32 * q + 4, :].bitcast(I32)
+                out=out_2[0, 4 * q : 4 * q + 4, :].rearrange("r (s c) -> s r c", s=2).bitcast(I32),
+                in_=y_scales[32 * q : 32 * q + 8, :].bitcast(I32),
             )

@@ -52,6 +52,11 @@ def tile_list_gallery_state_damping_kernel(
             nc.sync.dma_start(out=words[:], in_=tab_words[a].rearrange("p n t -> p (n t)").bitcast(I32))
             return words
 
+        def load_channels(name, vector, b):
+            values = kept(name, [P, PACK], F32)
+            nc.sync.dma_start(out=values[:], in_=vector[b * G : (b + 1) * G].rearrange("(p t) -> p t", t=PACK))
+            return values
+
         g_rows = gT.rearrange("(p t) m -> t p m", t=PACK)
         pages = {}
 
@@ -59,8 +64,8 @@ def tile_list_gallery_state_damping_kernel(
             pages[t] = slot(tag, "page%d" % t, [P, T], F32)
             nc.sync.dma_start(out=pages[t][:], in_=g_rows[t])
 
-        def quantize(name, grouped, width=G):
-            codes = kept(name + "_codes", [P, width], U32)
+        def quantize(name, grouped, width=G, tag=None):
+            codes = slot(tag or name, name + "_codes", [P, width], U32)
             scales = kept(name + "_scales", [P, width], U8)
             nc.vector.quantize_mx(out=codes[:].bitcast(FP8X4), scales=scales[:], in_=grouped)
             return codes, scales
@@ -87,29 +92,35 @@ def tile_list_gallery_state_damping_kernel(
         def half(h):
             return slice(h * HALF, (h + 1) * HALF)
 
-        w1_raw = {}
-        tab_s = kept("tab_s", [P, T], U8)
-        nc.gpsimd.memset(tab_s[:].bitcast(I32), 0)
-        tab_w = [load_table("C", 0)]
         offsets = keep.tile([P, S // 16], U16, name="offsets")
         nc.sync.dma_start(offsets[:], offs)
-        w1_raw[0, 0] = load_rows("B", "w1_raw00", w1[0:G, 0:G])
-        bias = kept("bias", [P, 2, PACK], F32)
-        nc.sync.dma_start(out=bias[:], in_=b1.rearrange("(b p t) -> p b t", b=2, t=PACK))
+        tab_s = slot("tab_s", "tab_s", [P, T], U8)
+        nc.vector.memset(tab_s[:].bitcast(I32), 0)
+        tab_w = [load_table("C", 0)]
+        bias = [load_channels("bias%d" % b, b1, b) for b in range(2)]
+        gains = [load_channels("gains%d" % b, gain, b) for b in range(2)]
+        w1_raw = {(0, 0): slot("B", "w1_raw00", [P, PACK, G], F32)}
+        rows_in = w1[0:G, 0:G].rearrange("(p j) c -> p j c", j=PACK)
+        for u in range(2):
+            nc.sync.dma_start(out=w1_raw[0, 0][:, 2 * u : 2 * u + 2, :], in_=rows_in[:, 2 * u : 2 * u + 2, :])
         for q in range(4):
             nc.sync.dma_start(
                 out=tab_s[32 * q : 32 * q + 8, :].bitcast(I32), in_=tab_scales[:, 4 * q : 4 * q + 4, :].bitcast(I32)
             )
-        tab_w.append(load_table("D", 1))
-        w4_raw = slot("A", "w4_raw", [P, 2, 2 * N], U8)
+        w4_raw = kept("w4_raw", [P, 2, 2 * N], U8)
         nc.sync.dma_start(out=w4_raw[:].bitcast(I32), in_=w4_words.rearrange("b p n -> p b n").bitcast(I32))
+        tab_w.append(load_table("D", 1))
+        w1_raw[1, 0] = load_rows("w10", "w1_raw10", w1[G : 2 * G, 0:G])
+        w1_raw[0, 1] = load_rows("w01", "w1_raw01", w1[0:G, G : 2 * G])
+        w1_raw[1, 1] = load_rows("w11", "w1_raw11", w1[G : 2 * G, G : 2 * G])
+        load_page("page3", 3)
+        tick_raw = [load_rows("tick0", "tick_raw0", tick[:, half(0)])]
+        w3_raw = load_rows("A", "w3_raw", w3)
+        load_page("page1", 1)
+        load_page("page0", 0)
+        load_page("page2", 2)
+        tick_raw.append(load_rows("tick1", "tick_raw1", tick[:, half(1)]))
 
-        padded = kept("padded", [P, P], F32)
-        nc.gpsimd.memset(padded[:], 0.0)
-        gains = padded[:, 0 : 2 * PACK].rearrange("p (b t) -> p b t", b=2)
-        nc.gpsimd.dma_start(out=gains, in_=gain.rearrange("(b p t) -> p b t", b=2, t=PACK))
-        identity = kept("identity", [P, P], F32)
-        make_identity(nc, identity[:])
         w4_raw_s = kept("w4_raw_s", [P, 2 * N], U8)
         nc.gpsimd.memset(w4_raw_s[:].bitcast(I32), 0)
         for q in range(4):
@@ -117,17 +128,16 @@ def tile_list_gallery_state_damping_kernel(
                 out=w4_raw_s[32 * q : 32 * q + 4, :].bitcast(I32).rearrange("i (a n) -> i a n", a=2),
                 in_=w4_scales[:, 4 * q : 4 * q + 4, :].rearrange("a i n -> i a n").bitcast(I32),
             )
-        w4_codes = kept("w4_codes", [P, 2, 2 * N], U8)
-        nc.scalar.copy(
-            out=w4_codes[:].bitcast(U16).rearrange("p b (t m) -> p b m t", t=PACK),
-            in_=w4_raw[:].bitcast(U16).rearrange("p b (m t) -> p b m t", t=PACK),
-        )
-
+        padded = kept("padded", [P, P], F32)
+        nc.gpsimd.memset(padded[:], 0.0)
+        nc.scalar.copy(out=padded[:, 0:PACK], in_=gains[1][:])
+        identity = kept("identity", [P, P], F32)
+        make_identity(nc, identity[:])
         v_words = [kept("v_words%d" % a, [P, S], U32) for a in range(2)]
         v_scales = kept("v_scales", [P, S], U8)
         w1_q = {}
 
-        def quantize_w1(a, b, copies, tags):
+        def quantize_w1(a, b, copies, tags, codes_tag=None):
             parts = len(copies)
             rows = PACK // parts
             grouped = [slot(tag, "w1_grouped", [P, G * rows], BF16) for tag in tags]
@@ -137,7 +147,7 @@ def tile_list_gallery_state_damping_kernel(
                     in_=w1_raw[a, b][:].rearrange("p j (m t) -> p m j t", t=PACK)[:, :, :, rows * u : rows * (u + 1)],
                 )
             for u in range(parts):
-                codes, scales = quantize("w1_%d%d%d" % (a, b, u), grouped[u][:], width=P * rows)
+                codes, scales = quantize("w1_%d%d%d" % (a, b, u), grouped[u][:], P * rows, codes_tag)
                 for e in range(rows):
                     w1_q[a, b, rows * u + e] = codes[:, e * P : (e + 1) * P], scales[:, e * P : (e + 1) * P]
 
@@ -146,16 +156,18 @@ def tile_list_gallery_state_damping_kernel(
 
         gather_words(0)
         nc.vector.tensor_copy(v_scales[:], tab_s[:].indirect(offsets[:]))
-        w1_raw[1, 0] = load_rows("C", "w1_raw10", w1[G : 2 * G, 0:G])
-        quantize_w1(0, 0, [nc.scalar.copy], ["g00"])
-        w4_plane = slot("g00", "w4_plane", [P, 2 * N], U8)
+        quantize_w1(0, 0, [nc.scalar.copy], ["g00"], "tab_s")
+        w4_plane = kept("w4_plane", [P, 2 * N], U8)
         nc.gpsimd.tensor_copy(
             out=w4_plane[:].rearrange("p (a t m) -> p a t m", a=2, t=PACK),
             in_=w4_raw_s[:].rearrange("p (a m t) -> p a t m", a=2, t=PACK),
         )
-        w1_raw[0, 1] = load_rows("B", "w1_raw01", w1[0:G, G : 2 * G])
+        w4_codes = kept("w4_codes", [P, 2, 2 * N], U8)
+        nc.scalar.copy(
+            out=w4_codes[:].bitcast(U16).rearrange("p b (t m) -> p b m t", t=PACK),
+            in_=w4_raw[:].bitcast(U16).rearrange("p b (m t) -> p b m t", t=PACK),
+        )
         gather_words(1)
-        w1_raw[1, 1] = load_rows("A", "w1_raw11", w1[G : 2 * G, G : 2 * G])
         quantize_w1(1, 0, [nc.vector.tensor_copy] * 2, ["w3_grouped", "g10b"])
         turned = psum.tile([P, P], F32, name="turned", tag="bank6", bufs=1)
         nc.tensor.transpose(turned[:], padded[:], identity[:])
@@ -163,7 +175,6 @@ def tile_list_gallery_state_damping_kernel(
         nc.scalar.copy(out=flipped[:], in_=turned[:])
         gains_psum = psum.tile([P, P], F32, name="gains_psum", tag="gain_bank", bufs=1)
         nc.tensor.transpose(gains_psum[:], flipped[:], identity[:])
-        load_page("C", 3)
 
         sig = {}
 
@@ -190,14 +201,14 @@ def tile_list_gallery_state_damping_kernel(
                 sig[b, h] = slot(tag, "sig%d%d" % (b, h), [P, PACK, HALF], F32)
             for t in rows:
                 nc.scalar.activation(
-                    out=sig[b, h][:, t, :], in_=x_acc[b, h, t][:], func=ACT.Sigmoid, bias=bias[:, b, t : t + 1]
+                    out=sig[b, h][:, t, :], in_=x_acc[b, h, t][:], func=ACT.Sigmoid, bias=bias[b][:, t : t + 1]
                 )
 
         def scale_on_gpsimd(b, h, t, scaled):
             nc.gpsimd.tensor_scalar(
                 out=scaled[:, t, :],
                 in0=sig[b, h][:, t, :],
-                scalar1=gains[:, b, t : t + 1],
+                scalar1=gains[b][:, t : t + 1],
                 scalar2=0.0,
                 op0=MULT,
                 op1=ADD,
@@ -261,7 +272,7 @@ def tile_list_gallery_state_damping_kernel(
                 squares = [square[:, cols] for cols in pieces(t, h)]
             for cols, square in zip(pieces(t, h), squares):
                 nc.scalar.activation(out=square, in_=e_acc[t, h][:, cols], func=ACT.Square)
-            root[t, h] = slot("sig10" if last else "root", "root", [P, HALF], F32, bufs=1 if last else 3)
+            root[t, h] = slot("B" if last else "root", "root", [P, HALF], F32, bufs=1 if last else 3)
             for cols, square in zip(pieces(t, h), squares):
                 nc.scalar.activation(out=root[t, h][:, cols], in_=square, func=ACT.Abs_reciprocal_sqrt, bias=1.0)
 
@@ -281,27 +292,22 @@ def tile_list_gallery_state_damping_kernel(
             return pair[0][:], pair[1][:]
 
         stage_one(0, 0, {0: 0, 1: 1, 2: 2, 3: 3})
-        sigmoids(0, 0, "E")
+        sigmoids(0, 0, "C")
         quantize_w1(0, 1, [nc.vector.tensor_copy] * 2, ["g01a", "g01b"])
-        tick_raw = [load_rows("B", "tick_raw0", tick[:, half(0)])]
         quantize_w1(1, 1, [nc.vector.tensor_copy] * 2, ["F", "h00_grouped"])
-        w3_raw = load_rows("A", "w3_raw", w3)
-        load_page("F", 1)
         gather_page(3, kept("picked3", [P, S], F32)[:])
         scaled = slot("h00_grouped", "scaled00", [P, PACK, HALF], BF16)
         for t in range(PACK):
             scale_on_gpsimd(0, 0, t, scaled)
         tick_grouped = slot("tick_grouped", "tick_grouped", [P, G * PACK], BF16)
         stage_one(1, 0, {0: 1, 1: 2, 2: 3, 3: 0})
-        sigmoids(1, 0, "sig10")
+        sigmoids(1, 0, "B")
         stage_one(0, 1, {0: 4, 1: 5, 2: 6})
 
-        load_page("E", 0)
         weave(nc.scalar.copy, tick_grouped[:], tick_raw[0][:])
-        load_page("B", 2)
         grouped = slot("h10_grouped", "h10_grouped", [P, G * PACK], BF16)
         dst, src = woven_views(grouped[:], sig[1, 0][:], run=2)
-        factor = gains_psum[:, PACK : 2 * PACK].unsqueeze(1).unsqueeze(3).broadcast_to([P, HALF // 2, PACK, 2])
+        factor = gains_psum[:, 0:PACK].unsqueeze(1).unsqueeze(3).broadcast_to([P, HALF // 2, PACK, 2])
         nc.vector.tensor_tensor(out=dst, in0=src, in1=factor, op=MULT)
         tick_q[0] = whole(quantize("tick0", tick_grouped[:]))
         h_q[1, 0] = whole(quantize("h10", grouped[:]))
@@ -314,7 +320,6 @@ def tile_list_gallery_state_damping_kernel(
         deal(nc.scalar.copy, grouped[:], w3_raw[:])
         w3_q = quantize("w3", grouped[:])
         sigmoids(0, 1, "D", range(PACK - 1))
-        tick_raw.append(load_rows("h00_grouped", "tick_raw1", tick[:, half(1)]))
         stage_one(1, 1, {0: 2, 1: 3, 2: 4, 3: 5})
         sigmoids(1, 1, "A")
         stage_one(0, 1, {3: 2})
@@ -387,10 +392,10 @@ def tile_list_gallery_state_damping_kernel(
             round_page(nc.scalar.copy, 1, side, 0, T // 2)
 
         y_scales = kept("y_scales", [P, T // 2], U8)
-        y_codes = kept("y_codes", [P, T], I32)
+        y_codes = slot("C", "y_codes", [P, T], I32)
         y_words = out_1[0].rearrange("p m t -> p (m t)").bitcast(I32)
         spans = [(0, 512), (512, 1024), (1024, 1536), (1536, 1792), (1792, 2048)]
-        woven = [kept("woven%d" % lo, [P, (hi - lo) * PACK], BF16) for lo, hi in spans]
+        woven = [slot(tag, "woven", [P, (hi - lo) * PACK], BF16) for tag, (lo, hi) in zip(("w10", "w01", "w11", "tick0", "tick1"), spans)]
 
         def weave_words(copy, c):
             side, lo = divmod(spans[c][0], T // 2)

@@ -25,7 +25,6 @@ HALF = 512
 LIST_COLS = HALF // 16
 LAST = 64
 SHARE = 384
-LATE_SHARE = 192
 
 
 def tile_list_gallery_state_damping_kernel(
@@ -70,12 +69,6 @@ def tile_list_gallery_state_damping_kernel(
             nc.vector.quantize_mx(out=codes[:].bitcast(FP8X4), scales=scales[:], in_=grouped)
             return codes, scales
 
-        def deal(copy, grouped, raw):
-            copy(
-                out=grouped.rearrange("p (t m j) -> p m j t", t=PACK, j=PACK),
-                in_=raw.rearrange("p j (m t) -> p m j t", t=PACK),
-            )
-
         def woven_views(grouped, raw, run=4):
             return (
                 grouped.rearrange("p (c i t) -> p c t i", i=run, t=PACK),
@@ -105,7 +98,7 @@ def tile_list_gallery_state_damping_kernel(
             nc.sync.dma_start(out=w1_raw[0, 0][:, 2 * u : 2 * u + 2, :], in_=rows_in[:, 2 * u : 2 * u + 2, :])
         for q in range(4):
             nc.sync.dma_start(
-                out=tab_s[32 * q : 32 * q + 8, :].bitcast(I32), in_=tab_scales[:, 4 * q : 4 * q + 4, :].bitcast(I32)
+                out=tab_s[32 * q + 4 : 32 * q + 12, :].bitcast(I32), in_=tab_scales[:, 4 * q : 4 * q + 4, :].bitcast(I32)
             )
         w4_raw = kept("w4_raw", [P, 2, 2 * N], U8)
         nc.sync.dma_start(out=w4_raw[:].bitcast(I32), in_=w4_words.rearrange("b p n -> p b n").bitcast(I32))
@@ -137,19 +130,23 @@ def tile_list_gallery_state_damping_kernel(
         v_scales = kept("v_scales", [P, S], U8)
         w1_q = {}
 
-        def quantize_w1(a, b, copies, tags, codes_tag=None):
+        def quantize_dealt(name, raw, copies, tags, codes_tag=None):
             parts = len(copies)
             rows = PACK // parts
-            grouped = [slot(tag, "w1_grouped", [P, G * rows], BF16) for tag in tags]
+            grouped = [slot(tag, name + "_grouped", [P, G * rows], BF16) for tag in tags]
             for u, copy in enumerate(copies):
                 copy(
                     out=grouped[u][:].rearrange("p (t m j) -> p m j t", t=rows, j=PACK),
-                    in_=w1_raw[a, b][:].rearrange("p j (m t) -> p m j t", t=PACK)[:, :, :, rows * u : rows * (u + 1)],
+                    in_=raw[:].rearrange("p j (m t) -> p m j t", t=PACK)[:, :, :, rows * u : rows * (u + 1)],
                 )
+            weights = []
             for u in range(parts):
-                codes, scales = quantize("w1_%d%d%d" % (a, b, u), grouped[u][:], P * rows, codes_tag)
-                for e in range(rows):
-                    w1_q[a, b, rows * u + e] = codes[:, e * P : (e + 1) * P], scales[:, e * P : (e + 1) * P]
+                codes, scales = quantize("%s_%d" % (name, u), grouped[u][:], P * rows, codes_tag)
+                weights.extend((codes[:, e * P : (e + 1) * P], scales[:, e * P : (e + 1) * P]) for e in range(rows))
+            return weights
+
+        def quantize_w1(a, b, copies, tags, codes_tag=None):
+            w1_q[a, b] = quantize_dealt("w1_%d%d" % (a, b), w1_raw[a, b], copies, tags, codes_tag)
 
         def gather_words(a):
             nc.vector.tensor_copy(v_words[a][:], tab_w[a][:].bitcast(U32).indirect(offsets[:]))
@@ -185,21 +182,20 @@ def tile_list_gallery_state_damping_kernel(
                 acc = psum.tile([P, HALF], F32, name="x_acc", tag="bank%d" % banks[t], bufs=1)
                 x_acc[b, h, t] = acc
                 for a in range(2):
-                    codes, scales = w1_q[a, b, t]
+                    codes, scales = w1_q[a, b][t]
                     nc.tensor.matmul_mx(
                         out=acc[:],
                         lhsT=codes.bitcast(FP8X4),
                         lhsT_scale=scales,
                         rhs=v_words[a][:, half(h)].bitcast(FP8X4),
-                        rhs_scale=v_scales[4 * a : P, half(h)],
+                        rhs_scale=v_scales[4 * (a + 1) : P, half(h)],
                         start=(a == 0),
                         stop=(a == 1),
                     )
 
-        def sigmoids(b, h, tag, rows=range(PACK)):
-            if tag:
-                sig[b, h] = slot(tag, "sig%d%d" % (b, h), [P, PACK, HALF], F32)
-            for t in rows:
+        def sigmoids(b, h, tag):
+            sig[b, h] = slot(tag, "sig%d%d" % (b, h), [P, PACK, HALF], F32)
+            for t in range(PACK):
                 nc.scalar.activation(
                     out=sig[b, h][:, t, :], in_=x_acc[b, h, t][:], func=ACT.Sigmoid, bias=bias[b][:, t : t + 1]
                 )
@@ -235,9 +231,8 @@ def tile_list_gallery_state_damping_kernel(
         e_acc, root, damp = {}, {}, {}
 
         def stage_two(t, h):
-            e_acc[t, h] = psum.tile([P, HALF], F32, name="e_acc", tag="bank%d" % ((0, 1, 3, 6), (4, 2, 5, 0))[h][t], bufs=1)
-            cols = slice(t * P, (t + 1) * P)
-            ticket = [(w3_q[0][:, cols].bitcast(FP8X4), w3_q[1][:, cols], tick_q[h])]
+            e_acc[t, h] = psum.tile([P, HALF], F32, name="e_acc", tag="bank%d" % ((0, 6, 1, 2), (0, 0, 1, 1))[h][t], bufs=1)
+            ticket = [(w3_q[t][0].bitcast(FP8X4), w3_q[t][1], tick_q[h])]
             gallery = [
                 (
                     w4_codes[:, b, 2 * t * P : 2 * (t + 1) * P].bitcast(FP4X4),
@@ -259,7 +254,7 @@ def tile_list_gallery_state_damping_kernel(
                 )
 
         def pieces(t, h):
-            width = HALF // 2 if (t, h) in ((0, 0), (2, 0), (3, 1)) else HALF
+            width = HALF // 2 if h == 0 or t in (0, 3) else HALF
             return [slice(lo, lo + width) for lo in range(0, HALF, width)]
 
         def inverse_root(t, h, square=None):
@@ -302,9 +297,10 @@ def tile_list_gallery_state_damping_kernel(
         tick_grouped = slot("tick_grouped", "tick_grouped", [P, G * PACK], BF16)
         stage_one(1, 0, {0: 1, 1: 2, 2: 3, 3: 0})
         sigmoids(1, 0, "B")
-        stage_one(0, 1, {0: 4, 1: 5, 2: 6})
+        stage_one(0, 1, {0: 4, 1: 5, 2: 6, 3: 1})
 
-        weave(nc.scalar.copy, tick_grouped[:], tick_raw[0][:])
+        weave(nc.vector.tensor_copy, tick_grouped[:, 0 : G * PACK // 2], tick_raw[0][:, :, 0 : HALF // 2])
+        weave(nc.scalar.copy, tick_grouped[:, G * PACK // 2 :], tick_raw[0][:, :, HALF // 2 :])
         grouped = slot("h10_grouped", "h10_grouped", [P, G * PACK], BF16)
         dst, src = woven_views(grouped[:], sig[1, 0][:], run=2)
         factor = gains_psum[:, 0:PACK].unsqueeze(1).unsqueeze(3).broadcast_to([P, HALF // 2, PACK, 2])
@@ -316,38 +312,33 @@ def tile_list_gallery_state_damping_kernel(
             weave_on_gpsimd(grouped[:], scaled, lo, lo + SHARE // 2)
         weave(nc.scalar.copy, grouped[:, SHARE * PACK :], scaled[:, :, SHARE:])
         h_q[0, 0] = whole(quantize("h00", grouped[:]))
-        grouped = slot("scaled", "w3_grouped", [P, G * PACK], BF16)
-        deal(nc.scalar.copy, grouped[:], w3_raw[:])
-        w3_q = quantize("w3", grouped[:])
-        sigmoids(0, 1, "D", range(PACK - 1))
+        w3_q = quantize_dealt("w3", w3_raw, [nc.scalar.copy] * 2, ["picked", "scaled"])
+        sigmoids(0, 1, "D")
         stage_one(1, 1, {0: 2, 1: 3, 2: 4, 3: 5})
         sigmoids(1, 1, "A")
-        stage_one(0, 1, {3: 2})
-        sigmoids(0, 1, None, [PACK - 1])
-        filler = kept("picked", [P, PACK - 1, S], F32)
+        filler = slot("picked", "picked", [P, PACK - 1, S], F32)
         for t in (1, 0, 2):
             gather_page(t, filler[:, t, :])
         for t in range(PACK):
             stage_two(t, 0)
 
-        scaled = [slot(tag, "scaled_late", [P, PACK, HALF], BF16) for tag in ("h10_grouped", "scaled")]
+        scaled = slot("scaled", "scaled_late", [P, 2, PACK, HALF], BF16)
         late = slot("woven00", "late_grouped", [P, 2 * G * PACK], BF16)
         for b in range(2):
             for t in range(PACK):
-                scale_on_gpsimd(b, 1, t, scaled[b])
-        weave_on_gpsimd(late[:], scaled[0], 0, LATE_SHARE)
+                scale_on_gpsimd(b, 1, t, scaled[:, b])
         inverse_root(0, 0)
         damping(0, 0)
         scatter_state(0, 0)
         inverse_root(1, 0)
-        inverse_root(3, 0)
         damping(1, 0)
         scatter_state(1, 0)
-        weave(nc.scalar.copy, late[:, LATE_SHARE * PACK : G * PACK], scaled[0][:, :, LATE_SHARE:])
-        weave(nc.scalar.copy, late[:, G * PACK :], scaled[1][:])
+        for b in range(2):
+            weave(nc.scalar.copy, late[:, b * G * PACK : (b + 1) * G * PACK], scaled[:, b])
         codes, scales = quantize("h_late", late[:], width=2 * G)
         for b in range(2):
             h_q[b, 1] = codes[:, b * G : (b + 1) * G], scales[:, b * G : (b + 1) * G]
+        inverse_root(3, 0)
         damping(3, 0, width=HALF // 2)
         scatter_state(3, 0, 0, HALF // 2)
         grouped = slot("w3_grouped", "tick_grouped", [P, G * PACK], BF16)

@@ -100,8 +100,6 @@ def tile_list_gallery_state_damping_kernel(
             nc.sync.dma_start(
                 out=tab_s[32 * q + 4 : 32 * q + 12, :].bitcast(I32), in_=tab_scales[:, 4 * q : 4 * q + 4, :].bitcast(I32)
             )
-        w4_raw = kept("w4_raw", [P, 2, 2 * N], U8)
-        nc.sync.dma_start(out=w4_raw[:].bitcast(I32), in_=w4_words.rearrange("b p n -> p b n").bitcast(I32))
         tab_w.append(load_table("D", 1))
         w1_raw[1, 0] = load_rows("w10", "w1_raw10", w1[G : 2 * G, 0:G])
         w1_raw[0, 1] = load_rows("w01", "w1_raw01", w1[0:G, G : 2 * G])
@@ -109,11 +107,17 @@ def tile_list_gallery_state_damping_kernel(
         load_page("page3", 3)
         tick_raw = [load_rows("tick0", "tick_raw0", tick[:, half(0)])]
         w3_raw = load_rows("A", "w3_raw", w3)
+        w4_raw = kept("w4_raw", [P, 2, 2 * N], U8)
+        nc.sync.dma_start(out=w4_raw[:].bitcast(I32), in_=w4_words.rearrange("b p n -> p b n").bitcast(I32))
         load_page("page1", 1)
         load_page("page0", 0)
         load_page("page2", 2)
         tick_raw.append(load_rows("tick1", "tick_raw1", tick[:, half(1)]))
 
+        padded = kept("padded", [P, P], F32)
+        nc.gpsimd.memset(padded[:], 0.0)
+        unread = kept("unread", [P, 1], F32)
+        nc.scalar.activation(out=unread[:], in_=padded[:, P - 1 : P], func=ACT.Sigmoid)
         w4_raw_s = kept("w4_raw_s", [P, 2 * N], U8)
         nc.gpsimd.memset(w4_raw_s[:].bitcast(I32), 0)
         for q in range(4):
@@ -121,12 +125,10 @@ def tile_list_gallery_state_damping_kernel(
                 out=w4_raw_s[32 * q : 32 * q + 4, :].bitcast(I32).rearrange("i (a n) -> i a n", a=2),
                 in_=w4_scales[:, 4 * q : 4 * q + 4, :].rearrange("a i n -> i a n").bitcast(I32),
             )
-        padded = kept("padded", [P, P], F32)
-        nc.gpsimd.memset(padded[:], 0.0)
         nc.scalar.copy(out=padded[:, 0:PACK], in_=gains[1][:])
         identity = kept("identity", [P, P], F32)
         make_identity(nc, identity[:])
-        v_words = [kept("v_words%d" % a, [P, S], U32) for a in range(2)]
+        v_words = [slot(tag, "v_words", [P, S], U32) for tag in ("v0", "B")]
         v_scales = kept("v_scales", [P, S], U8)
         w1_q = {}
 
@@ -159,13 +161,8 @@ def tile_list_gallery_state_damping_kernel(
             out=w4_plane[:].rearrange("p (a t m) -> p a t m", a=2, t=PACK),
             in_=w4_raw_s[:].rearrange("p (a m t) -> p a t m", a=2, t=PACK),
         )
-        w4_codes = kept("w4_codes", [P, 2, 2 * N], U8)
-        nc.scalar.copy(
-            out=w4_codes[:].bitcast(U16).rearrange("p b (t m) -> p b m t", t=PACK),
-            in_=w4_raw[:].bitcast(U16).rearrange("p b (m t) -> p b m t", t=PACK),
-        )
         gather_words(1)
-        quantize_w1(1, 0, [nc.vector.tensor_copy] * 2, ["w3_grouped", "g10b"])
+        quantize_w1(1, 0, [nc.scalar.copy] * 2, ["w3_grouped", "g10b"])
         turned = psum.tile([P, P], F32, name="turned", tag="bank6", bufs=1)
         nc.tensor.transpose(turned[:], padded[:], identity[:])
         flipped = kept("flipped", [P, P], F32)
@@ -296,7 +293,7 @@ def tile_list_gallery_state_damping_kernel(
             scale_on_gpsimd(0, 0, t, scaled)
         tick_grouped = slot("tick_grouped", "tick_grouped", [P, G * PACK], BF16)
         stage_one(1, 0, {0: 1, 1: 2, 2: 3, 3: 0})
-        sigmoids(1, 0, "B")
+        sigmoids(1, 0, "w10")
         stage_one(0, 1, {0: 4, 1: 5, 2: 6, 3: 1})
 
         weave(nc.vector.tensor_copy, tick_grouped[:, 0 : G * PACK // 2], tick_raw[0][:, :, 0 : HALF // 2])
@@ -313,6 +310,11 @@ def tile_list_gallery_state_damping_kernel(
         weave(nc.scalar.copy, grouped[:, SHARE * PACK :], scaled[:, :, SHARE:])
         h_q[0, 0] = whole(quantize("h00", grouped[:]))
         w3_q = quantize_dealt("w3", w3_raw, [nc.scalar.copy] * 2, ["picked", "scaled"])
+        w4_codes = kept("w4_codes", [P, 2, 2 * N], U8)
+        nc.scalar.copy(
+            out=w4_codes[:].bitcast(U16).rearrange("p b (t m) -> p b m t", t=PACK),
+            in_=w4_raw[:].bitcast(U16).rearrange("p b (m t) -> p b m t", t=PACK),
+        )
         sigmoids(0, 1, "D")
         stage_one(1, 1, {0: 2, 1: 3, 2: 4, 3: 5})
         sigmoids(1, 1, "A")

@@ -197,10 +197,10 @@ def tile_list_gallery_state_damping_kernel(
                     out=sig[b, h][:, t, :], in_=x_acc[b, h, t][:], func=ACT.Sigmoid, bias=bias[b][:, t : t + 1]
                 )
 
-        def scale_on_gpsimd(b, h, t, scaled):
+        def scale_on_gpsimd(b, h, t, scaled, width=HALF):
             nc.gpsimd.tensor_scalar(
-                out=scaled[:, t, :],
-                in0=sig[b, h][:, t, :],
+                out=scaled[:, t, 0:width],
+                in0=sig[b, h][:, t, 0:width],
                 scalar1=gains[b][:, t : t + 1],
                 scalar2=0.0,
                 op0=MULT,
@@ -290,10 +290,16 @@ def tile_list_gallery_state_damping_kernel(
         gather_page(3, kept("picked3", [P, S], F32)[:])
         scaled = slot("h00_grouped", "scaled00", [P, PACK, HALF], BF16)
         for t in range(PACK):
-            scale_on_gpsimd(0, 0, t, scaled)
+            scale_on_gpsimd(0, 0, t, scaled, HALF if t < PACK - 1 else HALF // 2)
         tick_grouped = slot("tick_grouped", "tick_grouped", [P, G * PACK], BF16)
         stage_one(1, 0, {0: 1, 1: 2, 2: 3, 3: 0})
         sigmoids(1, 0, "w10")
+        nc.scalar.activation(
+            out=scaled[:, PACK - 1, HALF // 2 :],
+            in_=sig[0, 0][:, PACK - 1, HALF // 2 :],
+            func=ACT.Copy,
+            scale=gains[0][:, PACK - 1 : PACK],
+        )
         stage_one(0, 1, {0: 4, 1: 5, 2: 6, 3: 1})
 
         weave(nc.vector.tensor_copy, tick_grouped[:, 0 : G * PACK // 2], tick_raw[0][:, :, 0 : HALF // 2])

@@ -390,40 +390,42 @@ def tile_list_gallery_state_damping_kernel(
         for side in range(2):
             round_page(nc.scalar.copy, 1, side, 0, T // 2)
 
-        y_scales = kept("y_scales", [P, T // 2], U8)
+        span = T // 8
+        y_scales = kept("y_scales", [P, 2 * span], U8)
         y_codes = slot("C", "y_codes", [P, T], I32)
         y_words = out_1[0].rearrange("p m t -> p (m t)").bitcast(I32)
-        spans = [(0, 512), (512, 1024), (1024, 1536), (1536, 1792), (1792, 2048)]
-        woven = [slot(tag, "woven", [P, (hi - lo) * PACK], BF16) for tag, (lo, hi) in zip(("w10", "w01", "w11", "tick0", "tick1"), spans)]
+        woven = [slot(tag, "woven", [P, 2 * span * PACK], BF16) for tag in ("w10", "w01", "w11", "tick0")]
+
+        def woven_span(c):
+            return woven[c // 2][:, c % 2 * span * PACK : (c % 2 + 1) * span * PACK]
 
         def weave_words(copy, c):
-            side, lo = divmod(spans[c][0], T // 2)
-            hi = lo + spans[c][1] - spans[c][0]
+            side, lo = divmod(c * span, T // 2)
             words = pairs[side][:].bitcast(F32).rearrange("p (u c) -> p u c", u=2)
             copy(
-                out=woven[c][:].bitcast(F32).rearrange("p (c i u) -> p c u i", i=4, u=2),
-                in_=words[:, :, lo:hi].rearrange("p u (c i) -> p c u i", i=4),
+                out=woven_span(c).bitcast(F32).rearrange("p (c i u) -> p c u i", i=4, u=2),
+                in_=words[:, :, lo : lo + span].rearrange("p u (c i) -> p c u i", i=4),
             )
 
         def quantize_y(c):
-            lo, hi = spans[c]
-            side = lo // (T // 2)
-            plane = y_scales[4 * side : P, lo - side * T // 2 : hi - side * T // 2]
-            nc.vector.quantize_mx(out=y_codes[:, lo:hi].bitcast(FP8X4), scales=plane, in_=woven[c][:])
-            if c != 3:
-                lo = spans[min(c, 3)][0]
-                nc.sync.dma_start(out=y_words[:, lo:hi], in_=y_codes[:, lo:hi])
+            plane = y_scales[4 * (c // 2) : P, c % 2 * span : (c % 2 + 1) * span]
+            cols = slice(c * span, (c + 1) * span)
+            nc.vector.quantize_mx(out=y_codes[:, cols].bitcast(FP8X4), scales=plane, in_=woven_span(c))
+            if c % 2 == 1 or c == 6:
+                cols = cols if c >= 6 else slice((c - 1) * span, (c + 1) * span)
+                nc.sync.dma_start(out=y_words[:, cols], in_=y_codes[:, cols])
 
         round_page(nc.vector.tensor_copy, 3, 0, 0, T // 4)
         round_page(nc.vector.tensor_copy, 3, 0, T // 4, T // 2)
         round_page(nc.scalar.copy, 3, 1, 0, T // 4)
         round_page(nc.scalar.copy, 3, 1, T // 4, T // 2)
-        for c in range(len(spans)):
-            weave_words(nc.vector.tensor_copy if c < 2 else nc.scalar.copy, c)
-        for c in range(len(spans)):
-            quantize_y(c)
+        for c in range(0, 8, 2):
+            for e in range(2):
+                weave_words(nc.vector.tensor_copy if c < 4 else nc.scalar.copy, c + e)
+            for e in range(2):
+                quantize_y(c + e)
         for q in range(4):
-            nc.sync.dma_start(
-                out=out_2[0, 4 * q : 4 * q + 4, :].rearrange("r (s c) -> s r c", s=2).bitcast(I32),
-                in_=y_scales[32 * q : 32 * q + 8, :].bitcast(I32),
+            (nc.sync, nc.scalar)[q % 2].dma_start(
+                out=out_2[0, 4 * q : 4 * q + 4, :].rearrange("r (s c) -> s r c", s=4).bitcast(I32),
+                in_=y_scales[32 * q : 32 * q + 16, :].bitcast(I32),
             )

@@ -197,10 +197,10 @@ def tile_list_gallery_state_damping_kernel(
                     out=sig[b, h][:, t, :], in_=x_acc[b, h, t][:], func=ACT.Sigmoid, bias=bias[b][:, t : t + 1]
                 )
 
-        def scale_on_gpsimd(b, h, t, scaled, width=HALF):
+        def scale_on_gpsimd(b, h, t, scaled):
             nc.gpsimd.tensor_scalar(
-                out=scaled[:, t, 0:width],
-                in0=sig[b, h][:, t, 0:width],
+                out=scaled[:, t, :],
+                in0=sig[b, h][:, t, :],
                 scalar1=gains[b][:, t : t + 1],
                 scalar2=0.0,
                 op0=MULT,
@@ -289,27 +289,49 @@ def tile_list_gallery_state_damping_kernel(
         quantize_w1(1, 1, [nc.vector.tensor_copy] * 2, ["F", "h00_grouped"])
         gather_page(3, kept("picked3", [P, S], F32)[:])
         scaled = slot("h00_grouped", "scaled00", [P, PACK, HALF], BF16)
-        for t in range(PACK):
-            scale_on_gpsimd(0, 0, t, scaled, HALF if t < PACK - 1 else HALF // 2)
+        for t in range(PACK - 1):
+            scale_on_gpsimd(0, 0, t, scaled)
         tick_grouped = slot("tick_grouped", "tick_grouped", [P, G * PACK], BF16)
-        stage_one(1, 0, {0: 1, 1: 2, 2: 3, 3: 0})
-        sigmoids(1, 0, "w10")
+        quarter = HALF // 2
+        sig10 = [slot(tag, "sig10", [P, PACK, quarter], F32) for tag in ("w10", "w01")]
+        for side in range(2):
+            cols = slice(side * quarter, (side + 1) * quarter)
+            for pair in range(2):
+                acc = psum.tile([P, 2, quarter], F32, name="x_pair", tag="bank%d" % (1, 2, 3, 0)[2 * side + pair], bufs=1)
+                for a in range(2):
+                    for e in range(2):
+                        codes, scales = w1_q[a, 1][2 * pair + e]
+                        nc.tensor.matmul_mx(
+                            out=acc[:, e, :],
+                            lhsT=codes.bitcast(FP8X4),
+                            lhsT_scale=scales,
+                            rhs=v_words[a][:, cols].bitcast(FP8X4),
+                            rhs_scale=v_scales[4 * (a + 1) : P, cols],
+                            start=(a, e) == (0, 0),
+                            stop=(a, e) == (1, 1),
+                        )
+                for e in range(2):
+                    t = 2 * pair + e
+                    nc.scalar.activation(
+                        out=sig10[side][:, t, :], in_=acc[:, e, :], func=ACT.Sigmoid, bias=bias[1][:, t : t + 1]
+                    )
         nc.scalar.activation(
-            out=scaled[:, PACK - 1, HALF // 2 :],
-            in_=sig[0, 0][:, PACK - 1, HALF // 2 :],
+            out=scaled[:, PACK - 1, :],
+            in_=sig[0, 0][:, PACK - 1, :],
             func=ACT.Copy,
             scale=gains[0][:, PACK - 1 : PACK],
         )
         stage_one(0, 1, {0: 4, 1: 5, 2: 6, 3: 1})
 
-        weave(nc.vector.tensor_copy, tick_grouped[:, 0 : G * PACK // 2], tick_raw[0][:, :, 0 : HALF // 2])
         weave(nc.scalar.copy, tick_grouped[:, G * PACK // 2 :], tick_raw[0][:, :, HALF // 2 :])
         grouped = slot("h10_grouped", "h10_grouped", [P, G * PACK], BF16)
-        dst, src = woven_views(grouped[:], sig[1, 0][:], run=2)
-        factor = gains_psum[:, 0:PACK].unsqueeze(1).unsqueeze(3).broadcast_to([P, HALF // 2, PACK, 2])
-        nc.vector.tensor_tensor(out=dst, in0=src, in1=factor, op=MULT)
-        tick_q[0] = whole(quantize("tick0", tick_grouped[:]))
+        factor = gains_psum[:, 0:PACK].unsqueeze(1).unsqueeze(3).broadcast_to([P, quarter // 2, PACK, 2])
+        for side in range(2):
+            dst, src = woven_views(grouped[:, side * quarter * PACK : (side + 1) * quarter * PACK], sig10[side][:], run=2)
+            nc.vector.tensor_tensor(out=dst, in0=src, in1=factor, op=MULT)
+        weave(nc.vector.tensor_copy, tick_grouped[:, 0 : G * PACK // 2], tick_raw[0][:, :, 0 : HALF // 2])
         h_q[1, 0] = whole(quantize("h10", grouped[:]))
+        tick_q[0] = whole(quantize("tick0", tick_grouped[:]))
         grouped = slot("woven00", "h00_grouped", [P, G * PACK], BF16)
         for lo in (0, SHARE // 2):
             weave_on_gpsimd(grouped[:], scaled, lo, lo + SHARE // 2)

@@ -92,14 +92,18 @@ def tile_list_gallery_state_damping_kernel(
         tab_w = [load_table("C", 0)]
         bias = [load_channels("bias%d" % b, b1, b) for b in range(2)]
         gains = [load_channels("gains%d" % b, gain, b) for b in range(2)]
-        w1_raw = {(0, 0): slot("B", "w1_raw00", [P, PACK, G], F32)}
-        rows_in = w1[0:G, 0:G].rearrange("(p j) c -> p j c", j=PACK)
-        for u in range(2):
-            nc.sync.dma_start(out=w1_raw[0, 0][:, 2 * u : 2 * u + 2, :], in_=rows_in[:, 2 * u : 2 * u + 2, :])
-        for q in range(4):
-            nc.sync.dma_start(
-                out=tab_s[32 * q + 4 : 32 * q + 12, :].bitcast(I32), in_=tab_scales[:, 4 * q : 4 * q + 4, :].bitcast(I32)
-            )
+
+        def load_scale_rows(q):
+            for a in range(2):
+                first = 32 * q + 4 * (a + 1)
+                nc.sync.dma_start(
+                    out=tab_s[first : first + 4, :].bitcast(I32), in_=tab_scales[a, 4 * q : 4 * q + 4, :].bitcast(I32)
+                )
+
+        load_scale_rows(0)
+        w1_raw = {(0, 0): load_rows("B", "w1_raw00", w1[0:G, 0:G])}
+        for q in range(1, 4):
+            load_scale_rows(q)
         tab_w.append(load_table("D", 1))
         w1_raw[1, 0] = load_rows("w10", "w1_raw10", w1[G : 2 * G, 0:G])
         w1_raw[0, 1] = load_rows("w01", "w1_raw01", w1[0:G, G : 2 * G])

@@ -93,11 +93,10 @@ def tile_list_gallery_state_damping_kernel(
         bias = [load_channels("bias%d" % b, b1, b) for b in range(2)]
         gains = [load_channels("gains%d" % b, gain, b) for b in range(2)]
 
-        def load_scale_rows(q):
+        def load_scale_rows(i):
             for a in range(2):
-                first = 32 * q + 4 * (a + 1)
                 nc.sync.dma_start(
-                    out=tab_s[first : first + 4, :].bitcast(I32), in_=tab_scales[a, 4 * q : 4 * q + 4, :].bitcast(I32)
+                    out=tab_s[4 * (a + 1) + i : P : 32, :].bitcast(I32), in_=tab_scales[a, i:16:4, :].bitcast(I32)
                 )
 
         load_scale_rows(0)

@@ -108,7 +108,7 @@ def tile_list_gallery_state_damping_kernel(
         w1_raw[0, 1] = load_rows("w01", "w1_raw01", w1[0:G, G : 2 * G])
         w1_raw[1, 1] = load_rows("w11", "w1_raw11", w1[G : 2 * G, G : 2 * G])
         load_page("page3", 3)
-        tick_raw = [load_rows("tick0", "tick_raw0", tick[:, half(0)])]
+        tick_raw = [load_rows("w01", "tick_raw0", tick[:, half(0)])]
         w3_raw = load_rows("A", "w3_raw", w3)
         w4_raw = kept("w4_raw", [P, 2, 2 * N], U8)
         nc.sync.dma_start(out=w4_raw[:].bitcast(I32), in_=w4_words.rearrange("b p n -> p b n").bitcast(I32))
@@ -296,7 +296,7 @@ def tile_list_gallery_state_damping_kernel(
             scale_on_gpsimd(0, 0, t, scaled)
         tick_grouped = slot("tick_grouped", "tick_grouped", [P, G * PACK], BF16)
         quarter = HALF // 2
-        sig10 = [slot(tag, "sig10", [P, PACK, quarter], F32) for tag in ("w10", "w01")]
+        sig10 = [slot(tag, "sig10", [P, PACK, quarter], F32) for tag in ("w10", "tick0")]
         for side in range(2):
             cols = slice(side * quarter, (side + 1) * quarter)
             for pair in range(2):

from contextlib import ExitStack

import concourse.mybir as mybir
from concourse.masks import make_identity

T, S, K, H, M, N = 2048, 1024, 1024, 1024, 512, 512
FLOPS = 2 * K * H * S + 2 * H * N * S + 2 * M * N * S

F32 = mybir.dt.float32
BF16 = mybir.dt.bfloat16
I32 = mybir.dt.int32
U32 = mybir.dt.uint32
U16 = mybir.dt.uint16
U8 = mybir.dt.uint8
FP8X4 = mybir.dt.float8_e4m3fn_x4
FP4X4 = mybir.dt.float4_e2m1fn_x4
ACT = mybir.ActivationFunctionType
MULT = mybir.AluOpType.mult
ADD = mybir.AluOpType.add

P = 128
PACK = 4
G = P * PACK
HALF = 512
LIST_COLS = HALF // 16
LAST = 64
SHARE = 384


def tile_list_gallery_state_damping_kernel(
    tc, tab_words, tab_scales, offs, gT, w1, b1, gain, w4_words, w4_scales, tick, w3, out_0, out_1, out_2
):
    nc = tc.nc
    with ExitStack() as ctx:
        keep = ctx.enter_context(tc.tile_pool(name="keep", bufs=1))
        psum = ctx.enter_context(tc.psum_pool(name="psum", bufs=7))

        def kept(name, shape, dtype):
            return keep.tile(shape, dtype, name=name, align_bytes=64)

        def slot(tag, name, shape, dtype, bufs=1):
            return keep.tile(shape, dtype, name=name, tag=tag, bufs=bufs, align_bytes=64)

        def load_rows(tag, name, rows):
            raw = slot(tag, name, [P, PACK, G], F32)
            nc.sync.dma_start(out=raw[:], in_=rows.rearrange("(p j) c -> p j c", j=PACK))
            return raw

        def load_table(tag, a):
            words = slot(tag, "tab_w%d" % a, [P, T], I32)
            nc.sync.dma_start(out=words[:], in_=tab_words[a].rearrange("p n t -> p (n t)").bitcast(I32))
            return words

        def load_channels(name, vector, b):
            values = kept(name, [P, PACK], F32)
            nc.sync.dma_start(out=values[:], in_=vector[b * G : (b + 1) * G].rearrange("(p t) -> p t", t=PACK))
            return values

        g_rows = gT.rearrange("(p t) m -> t p m", t=PACK)
        pages = {}

        def load_page(tag, t):
            pages[t] = slot(tag, "page%d" % t, [P, T], F32)
            nc.sync.dma_start(out=pages[t][:], in_=g_rows[t])

        def quantize(name, grouped, width=G, tag=None):
            codes = slot(tag or name, name + "_codes", [P, width], U32)
            scales = kept(name + "_scales", [P, width], U8)
            nc.vector.quantize_mx(out=codes[:].bitcast(FP8X4), scales=scales[:], in_=grouped)
            return codes, scales

        def woven_views(grouped, raw, run=4):
            return (
                grouped.rearrange("p (c i t) -> p c t i", i=run, t=PACK),
                raw.rearrange("p t (c i) -> p c t i", i=run),
            )

        def weave(copy, grouped, raw):
            dst, src = woven_views(grouped, raw)
            copy(out=dst, in_=src)

        def list_half(h):
            return offsets[:, h * LIST_COLS : (h + 1) * LIST_COLS]

        def half(h):
            return slice(h * HALF, (h + 1) * HALF)

        offsets = keep.tile([P, S // 16], U16, name="offsets")
        nc.sync.dma_start(offsets[:], offs)
        tab_s = slot("tab_s", "tab_s", [P, T], U8)
        nc.vector.memset(tab_s[:].bitcast(I32), 0)
        tab_w = [load_table("C", 0)]
        bias = [load_channels("bias%d" % b, b1, b) for b in range(2)]
        gains = [load_channels("gains%d" % b, gain, b) for b in range(2)]

        def load_scale_rows(i):
            for a in range(2):
                nc.sync.dma_start(
                    out=tab_s[4 * (a + 1) + i : P : 32, :].bitcast(I32), in_=tab_scales[a, i:16:4, :].bitcast(I32)
                )

        load_scale_rows(0)
        w1_raw = {(0, 0): load_rows("B", "w1_raw00", w1[0:G, 0:G])}
        for q in range(1, 4):
            load_scale_rows(q)
        tab_w.append(load_table("D", 1))
        w1_raw[1, 0] = load_rows("w10", "w1_raw10", w1[G : 2 * G, 0:G])
        w1_raw[0, 1] = load_rows("w01", "w1_raw01", w1[0:G, G : 2 * G])
        w1_raw[1, 1] = load_rows("w11", "w1_raw11", w1[G : 2 * G, G : 2 * G])
        load_page("page3", 3)
        tick_raw = [load_rows("w01", "tick_raw0", tick[:, half(0)])]
        w3_raw = load_rows("A", "w3_raw", w3)
        w4_raw = kept("w4_raw", [P, 2, 2 * N], U8)
        nc.sync.dma_start(out=w4_raw[:].bitcast(I32), in_=w4_words.rearrange("b p n -> p b n").bitcast(I32))
        load_page("page1", 1)
        load_page("page0", 0)
        load_page("page2", 2)
        tick_raw.append(load_rows("tick1", "tick_raw1", tick[:, half(1)]))

        padded = kept("padded", [P, P], F32)
        nc.gpsimd.memset(padded[:], 0.0)
        unread = kept("unread", [P, 1], F32)
        nc.scalar.activation(out=unread[:], in_=padded[:, P - 1 : P], func=ACT.Sigmoid)
        w4_raw_s = kept("w4_raw_s", [P, 2 * N], U8)
        nc.gpsimd.memset(w4_raw_s[:].bitcast(I32), 0)
        for q in range(4):
            nc.gpsimd.dma_start(
                out=w4_raw_s[32 * q : 32 * q + 4, :].bitcast(I32).rearrange("i (a n) -> i a n", a=2),
                in_=w4_scales[:, 4 * q : 4 * q + 4, :].rearrange("a i n -> i a n").bitcast(I32),
            )
        nc.scalar.copy(out=padded[:, 0:PACK], in_=gains[1][:])
        identity = kept("identity", [P, P], F32)
        make_identity(nc, identity[:])
        v_words = [slot(tag, "v_words", [P, S], U32) for tag in ("v0", "B")]
        v_scales = kept("v_scales", [P, S], U8)
        w1_q = {}

        def quantize_dealt(name, raw, copies, tags, codes_tag=None):
            parts = len(copies)
            rows = PACK // parts
            grouped = [slot(tag, name + "_grouped", [P, G * rows], BF16) for tag in tags]
            for u, copy in enumerate(copies):
                copy(
                    out=grouped[u][:].rearrange("p (t m j) -> p m j t", t=rows, j=PACK),
                    in_=raw[:].rearrange("p j (m t) -> p m j t", t=PACK)[:, :, :, rows * u : rows * (u + 1)],
                )
            weights = []
            for u in range(parts):
                codes, scales = quantize("%s_%d" % (name, u), grouped[u][:], P * rows, codes_tag)
                weights.extend((codes[:, e * P : (e + 1) * P], scales[:, e * P : (e + 1) * P]) for e in range(rows))
            return weights

        def quantize_w1(a, b, copies, tags, codes_tag=None):
            w1_q[a, b] = quantize_dealt("w1_%d%d" % (a, b), w1_raw[a, b], copies, tags, codes_tag)

        def gather_words(a):
            nc.vector.tensor_copy(v_words[a][:], tab_w[a][:].bitcast(U32).indirect(offsets[:]))

        gather_words(0)
        nc.vector.tensor_copy(v_scales[:], tab_s[:].indirect(offsets[:]))
        quantize_w1(0, 0, [nc.scalar.copy], ["g00"], "tab_s")
        w4_plane = kept("w4_plane", [P, 2 * N], U8)
        nc.gpsimd.tensor_copy(
            out=w4_plane[:].rearrange("p (a t m) -> p a t m", a=2, t=PACK),
            in_=w4_raw_s[:].rearrange("p (a m t) -> p a t m", a=2, t=PACK),
        )
        gather_words(1)
        quantize_w1(1, 0, [nc.scalar.copy] * 2, ["w3_grouped", "g10b"])
        turned = psum.tile([P, P], F32, name="turned", tag="bank6", bufs=1)
        nc.tensor.transpose(turned[:], padded[:], identity[:])
        flipped = kept("flipped", [P, P], F32)
        nc.scalar.copy(out=flipped[:], in_=turned[:])
        gains_psum = psum.tile([P, P], F32, name="gains_psum", tag="gain_bank", bufs=1)
        nc.tensor.transpose(gains_psum[:], flipped[:], identity[:])

        sig = {}

        x_acc = {}

        def stage_one(b, h, banks):
            for t in banks:
                acc = psum.tile([P, HALF], F32, name="x_acc", tag="bank%d" % banks[t], bufs=1)
                x_acc[b, h, t] = acc
                for a in range(2):
                    codes, scales = w1_q[a, b][t]
                    nc.tensor.matmul_mx(
                        out=acc[:],
                        lhsT=codes.bitcast(FP8X4),
                        lhsT_scale=scales,
                        rhs=v_words[a][:, half(h)].bitcast(FP8X4),
                        rhs_scale=v_scales[4 * (a + 1) : P, half(h)],
                        start=(a == 0),
                        stop=(a == 1),
                    )

        def sigmoids(b, h, tag):
            sig[b, h] = slot(tag, "sig%d%d" % (b, h), [P, PACK, HALF], F32)
            for t in range(PACK):
                nc.scalar.activation(
                    out=sig[b, h][:, t, :], in_=x_acc[b, h, t][:], func=ACT.Sigmoid, bias=bias[b][:, t : t + 1]
                )

        def scale_on_gpsimd(b, h, t, scaled):
            nc.gpsimd.tensor_scalar(
                out=scaled[:, t, :],
                in0=sig[b, h][:, t, :],
                scalar1=gains[b][:, t : t + 1],
                scalar2=0.0,
                op0=MULT,
                op1=ADD,
            )

        def weave_on_gpsimd(grouped, scaled, lo, hi):
            nc.gpsimd.tensor_scalar(
                out=grouped[:, lo * PACK : hi * PACK].rearrange("p (c t) -> p c t", t=PACK),
                in0=scaled[:, :, lo:hi].rearrange("p t c -> p c t"),
                scalar1=1.0,
                scalar2=0.0,
                op0=MULT,
                op1=ADD,
            )

        picked = {}

        def gather_page(t, into):
            nc.vector.tensor_copy(into, pages[t][:].indirect(offsets[:]))
            for h in range(2):
                picked[t, h] = into[:, half(h)]

        h_q, tick_q = {}, {}
        e_acc, root, damp = {}, {}, {}

        def stage_two(t, h):
            e_acc[t, h] = psum.tile([P, HALF], F32, name="e_acc", tag="bank%d" % ((0, 6, 1, 2), (0, 0, 1, 1))[h][t], bufs=1)
            ticket = [(w3_q[t][0].bitcast(FP8X4), w3_q[t][1], tick_q[h])]
            gallery = [
                (
                    w4_codes[:, b, 2 * t * P : 2 * (t + 1) * P].bitcast(FP4X4),
                    w4_plane[:, b * N + t * P : b * N + (t + 1) * P],
                    h_q[b, h],
                )
                for b in range(2)
            ]
            passes = gallery + ticket
            for i, (weights, weight_scales, moving) in enumerate(passes):
                nc.tensor.matmul_mx(
                    out=e_acc[t, h][:],
                    lhsT=weights,
                    lhsT_scale=weight_scales,
                    rhs=moving[0].bitcast(FP8X4),
                    rhs_scale=moving[1],
                    start=(i == 0),
                    stop=(i == len(passes) - 1),
                )

        def pieces(t, h):
            width = HALF // 2 if h == 0 or t in (0, 3) else HALF
            return [slice(lo, lo + width) for lo in range(0, HALF, width)]

        def inverse_root(t, h, square=None):
            last = (t, h) == (3, 1)
            if last:
                squares = [slot(tag, "square", [P, HALF // 2], F32)[:] for tag in ("D", "A")]
            else:
                if square is None:
                    square = slot("square", "square", [P, HALF], F32, bufs=2)
                squares = [square[:, cols] for cols in pieces(t, h)]
            for cols, square in zip(pieces(t, h), squares):
                nc.scalar.activation(out=square, in_=e_acc[t, h][:, cols], func=ACT.Square)
            root[t, h] = slot("B" if last else "root", "root", [P, HALF], F32, bufs=1 if last else 3)
            for cols, square in zip(pieces(t, h), squares):
                nc.scalar.activation(out=root[t, h][:, cols], in_=square, func=ACT.Abs_reciprocal_sqrt, bias=1.0)

        def square_root_factor(t, h, cols):
            nc.scalar.activation(out=damp[t, h][:, cols], in_=root[t, h][:, cols], func=ACT.Square)

        def damping(t, h, into=None, width=HALF):
            damp[t, h] = slot("damp", "damp", [P, HALF], F32, bufs=5)[:] if into is None else into
            for cols in pieces(t, h) if width == HALF else [slice(0, width)]:
                square_root_factor(t, h, cols)

        def scatter_state(t, h, lo=0, hi=HALF):
            entries = list_half(h)[:, lo // 16 : hi // 16]
            nc.vector.tensor_tensor(pages[t][:].indirect(entries), picked[t, h][:, lo:hi], damp[t, h][:, lo:hi], MULT)

        def whole(pair):
            return pair[0][:], pair[1][:]

        stage_one(0, 0, {0: 0, 1: 1, 2: 2, 3: 3})
        sigmoids(0, 0, "C")
        quantize_w1(0, 1, [nc.vector.tensor_copy] * 2, ["g01a", "g01b"])
        quantize_w1(1, 1, [nc.vector.tensor_copy] * 2, ["F", "h00_grouped"])
        gather_page(3, kept("picked3", [P, S], F32)[:])
        scaled = slot("h00_grouped", "scaled00", [P, PACK, HALF], BF16)
        for t in range(PACK - 1):
            scale_on_gpsimd(0, 0, t, scaled)
        tick_grouped = slot("tick_grouped", "tick_grouped", [P, G * PACK], BF16)
        quarter = HALF // 2
        sig10 = [slot(tag, "sig10", [P, PACK, quarter], F32) for tag in ("w10", "tick0")]
        for side in range(2):
            cols = slice(side * quarter, (side + 1) * quarter)
            for pair in range(2):
                acc = psum.tile([P, 2, quarter], F32, name="x_pair", tag="bank%d" % (1, 2, 3, 0)[2 * side + pair], bufs=1)
                for a in range(2):
                    for e in range(2):
                        codes, scales = w1_q[a, 1][2 * pair + e]
                        nc.tensor.matmul_mx(
                            out=acc[:, e, :],
                            lhsT=codes.bitcast(FP8X4),
                            lhsT_scale=scales,
                            rhs=v_words[a][:, cols].bitcast(FP8X4),
                            rhs_scale=v_scales[4 * (a + 1) : P, cols],
                            start=(a, e) == (0, 0),
                            stop=(a, e) == (1, 1),
                        )
                for e in range(2):
                    t = 2 * pair + e
                    nc.scalar.activation(
                        out=sig10[side][:, t, :], in_=acc[:, e, :], func=ACT.Sigmoid, bias=bias[1][:, t : t + 1]
                    )
        nc.scalar.activation(
            out=scaled[:, PACK - 1, :],
            in_=sig[0, 0][:, PACK - 1, :],
            func=ACT.Copy,
            scale=gains[0][:, PACK - 1 : PACK],
        )
        stage_one(0, 1, {0: 4, 1: 5, 2: 6, 3: 1})

        weave(nc.scalar.copy, tick_grouped[:, G * PACK // 2 :], tick_raw[0][:, :, HALF // 2 :])
        grouped = slot("h10_grouped", "h10_grouped", [P, G * PACK], BF16)
        factor = gains_psum[:, 0:PACK].unsqueeze(1).unsqueeze(3).broadcast_to([P, quarter // 2, PACK, 2])
        for side in range(2):
            dst, src = woven_views(grouped[:, side * quarter * PACK : (side + 1) * quarter * PACK], sig10[side][:], run=2)
            nc.vector.tensor_tensor(out=dst, in0=src, in1=factor, op=MULT)
        weave(nc.vector.tensor_copy, tick_grouped[:, 0 : G * PACK // 2], tick_raw[0][:, :, 0 : HALF // 2])
        h_q[1, 0] = whole(quantize("h10", grouped[:]))
        tick_q[0] = whole(quantize("tick0", tick_grouped[:]))
        grouped = slot("woven00", "h00_grouped", [P, G * PACK], BF16)
        for lo in (0, SHARE // 2):
            weave_on_gpsimd(grouped[:], scaled, lo, lo + SHARE // 2)
        weave(nc.scalar.copy, grouped[:, SHARE * PACK :], scaled[:, :, SHARE:])
        h_q[0, 0] = whole(quantize("h00", grouped[:]))
        w3_q = quantize_dealt("w3", w3_raw, [nc.scalar.copy] * 2, ["picked", "scaled"])
        w4_codes = kept("w4_codes", [P, 2, 2 * N], U8)
        nc.scalar.copy(
            out=w4_codes[:].bitcast(U16).rearrange("p b (t m) -> p b m t", t=PACK),
            in_=w4_raw[:].bitcast(U16).rearrange("p b (m t) -> p b m t", t=PACK),
        )
        sigmoids(0, 1, "D")
        stage_one(1, 1, {0: 2, 1: 3, 2: 4, 3: 5})
        sigmoids(1, 1, "A")
        filler = slot("picked", "picked", [P, PACK - 1, S], F32)
        for t in (1, 0, 2):
            gather_page(t, filler[:, t, :])
        for t in range(PACK):
            stage_two(t, 0)

        scaled = slot("scaled", "scaled_late", [P, 2, PACK, HALF], BF16)
        late = slot("woven00", "late_grouped", [P, 2 * G * PACK], BF16)
        for b in range(2):
            for t in range(PACK):
                scale_on_gpsimd(b, 1, t, scaled[:, b])
        inverse_root(0, 0)
        damping(0, 0)
        scatter_state(0, 0)
        inverse_root(1, 0)
        damping(1, 0)
        scatter_state(1, 0)
        for b in range(2):
            weave(nc.scalar.copy, late[:, b * G * PACK : (b + 1) * G * PACK], scaled[:, b])
        codes, scales = quantize("h_late", late[:], width=2 * G)
        for b in range(2):
            h_q[b, 1] = codes[:, b * G : (b + 1) * G], scales[:, b * G : (b + 1) * G]
        inverse_root(3, 0)
        damping(3, 0, width=HALF // 2)
        scatter_state(3, 0, 0, HALF // 2)
        grouped = slot("w3_grouped", "tick_grouped", [P, G * PACK], BF16)
        weave(nc.scalar.copy, grouped[:], tick_raw[1][:])
        square_root_factor(3, 0, slice(HALF // 2, HALF))
        tick_q[1] = whole(quantize("tick1", grouped[:]))
        scatter_state(3, 0, HALF // 2, HALF)
        inverse_root(2, 0)
        damping(2, 0)
        scatter_state(2, 0)

        y_rows = out_0.rearrange("(p t) m -> t p m", t=PACK)
        order = (0, 2, 1, 3)
        for t in order:
            stage_two(t, 1)

        def finish_page(t):
            scatter_state(t, 1)
            nc.sync.dma_start(out=y_rows[t], in_=pages[t][:])

        for t in order[:3]:
            inverse_root(t, 1)
            damping(t, 1)
            finish_page(t)
        inverse_root(3, 1)
        damping(3, 1, width=HALF // 2)
        square_root_factor(3, 1, slice(HALF // 2, HALF - LAST))

        pairs = [slot(tag, "pairs", [P, 2 * T], BF16) for tag in ("D", "A")]

        def round_page(copy, t, side, lo, hi):
            base = side * T // 2
            copy(out=pairs[side][:].rearrange("p (u c e) -> p u c e", u=2, e=2)[:, t // 2, lo:hi, t % 2], in_=pages[t][:, base + lo : base + hi])

        for side in range(2):
            round_page(nc.scalar.copy, 0, side, 0, T // 2)
        round_page(nc.scalar.copy, 2, 0, 0, T // 2)
        square_root_factor(3, 1, slice(HALF - LAST, HALF))
        finish_page(3)
        round_page(nc.scalar.copy, 2, 1, 0, T // 2)
        for side in range(2):
            round_page(nc.scalar.copy, 1, side, 0, T // 2)

        span = T // 8
        y_scales = kept("y_scales", [P, 2 * span], U8)
        y_codes = slot("C", "y_codes", [P, T], I32)
        y_words = out_1[0].rearrange("p m t -> p (m t)").bitcast(I32)
        woven = [slot(tag, "woven", [P, 2 * span * PACK], BF16) for tag in ("w10", "w01", "w11", "tick0")]

        def woven_span(c):
            return woven[c // 2][:, c % 2 * span * PACK : (c % 2 + 1) * span * PACK]

        def weave_words(copy, c):
            side, lo = divmod(c * span, T // 2)
            words = pairs[side][:].bitcast(F32).rearrange("p (u c) -> p u c", u=2)
            copy(
                out=woven_span(c).bitcast(F32).rearrange("p (c i u) -> p c u i", i=4, u=2),
                in_=words[:, :, lo : lo + span].rearrange("p u (c i) -> p c u i", i=4),
            )

        def quantize_y(c):
            plane = y_scales[4 * (c // 2) : P, c % 2 * span : (c % 2 + 1) * span]
            cols = slice(c * span, (c + 1) * span)
            nc.vector.quantize_mx(out=y_codes[:, cols].bitcast(FP8X4), scales=plane, in_=woven_span(c))
            if c % 2 == 1 or c == 6:
                cols = cols if c >= 6 else slice((c - 1) * span, (c + 1) * span)
                nc.sync.dma_start(out=y_words[:, cols], in_=y_codes[:, cols])

        round_page(nc.vector.tensor_copy, 3, 0, 0, T // 4)
        round_page(nc.vector.tensor_copy, 3, 0, T // 4, T // 2)
        round_page(nc.scalar.copy, 3, 1, 0, T // 4)
        round_page(nc.scalar.copy, 3, 1, T // 4, T // 2)
        for c in range(0, 8, 2):
            for e in range(2):
                weave_words(nc.vector.tensor_copy if c < 4 else nc.scalar.copy, c + e)
            for e in range(2):
                quantize_y(c + e)
        for q in range(4):
            (nc.sync, nc.scalar)[q % 2].dma_start(
                out=out_2[0, 4 * q : 4 * q + 4, :].rearrange("r (s c) -> s r c", s=4).bitcast(I32),
                in_=y_scales[32 * q : 32 * q + 16, :].bitcast(I32),
            )
